import numpy as np
import ml_dtypes


def mxq(x, axis, fmt="e4m3"):
    dtype, down = {"e4m3": (ml_dtypes.float8_e4m3fn, 7), "e5m2": (ml_dtypes.float8_e5m2, 14)}[fmt]
    v = np.moveaxis(np.asarray(x, np.float32).astype(ml_dtypes.bfloat16).astype(np.float64), axis, -1)
    blocks = v.reshape(v.shape[:-1] + (-1, 32))
    amax = np.abs(blocks).max(-1, keepdims=True)
    byte = np.maximum(np.where(amax > 0, np.frexp(amax)[1] - 1 + 127, 0) - down, 1)
    scale = np.exp2(byte - 127.0)
    codes = (blocks / scale).astype(np.float32).astype(dtype).astype(np.float64)
    return np.moveaxis((codes * scale).reshape(v.shape), -1, axis)


WIDE = False


def mx_kscale(k):
    if not WIDE:
        return np.ones(k)
    levels = np.array([10, -10, 5, -5, 0])
    if k % 512:
        return np.exp2(np.random.permutation(np.resize(levels, k // 32))).repeat(32)
    a = np.empty((k // 512, 16))
    for p in range(k // 512):
        a[p, :8] = np.random.permutation(np.resize(levels, 8))
        for g in range(8):
            far = levels[np.abs(levels - a[p, g]) >= 10]
            a[p, g + 8] = far[np.random.randint(len(far))]
    return np.exp2(a.ravel()).repeat(32)


def f64(x):
    return np.asarray(x).astype(np.float64)


def striped(idx):
    return np.tile(idx.reshape(-1, 16).T, (8, 1)).astype(np.uint16)


def unstriped(offs):
    return offs[:16].T.reshape(-1).astype(np.int64)


E2M1 = np.array([0.0, 0.5, 1.0, 1.5, 2.0, 3.0, 4.0, 6.0, -0.0, -0.5, -1.0, -1.5, -2.0, -3.0, -4.0, -6.0])


def pack_weight(w, fmt):
    k, n = w.shape
    w = f64(np.asarray(w, np.float32).astype(ml_dtypes.bfloat16)).reshape(k // 32, 32, n)
    amax = np.abs(w).max(1)
    if fmt == "e4m3":
        byte = np.frexp(amax)[1] - 1 + 127 - 7
    else:
        mant, ex = np.frexp(amax / 6.0)
        byte = np.where(mant > 0.5, ex, ex - 1) + 127
    byte = np.clip(np.where(amax > 0, byte, 1), 1, 254)
    scaled = (w * np.exp2(127.0 - byte)[:, None, :]).reshape(k, n).astype(np.float32)
    by_word = np.ascontiguousarray(scaled.reshape(k // 512, 128, 4, n).transpose(0, 1, 3, 2))
    if fmt == "e4m3":
        words = by_word.astype(ml_dtypes.float8_e4m3fn).view(np.uint8)
    else:
        c = by_word.astype(ml_dtypes.float4_e2m1fn).view(np.uint8) & 0xF
        words = (c[..., 0::2] | (c[..., 1::2] << 4)).reshape(k // 512, 128, 2 * n)
    return np.ascontiguousarray(words), np.ascontiguousarray(byte.astype(np.uint8).reshape(k // 512, 16, n))


def unpack_weight(words, scales, fmt):
    g, _, n = scales.shape
    words = np.ascontiguousarray(words).reshape(g, 128, n, -1)
    if fmt == "e4m3":
        vals = words.view(ml_dtypes.float8_e4m3fn).astype(np.float64)
    else:
        nib = np.empty((g, 128, n, 4), np.uint8)
        nib[..., 0::2] = words & 0xF
        nib[..., 1::2] = words >> 4
        vals = E2M1[nib]
    vals = vals * np.repeat(np.exp2(scales.astype(np.float64) - 127.0), 8, axis=1)[..., None]
    return vals.transpose(0, 1, 3, 2).reshape(g * 512, n)


def gelu(v):
    return 0.5 * v * (1.0 + np.tanh(np.sqrt(2.0 / np.pi) * (v + 0.044715 * v**3)))


def bf(x):
    return np.asarray(x, np.float32).astype(ml_dtypes.bfloat16)


def planes(Y):
    n, m = Y.shape
    b = f64(bf(Y)).reshape(n // 32, 32, m)
    amax = np.abs(b).max(1)
    byte = np.clip(np.where(amax > 0, np.frexp(amax)[1] - 1 + 127 - 7, 1), 1, 254)
    codes = (b * np.exp2(127.0 - byte)[:, None, :]).reshape(n, m).astype(np.float32).astype(ml_dtypes.float8_e4m3fn).view(np.uint8)
    words = codes.reshape(n // 512, 128, 4, m).transpose(0, 1, 3, 2)
    return np.ascontiguousarray(words), np.ascontiguousarray(byte.astype(np.uint8).reshape(n // 512, 16, m))


K, K2, H, N, T, S, T2 = 1024, 512, 1024, 1024, 2048, 512, 1024

def setup_inputs():
    n = np.random.standard_normal
    s = mx_kscale(K)[:, None]
    s2 = mx_kscale(K2)[:, None]
    u = mx_kscale(H)[:, None]
    tab_words, tab_scales = pack_weight(n((K, T)) * s, "e4m3")
    tab2_words, tab2_scales = pack_weight(n((K2, T)) * s2, "e4m3")
    w2_words, w2_scales = pack_weight(0.5 * n((K2, H)) / np.sqrt(K2) / s2, "e2m1")
    perm = np.random.permutation(T2)
    return {
        "tab_words": tab_words, "tab_scales": tab_scales,
        "offs": striped(np.random.permutation(T)[:S]),
        "tab2_words": tab2_words, "tab2_scales": tab2_scales,
        "offs2": striped(np.random.permutation(T)[:S]),
        "w1": (0.5 * n((K, H)) / np.sqrt(K) / s).astype(np.float32),
        "ctr": (0.4 * n(H)).astype(np.float32),
        "w2_words": w2_words, "w2_scales": w2_scales,
        "offs3": striped(perm[:S]), "offs4": striped(perm[S:]),
        "wg1": np.exp(0.3 * n((128, S))).astype(np.float32),
        "wg2": np.exp(0.3 * n((128, S))).astype(np.float32),
        "style": (n((H, T2)) * u).astype(np.float32),
        "w3": (n((H, N)) * np.exp(0.8 * n(N)) / np.sqrt(H) / u).astype(np.float32),
    }

def reference(tab_words, tab_scales, offs, tab2_words, tab2_scales, offs2, w1, ctr, w2_words, w2_scales, offs3, offs4, wg1, wg2, style, w3):
    v = unpack_weight(tab_words, tab_scales, "e4m3")[:, unstriped(offs)]
    v2 = unpack_weight(tab2_words, tab2_scales, "e4m3")[:, unstriped(offs2)]
    d = (mxq(f64(w1), 0, "e4m3").T @ v) - f64(ctr)[:, None]
    h1 = np.exp(-np.square(d))
    h2 = np.cos(unpack_weight(w2_words, w2_scales, "e2m1").T @ v2)
    page = np.zeros((H, T2))
    page[:, unstriped(offs3)] = np.tile(f64(wg1), (H // 128, 1)) * h1
    page[:, unstriped(offs4)] = np.tile(f64(wg2), (H // 128, 1)) * h2
    z = page * f64(style)
    y = mxq(f64(w3), 0, "e4m3").T @ mxq(z, 0, "e4m3")
    words, scales = planes(y)
    return y, words, scales

@@ -1,0 +1,294 @@
+import math
+from contextlib import ExitStack
+
+import concourse.mybir as mybir
+
+F32 = mybir.dt.float32
+BF16 = mybir.dt.bfloat16
+I32 = mybir.dt.int32
+U32 = mybir.dt.uint32
+U16 = mybir.dt.uint16
+U8 = mybir.dt.uint8
+FP8X4 = mybir.dt.float8_e4m3fn_x4
+FP4X4 = mybir.dt.float4_e2m1fn_x4
+ACT = mybir.ActivationFunctionType
+MULT = mybir.AluOpType.mult
+ADD = mybir.AluOpType.add
+
+P = 128
+K, K2, H, N, T, S, T2 = 1024, 512, 1024, 1024, 2048, 512, 1024
+FLOPS = 2 * K * H * S + 2 * K2 * H * S + 2 * H * N * T2
+CHUNK = 256
+CHUNKS = T2 // CHUNK
+TILES = H // P
+
+
+def tile_list_crowd_steering_features_kernel(
+    tc, tab_words, tab_scales, offs, tab2_words, tab2_scales, offs2, w1, ctr, w2_words, w2_scales,
+    offs3, offs4, wg1, wg2, style, w3, out_0, out_1, out_2,
+):
+    nc = tc.nc
+    with ExitStack() as ctx:
+        lists = ctx.enter_context(tc.tile_pool(name="lists", bufs=1))
+        keep = ctx.enter_context(tc.tile_pool(name="keep", bufs=1))
+        psum = ctx.enter_context(tc.psum_pool(name="psum", bufs=1))
+
+        def held(name, shape, dtype, tag=None, bufs=1):
+            return keep.tile(shape, dtype, name=name, tag=tag or name, bufs=bufs, align_bytes=64)
+
+        def load_list(name, src):
+            lst = lists.tile([P, S // 16], U16, name=name, tag=name)
+            nc.sync.dma_start(lst[:], src)
+            return lst
+
+        def load_scale_rows(name, src):
+            passes, cols = src.shape[0], src.shape[2]
+            plane = held(name, [P, cols], U8)
+            nc.vector.memset(plane[:].bitcast(I32), 0)
+            for q in range(4):
+                nc.sync.dma_start(
+                    plane[32 * q : 32 * q + 4 * passes, :].bitcast(I32),
+                    src[:, 4 * q : 4 * q + 4, :].bitcast(I32),
+                )
+            return plane
+
+        def load_words(name, src, tag):
+            words = held(name, [P, T], I32, tag=tag)
+            nc.sync.dma_start(words[:], src.rearrange("p n i -> p (n i)").bitcast(I32))
+            return words
+
+        def load_gains(name, src):
+            gains = held(name, [P, 4, S], F32)
+            for q in range(4):
+                nc.sync.dma_start(gains[32 * q : 32 * q + 32], src.rearrange("(u t) j -> u t j", t=4))
+            return gains
+
+        def gather(name, window, lst, dtype):
+            picked = held(name, [P, S], dtype)
+            nc.vector.tensor_copy(picked[:], window[:].bitcast(dtype).indirect(lst[:]))
+            return picked
+
+        def load_weight(name, src):
+            raws = {}
+            for half in range(2):
+                for a in range(2):
+                    raw = held(f"{name}_raw{half}{a}", [P, 4, 512], F32, tag="stage", bufs=4)
+                    rows = src[512 * a : 512 * (a + 1), 512 * half : 512 * (half + 1)]
+                    nc.sync.dma_start(raw[:], rows.rearrange("(p j) c -> p j c", j=4))
+                    raws[half, a] = raw
+            return raws
+
+        def quantise_weight(name, raws, half, tag):
+            rounded = held(f"{name}_bf{half}", [P, 2, 2048], BF16, tag=tag)
+            for a in range(2):
+                nc.scalar.copy(
+                    rounded[:, a, :].rearrange("p (t m j) -> p m t j", t=4, j=4),
+                    raws[half, a][:].rearrange("p j (m t) -> p m t j", t=4),
+                )
+            codes = held(f"{name}_codes{half}", [P, 1024], U32)
+            scales = held(f"{name}_scales{half}", [P, 1024], U8)
+            nc.vector.quantize_mx(codes[:].bitcast(FP8X4), scales[:], rounded[:].rearrange("p a c -> p (a c)"))
+            return codes, scales
+
+        def bank(idx, name):
+            return psum.tile([P, 512], F32, name=name, tag=f"bank{idx % 8}")
+
+        zero = held("zero", [P, 1], F32)
+        nc.vector.memset(zero[:], 0.0)
+        sin_zero = held("sin_zero", [P, 1], F32)
+        nc.scalar.activation(sin_zero[:], zero[:], ACT.Sin)
+        half_pi = held("half_pi", [P, 1], F32)
+        nc.vector.tensor_scalar(half_pi[:], sin_zero[:], 1.0, math.pi / 2, op0=MULT, op1=ADD)
+
+        w2_plane = load_scale_rows("w2_plane", w2_scales)
+        w2_raw = held("w2_raw", [P, 2 * H], U8)
+        nc.sync.dma_start(w2_raw[:].bitcast(I32), w2_words[0].bitcast(I32))
+        list2 = load_list("list2", offs2)
+        tab2 = load_words("tab2", tab2_words[0], "big0")
+        tab2_plane = load_scale_rows("tab2_plane", tab2_scales)
+        gains2 = load_gains("gains2", wg2)
+        list4 = load_list("list4", offs4)
+        list1 = load_list("list1", offs)
+        tab = [load_words(f"tab{a}", tab_words[a], f"big{1 + a}") for a in range(2)]
+        tab_plane = load_scale_rows("tab_plane", tab_scales)
+        w1_raw = load_weight("w1", w1)
+        centre = held("centre", [P, 2, 4], F32)
+        nc.sync.dma_start(centre[:], ctr.rearrange("(g p t) -> p g t", g=2, t=4))
+        list3 = load_list("list3", offs3)
+        gains1 = load_gains("gains1", wg1)
+        styles = []
+        for i in range(TILES):
+            g, t = divmod(i, 4)
+            st = held(f"style{i}", [P, T2], F32)
+            nc.sync.dma_start(st[:], style.rearrange("(g p t) n -> g t p n", g=2, t=4)[g, t])
+            styles.append(st)
+
+        w2_dealt = held("w2_dealt", [P, 2 * H], U8)
+        nc.vector.tensor_copy(
+            w2_dealt[:].rearrange("p (g t m e) -> p g t m e", g=2, t=4, e=2),
+            w2_raw[:].rearrange("p (g m t e) -> p g t m e", g=2, t=4, e=2),
+        )
+        w2_plane_dealt = held("w2_plane_dealt", [P, H], U8)
+        nc.vector.tensor_copy(
+            w2_plane_dealt[:].rearrange("p (g t m) -> p g t m", g=2, t=4),
+            w2_plane[:].rearrange("p (g m t) -> p g t m", g=2, t=4),
+        )
+        v2_words = gather("v2_words", tab2, list2, U32)
+        v2_scales = gather("v2_scales", tab2_plane, list2, U8)
+
+        h2 = []
+        for i in range(TILES):
+            acc = bank(i, f"angle{i}")
+            nc.tensor.matmul_mx(
+                acc[:],
+                lhsT=w2_dealt[:, 2 * P * i : 2 * P * (i + 1)].bitcast(FP4X4),
+                lhsT_scale=w2_plane_dealt[:, P * i : P * (i + 1)],
+                rhs=v2_words[:].bitcast(FP8X4),
+                rhs_scale=v2_scales[:],
+                start=True,
+                stop=True,
+            )
+            h = held(f"h2_{i}", [P, S], F32, tag="h", bufs=10)
+            nc.scalar.activation(h[:], acc[:], ACT.Abs)
+            nc.scalar.activation(h[:], h[:], ACT.Sin, bias=half_pi[:], scale=-1.0)
+            h2.append(h)
+
+        pages = {}
+
+        def place_runners(i, tag):
+            pages[i] = held(f"page{i}", [P, T2], F32, tag=tag)
+            nc.vector.tensor_tensor(pages[i][:].indirect(list4[:]), h2[i][:], gains2[:, i % 4, :], MULT)
+
+        for i in range(5):
+            place_runners(i, f"page{i}")
+
+        v_words = [gather(f"v_words{a}", tab[a], list1, U32) for a in range(2)]
+        v_scales = gather("v_scales", tab_plane, list1, U8)
+        h1 = []
+        for half in range(2):
+            codes, scales = quantise_weight("w1", w1_raw, half, f"round{half}")
+            place_runners(5 + half, f"round{half}")
+            for t in range(4):
+                i = 4 * half + t
+                acc = bank(i, f"dist{i}")
+                for a in range(2):
+                    cols = slice(512 * a + P * t, 512 * a + P * (t + 1))
+                    nc.tensor.matmul_mx(
+                        acc[:],
+                        lhsT=codes[:, cols].bitcast(FP8X4),
+                        lhsT_scale=scales[:, cols],
+                        rhs=v_words[a][:].bitcast(FP8X4),
+                        rhs_scale=v_scales[4 * a : P, :],
+                        start=(a == 0),
+                        stop=(a == 1),
+                    )
+                h = held(f"h1_{i}", [P, S], F32, tag="h", bufs=10)
+                nc.scalar.activation(h[:], acc[:], ACT.Square, bias=centre[:, half, t : t + 1], scale=-1.0)
+                nc.scalar.activation(h[:], h[:], ACT.Exp, scale=-1.0)
+                h1.append(h)
+
+        w3_raw = load_weight("w3", w3)
+        z_rows = [held(f"z_rows{g}", [P, CHUNKS, 4, CHUNK], BF16, tag=f"big{g}") for g in range(2)]
+        z_woven = [held("z_woven0", [P, CHUNKS, CHUNK, 4], BF16, tag="big2"), None]
+        z_codes = [held(f"z_codes{g}", [P, T2], U32) for g in range(2)]
+        z_scales = [held(f"z_scales{g}", [P, T2], U8) for g in range(2)]
+
+        def place_walkers(i):
+            nc.vector.tensor_tensor(pages[i][:].indirect(list3[:]), h1[i][:], gains1[:, i % 4, :], MULT)
+
+        def apply_style(i, chunks):
+            g, t = divmod(i, 4)
+            nc.vector.tensor_tensor(
+                z_rows[g][:, chunks, t, :],
+                pages[i][:].rearrange("p (c n) -> p c n", n=CHUNK)[:, chunks, :],
+                styles[i][:].rearrange("p (c n) -> p c n", n=CHUNK)[:, chunks, :],
+                MULT,
+            )
+
+        def weave(copy, g, c):
+            copy(
+                z_woven[g][:, c].rearrange("p (n i) t -> p n t i", i=4),
+                z_rows[g][:, c].rearrange("p t (n i) -> p n t i", i=4),
+            )
+
+        def quantise_z(g, c0, c1):
+            cols = slice(CHUNK * c0, CHUNK * c1)
+            nc.vector.quantize_mx(
+                z_codes[g][:, cols].bitcast(FP8X4),
+                z_scales[g][:, cols],
+                z_woven[g][:, c0:c1].rearrange("p c n t -> p (c n t)"),
+            )
+
+        for i in range(4):
+            place_walkers(i)
+            apply_style(i, slice(0, CHUNKS))
+        for c in range(CHUNKS):
+            weave(nc.scalar.copy, 0, c)
+        w3_q = [quantise_weight("w3", w3_raw, half, f"round{2 + half}") for half in range(2)]
+        z_woven[1] = held("z_woven1", [P, CHUNKS, CHUNK, 4], BF16, tag="round2")
+        place_walkers(4)
+        apply_style(4, slice(0, CHUNKS))
+        quantise_z(0, 0, CHUNKS)
+        for i in range(5, 7):
+            place_walkers(i)
+            apply_style(i, slice(0, CHUNKS))
+        place_runners(7, "round3")
+        place_walkers(7)
+
+        def project(acc, c, g_out, pair, a):
+            codes, scales = w3_q[g_out]
+            for e in range(2):
+                t = 2 * pair + e
+                cols = slice(512 * a + P * t, 512 * a + P * (t + 1))
+                agents = slice(CHUNK * c, CHUNK * (c + 1))
+                nc.tensor.matmul_mx(
+                    acc[:, CHUNK * e : CHUNK * (e + 1)],
+                    lhsT=codes[:, cols].bitcast(FP8X4),
+                    lhsT_scale=scales[:, cols],
+                    rhs=z_codes[a][:, agents].bitcast(FP8X4),
+                    rhs_scale=z_scales[a][:, agents],
+                    start=(a == 0 and e == 0),
+                    stop=(a == 1 and e == 1),
+                )
+
+        for c in range(CHUNKS):
+            apply_style(7, slice(c, c + 1))
+            weave(nc.scalar.copy if c == 1 else nc.vector.tensor_copy, 1, c)
+            quantise_z(1, c, c + 1)
+
+        y_codes = [held(f"y_codes{g}", [P, T2], U32) for g in range(2)]
+        y_scales = held("y_scales", [P, 2, T2], U8)
+        y_rows = out_0.rearrange("(g p t) n -> g p t n", g=2, t=4)
+        for c in range(CHUNKS):
+            agents = slice(CHUNK * c, CHUNK * (c + 1))
+            for g_out in range(2):
+                if g_out == 0:
+                    y_pair = held(f"y{c}", [P, 2, 4, CHUNK], F32, tag="stage", bufs=4)
+                y = y_pair[:, g_out]
+                for pair in range(2):
+                    acc = bank(4 * c + 2 * g_out + pair, f"y{c}{g_out}{pair}")
+                    for a in range(2):
+                        project(acc, c, g_out, pair, a)
+                    nc.scalar.copy(y[:, 2 * pair : 2 * pair + 2, :].rearrange("p t n -> p (t n)"), acc[:])
+                nc.sync.dma_start(y_rows[g_out][:, :, agents], y)
+                y_woven = held(f"y_woven{c}{g_out}", [P, CHUNK, 4], BF16, tag=f"round{g_out}")
+                nc.vector.tensor_copy(
+                    y_woven[:].rearrange("p (n i) t -> p n t i", i=4),
+                    y.rearrange("p t (n i) -> p n t i", i=4),
+                )
+                nc.vector.quantize_mx(
+                    y_codes[g_out][:, agents].bitcast(FP8X4),
+                    y_scales[:, g_out, agents],
+                    y_woven[:].rearrange("p n t -> p (n t)"),
+                )
+                if c % 2 == 1:
+                    both = slice(CHUNK * (c - 1), CHUNK * (c + 1))
+                    nc.sync.dma_start(
+                        out_1[g_out].rearrange("p n i -> p (n i)").bitcast(I32)[:, both],
+                        y_codes[g_out][:, both].bitcast(I32),
+                    )
+        for q in range(4):
+            nc.sync.dma_start(
+                out_2[:, 4 * q : 4 * q + 4, :].rearrange("g r n -> r g n").bitcast(I32),
+                y_scales[32 * q : 32 * q + 4].bitcast(I32),
+            )

@@ -59,7 +59,7 @@ def tile_list_crowd_steering_features_kernel(
 
         def load_gains(name, src):
             gains = held(name, [P, 4, S], F32)
-            for q in range(4):
+            for q in (0, 2, 1, 3):
                 nc.sync.dma_start(gains[32 * q : 32 * q + 32], src.rearrange("(u t) j -> u t j", t=4))
             return gains
 
@@ -72,7 +72,7 @@ def tile_list_crowd_steering_features_kernel(
             raws = {}
             for half in range(2):
                 for a in range(2):
-                    raw = held(f"{name}_raw{half}{a}", [P, 4, 512], F32, tag="stage", bufs=4)
+                    raw = held(f"{name}_raw{half}{a}", [P, 4, 512], F32, tag=f"stage{2 * half + a}")
                     rows = src[512 * a : 512 * (a + 1), 512 * half : 512 * (half + 1)]
                     nc.sync.dma_start(raw[:], rows.rearrange("(p j) c -> p j c", j=4))
                     raws[half, a] = raw
@@ -100,17 +100,18 @@ def tile_list_crowd_steering_features_kernel(
         half_pi = held("half_pi", [P, 1], F32)
         nc.vector.tensor_scalar(half_pi[:], sin_zero[:], 1.0, math.pi / 2, op0=MULT, op1=ADD)
 
-        w2_plane = load_scale_rows("w2_plane", w2_scales)
+        tab2_plane = load_scale_rows("tab2_plane", tab2_scales)
+        list2 = load_list("list2", offs2)
         w2_raw = held("w2_raw", [P, 2 * H], U8)
         nc.sync.dma_start(w2_raw[:].bitcast(I32), w2_words[0].bitcast(I32))
-        list2 = load_list("list2", offs2)
         tab2 = load_words("tab2", tab2_words[0], "big0")
-        tab2_plane = load_scale_rows("tab2_plane", tab2_scales)
-        gains2 = load_gains("gains2", wg2)
-        list4 = load_list("list4", offs4)
+        w2_plane = load_scale_rows("w2_plane", w2_scales)
         list1 = load_list("list1", offs)
-        tab = [load_words(f"tab{a}", tab_words[a], f"big{1 + a}") for a in range(2)]
+        tab = [load_words("tab0", tab_words[0], "big1")]
+        list4 = load_list("list4", offs4)
+        gains2 = load_gains("gains2", wg2)
         tab_plane = load_scale_rows("tab_plane", tab_scales)
+        tab.append(load_words("tab1", tab_words[1], "big2"))
         w1_raw = load_weight("w1", w1)
         centre = held("centre", [P, 2, 4], F32)
         nc.sync.dma_start(centre[:], ctr.rearrange("(g p t) -> p g t", g=2, t=4))
@@ -128,13 +129,15 @@ def tile_list_crowd_steering_features_kernel(
             w2_dealt[:].rearrange("p (g t m e) -> p g t m e", g=2, t=4, e=2),
             w2_raw[:].rearrange("p (g m t e) -> p g t m e", g=2, t=4, e=2),
         )
-        w2_plane_dealt = held("w2_plane_dealt", [P, H], U8)
-        nc.vector.tensor_copy(
-            w2_plane_dealt[:].rearrange("p (g t m) -> p g t m", g=2, t=4),
-            w2_plane[:].rearrange("p (g m t) -> p g t m", g=2, t=4),
-        )
-        v2_words = gather("v2_words", tab2, list2, U32)
         v2_scales = gather("v2_scales", tab2_plane, list2, U8)
+        v2_words = gather("v2_words", tab2, list2, U32)
+        w2_plane_dealt = held("w2_plane_dealt", [P, H], U8)
+        for g in range(2):
+            cols = slice(512 * g, 512 * (g + 1))
+            nc.vector.tensor_copy(
+                w2_plane_dealt[:, cols].rearrange("p (t m) -> p t m", t=4),
+                w2_plane[:, cols].rearrange("p (m t) -> p t m", t=4),
+            )
 
         h2 = []
         for i in range(TILES):
@@ -151,13 +154,14 @@ def tile_list_crowd_steering_features_kernel(
             h = held(f"h2_{i}", [P, S], F32, tag="h", bufs=10)
             nc.scalar.activation(h[:], acc[:], ACT.Abs)
             nc.scalar.activation(h[:], h[:], ACT.Sin, bias=half_pi[:], scale=-1.0)
+            nc.gpsimd.tensor_tensor(h[:], h[:], gains2[:, i % 4, :], MULT)
             h2.append(h)
 
         pages = {}
 
         def place_runners(i, tag):
             pages[i] = held(f"page{i}", [P, T2], F32, tag=tag)
-            nc.vector.tensor_tensor(pages[i][:].indirect(list4[:]), h2[i][:], gains2[:, i % 4, :], MULT)
+            nc.vector.tensor_copy(pages[i][:].indirect(list4[:]), h2[i][:])
 
         for i in range(5):
             place_runners(i, f"page{i}")
@@ -185,20 +189,22 @@ def tile_list_crowd_steering_features_kernel(
                 h = held(f"h1_{i}", [P, S], F32, tag="h", bufs=10)
                 nc.scalar.activation(h[:], acc[:], ACT.Square, bias=centre[:, half, t : t + 1], scale=-1.0)
                 nc.scalar.activation(h[:], h[:], ACT.Exp, scale=-1.0)
+                nc.gpsimd.tensor_tensor(h[:], h[:], gains1[:, t, :], MULT)
                 h1.append(h)
 
         w3_raw = load_weight("w3", w3)
-        z_rows = [held(f"z_rows{g}", [P, CHUNKS, 4, CHUNK], BF16, tag=f"big{g}") for g in range(2)]
-        z_woven = [held("z_woven0", [P, CHUNKS, CHUNK, 4], BF16, tag="big2"), None]
+        z_rows = [held(f"z_rows{g}", [P, CHUNKS, 4, CHUNK], BF16, tag=("gains1", "big1")[g]) for g in range(2)]
+        z_woven = [None, None]
         z_codes = [held(f"z_codes{g}", [P, T2], U32) for g in range(2)]
         z_scales = [held(f"z_scales{g}", [P, T2], U8) for g in range(2)]
 
         def place_walkers(i):
-            nc.vector.tensor_tensor(pages[i][:].indirect(list3[:]), h1[i][:], gains1[:, i % 4, :], MULT)
+            nc.vector.tensor_copy(pages[i][:].indirect(list3[:]), h1[i][:])
 
         def apply_style(i, chunks):
             g, t = divmod(i, 4)
-            nc.vector.tensor_tensor(
+            engine = nc.vector if i == 7 else nc.gpsimd
+            engine.tensor_tensor(
                 z_rows[g][:, chunks, t, :],
                 pages[i][:].rearrange("p (c n) -> p c n", n=CHUNK)[:, chunks, :],
                 styles[i][:].rearrange("p (c n) -> p c n", n=CHUNK)[:, chunks, :],
@@ -221,18 +227,22 @@ def tile_list_crowd_steering_features_kernel(
 
         for i in range(4):
             place_walkers(i)
-            apply_style(i, slice(0, CHUNKS))
+            apply_style(i, slice(0, 2))
+            apply_style(i, slice(2, 4))
+        w3_q = [quantise_weight("w3", w3_raw, half, f"round{2 + half}") for half in range(2)]
+        z_woven[0] = held("z_woven0", [P, CHUNKS, CHUNK, 4], BF16, tag="stage3")
         for c in range(CHUNKS):
             weave(nc.scalar.copy, 0, c)
-        w3_q = [quantise_weight("w3", w3_raw, half, f"round{2 + half}") for half in range(2)]
         z_woven[1] = held("z_woven1", [P, CHUNKS, CHUNK, 4], BF16, tag="round2")
         place_walkers(4)
-        apply_style(4, slice(0, CHUNKS))
+        apply_style(4, slice(0, 2))
+        apply_style(4, slice(2, 4))
         quantise_z(0, 0, CHUNKS)
         for i in range(5, 7):
             place_walkers(i)
-            apply_style(i, slice(0, CHUNKS))
-        place_runners(7, "round3")
+            apply_style(i, slice(0, 2))
+            apply_style(i, slice(2, 4))
+        place_runners(7, "stage3")
         place_walkers(7)
 
         def project(acc, c, g_out, pair, a):
@@ -263,7 +273,7 @@ def tile_list_crowd_steering_features_kernel(
             agents = slice(CHUNK * c, CHUNK * (c + 1))
             for g_out in range(2):
                 if g_out == 0:
-                    y_pair = held(f"y{c}", [P, 2, 4, CHUNK], F32, tag="stage", bufs=4)
+                    y_pair = held(f"y{c}", [P, 2, 4, CHUNK], F32, tag=("stage0", "stage1", "stage2", "big2")[c])
                 y = y_pair[:, g_out]
                 for pair in range(2):
                     acc = bank(4 * c + 2 * g_out + pair, f"y{c}{g_out}{pair}")

@@ -31,6 +31,7 @@ def tile_list_crowd_steering_features_kernel(
     with ExitStack() as ctx:
         lists = ctx.enter_context(tc.tile_pool(name="lists", bufs=1))
         keep = ctx.enter_context(tc.tile_pool(name="keep", bufs=1))
+        shared = ctx.enter_context(tc.tile_pool(name="shared", bufs=1))
         psum = ctx.enter_context(tc.psum_pool(name="psum", bufs=1))
 
         def held(name, shape, dtype, tag=None, bufs=1):
@@ -52,16 +53,23 @@ def tile_list_crowd_steering_features_kernel(
                 )
             return plane
 
+        def load_scale_rows_repeated(name, src):
+            plane = held(name, [P, src.shape[2]], U8)
+            for q in range(4):
+                rows = src[0, 4 * q : 4 * q + 4, :].bitcast(I32)
+                nc.sync.dma_start(plane[32 * q : 32 * q + 32, :].bitcast(I32), rows.partition_broadcast(8))
+            return plane
+
         def load_words(name, src, tag):
             words = held(name, [P, T], I32, tag=tag)
             nc.sync.dma_start(words[:], src.rearrange("p n i -> p (n i)").bitcast(I32))
             return words
 
-        def load_gains(name, src):
-            gains = held(name, [P, 4, S], F32)
+        def load_gains(name, src, t0, t1):
+            gains = held(name, [P, t1 - t0, S], F32)
             for q in (0, 2, 1, 3):
-                nc.sync.dma_start(gains[32 * q : 32 * q + 32], src.rearrange("(u t) j -> u t j", t=4))
-            return gains
+                nc.sync.dma_start(gains[32 * q : 32 * q + 32], src.rearrange("(u t) j -> u t j", t=4)[:, t0:t1, :])
+            return [gains[:, t, :] for t in range(t1 - t0)]
 
         def gather(name, window, lst, dtype):
             picked = held(name, [P, S], dtype)
@@ -70,23 +78,22 @@ def tile_list_crowd_steering_features_kernel(
 
         def load_weight(name, src):
             raws = {}
-            for half in range(2):
-                for a in range(2):
-                    raw = held(f"{name}_raw{half}{a}", [P, 4, 512], F32, tag=f"stage{2 * half + a}")
+            for a in range(2):
+                for half in range(2):
+                    raw = held(f"{name}_raw{half}{a}", [P, 4, 512], F32, tag=f"stage{2 * a + half}")
                     rows = src[512 * a : 512 * (a + 1), 512 * half : 512 * (half + 1)]
                     nc.sync.dma_start(raw[:], rows.rearrange("(p j) c -> p j c", j=4))
                     raws[half, a] = raw
             return raws
 
-        def quantise_weight(name, raws, half, tag):
-            rounded = held(f"{name}_bf{half}", [P, 2, 2048], BF16, tag=tag)
-            for a in range(2):
+        def quantise_weight(name, raws, a, rounded):
+            for half in range(2):
                 nc.scalar.copy(
-                    rounded[:, a, :].rearrange("p (t m j) -> p m t j", t=4, j=4),
+                    rounded[:, half, :].rearrange("p (t m j) -> p m t j", t=4, j=4),
                     raws[half, a][:].rearrange("p j (m t) -> p m t j", t=4),
                 )
-            codes = held(f"{name}_codes{half}", [P, 1024], U32)
-            scales = held(f"{name}_scales{half}", [P, 1024], U8)
+            codes = held(f"{name}_codes{a}", [P, 1024], U32)
+            scales = held(f"{name}_scales{a}", [P, 1024], U8)
             nc.vector.quantize_mx(codes[:].bitcast(FP8X4), scales[:], rounded[:].rearrange("p a c -> p (a c)"))
             return codes, scales
 
@@ -100,23 +107,24 @@ def tile_list_crowd_steering_features_kernel(
         half_pi = held("half_pi", [P, 1], F32)
         nc.vector.tensor_scalar(half_pi[:], sin_zero[:], 1.0, math.pi / 2, op0=MULT, op1=ADD)
 
-        tab2_plane = load_scale_rows("tab2_plane", tab2_scales)
+        tab2_plane = load_scale_rows_repeated("tab2_plane", tab2_scales)
         list2 = load_list("list2", offs2)
         w2_raw = held("w2_raw", [P, 2 * H], U8)
         nc.sync.dma_start(w2_raw[:].bitcast(I32), w2_words[0].bitcast(I32))
         tab2 = load_words("tab2", tab2_words[0], "big0")
-        w2_plane = load_scale_rows("w2_plane", w2_scales)
+        w2_plane = load_scale_rows_repeated("w2_plane", w2_scales)
+        list4 = load_list("list4", offs4)
+        gains2 = load_gains("gains2_first", wg2, 0, 1)
         list1 = load_list("list1", offs)
         tab = [load_words("tab0", tab_words[0], "big1")]
-        list4 = load_list("list4", offs4)
-        gains2 = load_gains("gains2", wg2)
+        gains2 = gains2 + load_gains("gains2_rest", wg2, 1, 4)
         tab_plane = load_scale_rows("tab_plane", tab_scales)
         tab.append(load_words("tab1", tab_words[1], "big2"))
         w1_raw = load_weight("w1", w1)
         centre = held("centre", [P, 2, 4], F32)
         nc.sync.dma_start(centre[:], ctr.rearrange("(g p t) -> p g t", g=2, t=4))
         list3 = load_list("list3", offs3)
-        gains1 = load_gains("gains1", wg1)
+        gains1 = load_gains("gains1", wg1, 0, 4)
         styles = []
         for i in range(TILES):
             g, t = divmod(i, 4)
@@ -124,73 +132,102 @@ def tile_list_crowd_steering_features_kernel(
             nc.sync.dma_start(st[:], style.rearrange("(g p t) n -> g t p n", g=2, t=4)[g, t])
             styles.append(st)
 
-        w2_dealt = held("w2_dealt", [P, 2 * H], U8)
-        nc.vector.tensor_copy(
-            w2_dealt[:].rearrange("p (g t m e) -> p g t m e", g=2, t=4, e=2),
-            w2_raw[:].rearrange("p (g m t e) -> p g t m e", g=2, t=4, e=2),
-        )
-        v2_scales = gather("v2_scales", tab2_plane, list2, U8)
-        v2_words = gather("v2_words", tab2, list2, U32)
-        w2_plane_dealt = held("w2_plane_dealt", [P, H], U8)
-        for g in range(2):
-            cols = slice(512 * g, 512 * (g + 1))
+        w2_dealt = held("w2_dealt", [P, 2, H], U8)
+        w2_plane_dealt = held("w2_plane_dealt", [P, 2, 512], U8)
+
+        def deal_words(g):
             nc.vector.tensor_copy(
-                w2_plane_dealt[:, cols].rearrange("p (t m) -> p t m", t=4),
-                w2_plane[:, cols].rearrange("p (m t) -> p t m", t=4),
+                w2_dealt[:, g, :].rearrange("p (t m e) -> p t m e", t=4, e=2),
+                w2_raw[:, H * g : H * (g + 1)].rearrange("p (m t e) -> p t m e", t=4, e=2),
             )
 
-        h2 = []
-        for i in range(TILES):
-            acc = bank(i, f"angle{i}")
-            nc.tensor.matmul_mx(
-                acc[:],
-                lhsT=w2_dealt[:, 2 * P * i : 2 * P * (i + 1)].bitcast(FP4X4),
-                lhsT_scale=w2_plane_dealt[:, P * i : P * (i + 1)],
-                rhs=v2_words[:].bitcast(FP8X4),
-                rhs_scale=v2_scales[:],
-                start=True,
-                stop=True,
+        def deal_scales(g):
+            nc.vector.tensor_copy(
+                w2_plane_dealt[:, g, :].rearrange("p (t m) -> p t m", t=4),
+                w2_plane[:, 512 * g : 512 * (g + 1)].rearrange("p (m t) -> p t m", t=4),
             )
+
+        v2_scales = gather("v2_scales", tab2_plane, list2, U8)
+        deal_words(0)
+        v2_words = held("v2_words", [P, S], U32)
+        halves = [slice(0, S // 2), slice(S // 2, S)]
+        for cols in halves:
+            entries = slice(cols.start // 16, cols.stop // 16)
+            nc.vector.tensor_copy(v2_words[:, cols], tab2[:].bitcast(U32).indirect(list2[:, entries]))
+            if cols.start == 0:
+                deal_scales(0)
+        deal_words(1)
+        deal_scales(1)
+
+        h2, h1, pages = {}, {}, {}
+
+        def runners(i, pieces):
+            g, t = divmod(i, 4)
             h = held(f"h2_{i}", [P, S], F32, tag="h", bufs=10)
-            nc.scalar.activation(h[:], acc[:], ACT.Abs)
-            nc.scalar.activation(h[:], h[:], ACT.Sin, bias=half_pi[:], scale=-1.0)
-            nc.gpsimd.tensor_tensor(h[:], h[:], gains2[:, i % 4, :], MULT)
-            h2.append(h)
+            for n, cols in enumerate(pieces):
+                acc = bank(i + 7 * n, f"angle{i}_{n}")
+                nc.tensor.matmul_mx(
+                    acc[:, cols],
+                    lhsT=w2_dealt[:, g, 2 * P * t : 2 * P * (t + 1)].bitcast(FP4X4),
+                    lhsT_scale=w2_plane_dealt[:, g, P * t : P * (t + 1)],
+                    rhs=v2_words[:, cols].bitcast(FP8X4),
+                    rhs_scale=v2_scales[:, cols],
+                    start=True,
+                    stop=True,
+                )
+                nc.scalar.activation(h[:, cols], acc[:, cols], ACT.Abs)
+                nc.scalar.activation(h[:, cols], h[:, cols], ACT.Sin, bias=half_pi[:], scale=-1.0)
+            h2[i] = h
 
-        pages = {}
+        def weigh_runners(i):
+            nc.gpsimd.tensor_tensor(h2[i][:], h2[i][:], gains2[i % 4], MULT)
 
-        def place_runners(i, tag):
-            pages[i] = held(f"page{i}", [P, T2], F32, tag=tag)
-            nc.vector.tensor_copy(pages[i][:].indirect(list4[:]), h2[i][:])
+        def place_runners(i, page):
+            pages[i] = page
+            nc.vector.tensor_copy(page[:].indirect(list4[:]), h2[i][:])
 
-        for i in range(5):
-            place_runners(i, f"page{i}")
+        runners(0, halves)
+        pages[0] = held("page0", [P, T2], F32)
+        nc.vector.tensor_tensor(pages[0][:].indirect(list4[:]), h2[0][:], gains2[0], MULT)
+        for i in range(1, 3):
+            runners(i, [slice(0, S)])
+            weigh_runners(i)
+            place_runners(i, held(f"page{i}", [P, T2], F32))
 
         v_words = [gather(f"v_words{a}", tab[a], list1, U32) for a in range(2)]
         v_scales = gather("v_scales", tab_plane, list1, U8)
-        h1 = []
-        for half in range(2):
-            codes, scales = quantise_weight("w1", w1_raw, half, f"round{half}")
-            place_runners(5 + half, f"round{half}")
-            for t in range(4):
-                i = 4 * half + t
-                acc = bank(i, f"dist{i}")
-                for a in range(2):
-                    cols = slice(512 * a + P * t, 512 * a + P * (t + 1))
-                    nc.tensor.matmul_mx(
-                        acc[:],
-                        lhsT=codes[:, cols].bitcast(FP8X4),
-                        lhsT_scale=scales[:, cols],
-                        rhs=v_words[a][:].bitcast(FP8X4),
-                        rhs_scale=v_scales[4 * a : P, :],
-                        start=(a == 0),
-                        stop=(a == 1),
-                    )
-                h = held(f"h1_{i}", [P, S], F32, tag="h", bufs=10)
-                nc.scalar.activation(h[:], acc[:], ACT.Square, bias=centre[:, half, t : t + 1], scale=-1.0)
-                nc.scalar.activation(h[:], h[:], ACT.Exp, scale=-1.0)
-                nc.gpsimd.tensor_tensor(h[:], h[:], gains1[:, t, :], MULT)
-                h1.append(h)
+        w1_q = [
+            quantise_weight("w1", w1_raw, 0, held("w1_bf0", [P, 2, 2048], BF16, tag="round0")),
+            quantise_weight(
+                "w1", w1_raw, 1, shared.tile([P, 2, 2048], BF16, name="w1_bf1", offset=0, align_bytes=64)
+            ),
+        ]
+        for i in range(3, TILES):
+            runners(i, [slice(0, S)])
+            weigh_runners(i)
+        place_runners(3, held("page3", [P, T2], F32, tag="round0"))
+        for i in (4, 5):
+            place_runners(i, shared.tile([P, T2], F32, name=f"page{i}", offset=4096 * (i - 4), align_bytes=64))
+        for i in range(TILES):
+            half, t = divmod(i, 4)
+            acc = bank(i, f"dist{i}")
+            cols = slice(P * i, P * (i + 1))
+            for a in range(2):
+                codes, scales = w1_q[a]
+                nc.tensor.matmul_mx(
+                    acc[:],
+                    lhsT=codes[:, cols].bitcast(FP8X4),
+                    lhsT_scale=scales[:, cols],
+                    rhs=v_words[a][:].bitcast(FP8X4),
+                    rhs_scale=v_scales[4 * a : P, :],
+                    start=(a == 0),
+                    stop=(a == 1),
+                )
+            h = held(f"h1_{i}", [P, S], F32, tag="h", bufs=10)
+            nc.scalar.activation(h[:], acc[:], ACT.Square, bias=centre[:, half, t : t + 1], scale=-1.0)
+            nc.scalar.activation(h[:], h[:], ACT.Exp, scale=-1.0)
+            nc.gpsimd.tensor_tensor(h[:], h[:], gains1[t], MULT)
+            h1[i] = h
 
         w3_raw = load_weight("w3", w3)
         z_rows = [held(f"z_rows{g}", [P, CHUNKS, 4, CHUNK], BF16, tag=("gains1", "big1")[g]) for g in range(2)]
@@ -225,31 +262,31 @@ def tile_list_crowd_steering_features_kernel(
                 z_woven[g][:, c0:c1].rearrange("p c n t -> p (c n t)"),
             )
 
-        for i in range(4):
+        for i in range(6):
             place_walkers(i)
             apply_style(i, slice(0, 2))
             apply_style(i, slice(2, 4))
-        w3_q = [quantise_weight("w3", w3_raw, half, f"round{2 + half}") for half in range(2)]
+        w3_q = [
+            quantise_weight("w3", w3_raw, a, held(f"w3_bf{a}", [P, 2, 2048], BF16, tag=f"round{2 + a}"))
+            for a in range(2)
+        ]
         z_woven[0] = held("z_woven0", [P, CHUNKS, CHUNK, 4], BF16, tag="stage3")
         for c in range(CHUNKS):
             weave(nc.scalar.copy, 0, c)
-        z_woven[1] = held("z_woven1", [P, CHUNKS, CHUNK, 4], BF16, tag="round2")
-        place_walkers(4)
-        apply_style(4, slice(0, 2))
-        apply_style(4, slice(2, 4))
+        z_woven[1] = held("z_woven1", [P, CHUNKS, CHUNK, 4], BF16, tag="round3")
+        place_runners(6, held("page6", [P, T2], F32, tag="round2"))
+        place_walkers(6)
         quantise_z(0, 0, CHUNKS)
-        for i in range(5, 7):
-            place_walkers(i)
-            apply_style(i, slice(0, 2))
-            apply_style(i, slice(2, 4))
-        place_runners(7, "stage3")
+        apply_style(6, slice(0, 1))
+        apply_style(6, slice(1, 4))
+        place_runners(7, held("page7", [P, T2], F32, tag="stage3"))
         place_walkers(7)
 
         def project(acc, c, g_out, pair, a):
-            codes, scales = w3_q[g_out]
+            codes, scales = w3_q[a]
             for e in range(2):
                 t = 2 * pair + e
-                cols = slice(512 * a + P * t, 512 * a + P * (t + 1))
+                cols = slice(512 * g_out + P * t, 512 * g_out + P * (t + 1))
                 agents = slice(CHUNK * c, CHUNK * (c + 1))
                 nc.tensor.matmul_mx(
                     acc[:, CHUNK * e : CHUNK * (e + 1)],
@@ -269,34 +306,40 @@ def tile_list_crowd_steering_features_kernel(
         y_codes = [held(f"y_codes{g}", [P, T2], U32) for g in range(2)]
         y_scales = held("y_scales", [P, 2, T2], U8)
         y_rows = out_0.rearrange("(g p t) n -> g p t n", g=2, t=4)
-        for c in range(CHUNKS):
+        y_tags = ("stage0", "stage1", "stage2", "big2")
+        y = {(half, g): held(f"y{half}{g}", [P, 4, 512], F32, tag=y_tags[2 * half + g]) for half in range(2) for g in range(2)}
+        order = [(c, g) for c in (0, 1) for g in range(2)] + [(c, g) for g in range(2) for c in (2, 3)]
+        for step, (c, g_out) in enumerate(order):
+            half = c // 2
+            both = slice(512 * half, 512 * (half + 1))
             agents = slice(CHUNK * c, CHUNK * (c + 1))
-            for g_out in range(2):
-                if g_out == 0:
-                    y_pair = held(f"y{c}", [P, 2, 4, CHUNK], F32, tag=("stage0", "stage1", "stage2", "big2")[c])
-                y = y_pair[:, g_out]
-                for pair in range(2):
-                    acc = bank(4 * c + 2 * g_out + pair, f"y{c}{g_out}{pair}")
-                    for a in range(2):
-                        project(acc, c, g_out, pair, a)
-                    nc.scalar.copy(y[:, 2 * pair : 2 * pair + 2, :].rearrange("p t n -> p (t n)"), acc[:])
-                nc.sync.dma_start(y_rows[g_out][:, :, agents], y)
-                y_woven = held(f"y_woven{c}{g_out}", [P, CHUNK, 4], BF16, tag=f"round{g_out}")
-                nc.vector.tensor_copy(
-                    y_woven[:].rearrange("p (n i) t -> p n t i", i=4),
-                    y.rearrange("p t (n i) -> p n t i", i=4),
+            local = slice(CHUNK * (c % 2), CHUNK * (c % 2 + 1))
+            rows = y[half, g_out]
+            for pair in range(2):
+                slots = slice(2 * pair, 2 * pair + 2)
+                acc = bank(2 * step + pair, f"y{c}{g_out}{pair}")
+                for a in range(2):
+                    project(acc, c, g_out, pair, a)
+                nc.scalar.copy(rows[:, slots, local], acc[:].rearrange("p (t n) -> p t n", t=2))
+                if half == 0:
+                    nc.sync.dma_start(y_rows[g_out][:, slots, agents], rows[:, slots, local])
+                elif c % 2 == 1:
+                    nc.sync.dma_start(y_rows[g_out][:, slots, both], rows[:, slots, :])
+            y_woven = held(f"y_woven{c}{g_out}", [P, CHUNK, 4], BF16, tag=f"page{step % 2}")
+            nc.vector.tensor_copy(
+                y_woven[:].rearrange("p (n i) t -> p n t i", i=4),
+                rows[:, :, local].rearrange("p t (n i) -> p n t i", i=4),
+            )
+            nc.vector.quantize_mx(
+                y_codes[g_out][:, agents].bitcast(FP8X4),
+                y_scales[:, g_out, agents],
+                y_woven[:].rearrange("p n t -> p (n t)"),
+            )
+            if c % 2 == 1:
+                nc.sync.dma_start(
+                    out_1[g_out].rearrange("p n i -> p (n i)").bitcast(I32)[:, both],
+                    y_codes[g_out][:, both].bitcast(I32),
                 )
-                nc.vector.quantize_mx(
-                    y_codes[g_out][:, agents].bitcast(FP8X4),
-                    y_scales[:, g_out, agents],
-                    y_woven[:].rearrange("p n t -> p (n t)"),
-                )
-                if c % 2 == 1:
-                    both = slice(CHUNK * (c - 1), CHUNK * (c + 1))
-                    nc.sync.dma_start(
-                        out_1[g_out].rearrange("p n i -> p (n i)").bitcast(I32)[:, both],
-                        y_codes[g_out][:, both].bitcast(I32),
-                    )
         for q in range(4):
             nc.sync.dma_start(
                 out_2[:, 4 * q : 4 * q + 4, :].rearrange("g r n -> r g n").bitcast(I32),

@@ -76,21 +76,20 @@ def tile_list_crowd_steering_features_kernel(
             nc.vector.tensor_copy(picked[:], window[:].bitcast(dtype).indirect(lst[:]))
             return picked
 
-        def load_weight(name, src):
-            raws = {}
-            for a in range(2):
-                for half in range(2):
-                    raw = held(f"{name}_raw{half}{a}", [P, 4, 512], F32, tag=f"stage{2 * a + half}")
-                    rows = src[512 * a : 512 * (a + 1), 512 * half : 512 * (half + 1)]
-                    nc.sync.dma_start(raw[:], rows.rearrange("(p j) c -> p j c", j=4))
-                    raws[half, a] = raw
+        def load_weight(name, src, a):
+            raws = []
+            for half in range(2):
+                raw = held(f"{name}_raw{half}{a}", [P, 4, 512], F32, tag=f"stage{2 * a + half}")
+                rows = src[512 * a : 512 * (a + 1), 512 * half : 512 * (half + 1)]
+                nc.sync.dma_start(raw[:], rows.rearrange("(p j) c -> p j c", j=4))
+                raws.append(raw)
             return raws
 
         def quantise_weight(name, raws, a, rounded):
             for half in range(2):
                 nc.scalar.copy(
-                    rounded[:, half, :].rearrange("p (t m j) -> p m t j", t=4, j=4),
-                    raws[half, a][:].rearrange("p j (m t) -> p m t j", t=4),
+                    rounded[:, half, :].rearrange("p (t m u e) -> p m u t e", t=4, u=2, e=2),
+                    raws[a][half][:].rearrange("p (u e) (m t) -> p m u t e", e=2, t=4),
                 )
             codes = held(f"{name}_codes{a}", [P, 1024], U32)
             scales = held(f"{name}_scales{a}", [P, 1024], U8)
@@ -114,13 +113,14 @@ def tile_list_crowd_steering_features_kernel(
         tab2 = load_words("tab2", tab2_words[0], "big0")
         w2_plane = load_scale_rows_repeated("w2_plane", w2_scales)
         list4 = load_list("list4", offs4)
-        gains2 = load_gains("gains2_first", wg2, 0, 1)
+        gains2 = load_gains("gains2_first", wg2, 0, 2)
         list1 = load_list("list1", offs)
         tab = [load_words("tab0", tab_words[0], "big1")]
-        gains2 = gains2 + load_gains("gains2_rest", wg2, 1, 4)
+        gains2 = gains2 + load_gains("gains2_rest", wg2, 2, 4)
         tab_plane = load_scale_rows("tab_plane", tab_scales)
+        w1_raw = [load_weight("w1", w1, 0)]
         tab.append(load_words("tab1", tab_words[1], "big2"))
-        w1_raw = load_weight("w1", w1)
+        w1_raw.append(load_weight("w1", w1, 1))
         centre = held("centre", [P, 2, 4], F32)
         nc.sync.dma_start(centre[:], ctr.rearrange("(g p t) -> p g t", g=2, t=4))
         list3 = load_list("list3", offs3)
@@ -229,7 +229,7 @@ def tile_list_crowd_steering_features_kernel(
             nc.gpsimd.tensor_tensor(h[:], h[:], gains1[t], MULT)
             h1[i] = h
 
-        w3_raw = load_weight("w3", w3)
+        w3_raw = [load_weight("w3", w3, a) for a in range(2)]
         z_rows = [held(f"z_rows{g}", [P, CHUNKS, 4, CHUNK], BF16, tag=("gains1", "big1")[g]) for g in range(2)]
         z_woven = [None, None]
         z_codes = [held(f"z_codes{g}", [P, T2], U32) for g in range(2)]
@@ -306,6 +306,24 @@ def tile_list_crowd_steering_features_kernel(
         y_codes = [held(f"y_codes{g}", [P, T2], U32) for g in range(2)]
         y_scales = held("y_scales", [P, 2, T2], U8)
         y_rows = out_0.rearrange("(g p t) n -> g p t n", g=2, t=4)
+
+        def emit_planes(copy, values, g_out, agents, tag):
+            width = agents.stop - agents.start
+            woven = held(f"y_woven{g_out}_{agents.start}", [P, width, 4], BF16, tag=tag)
+            copy(
+                woven[:].rearrange("p (n i) t -> p n t i", i=4),
+                values.rearrange("p t (n i) -> p n t i", i=4),
+            )
+            nc.vector.quantize_mx(
+                y_codes[g_out][:, agents].bitcast(FP8X4),
+                y_scales[:, g_out, agents],
+                woven[:].rearrange("p n t -> p (n t)"),
+            )
+            nc.sync.dma_start(
+                out_1[g_out].rearrange("p n i -> p (n i)").bitcast(I32)[:, agents],
+                y_codes[g_out][:, agents].bitcast(I32),
+            )
+
         y_tags = ("stage0", "stage1", "stage2", "big2")
         y = {(half, g): held(f"y{half}{g}", [P, 4, 512], F32, tag=y_tags[2 * half + g]) for half in range(2) for g in range(2)}
         order = [(c, g) for c in (0, 1) for g in range(2)] + [(c, g) for g in range(2) for c in (2, 3)]
@@ -325,23 +343,13 @@ def tile_list_crowd_steering_features_kernel(
                     nc.sync.dma_start(y_rows[g_out][:, slots, agents], rows[:, slots, local])
                 elif c % 2 == 1:
                     nc.sync.dma_start(y_rows[g_out][:, slots, both], rows[:, slots, :])
-            y_woven = held(f"y_woven{c}{g_out}", [P, CHUNK, 4], BF16, tag=f"page{step % 2}")
-            nc.vector.tensor_copy(
-                y_woven[:].rearrange("p (n i) t -> p n t i", i=4),
-                rows[:, :, local].rearrange("p t (n i) -> p n t i", i=4),
-            )
-            nc.vector.quantize_mx(
-                y_codes[g_out][:, agents].bitcast(FP8X4),
-                y_scales[:, g_out, agents],
-                y_woven[:].rearrange("p n t -> p (n t)"),
-            )
-            if c % 2 == 1:
-                nc.sync.dma_start(
-                    out_1[g_out].rearrange("p n i -> p (n i)").bitcast(I32)[:, both],
-                    y_codes[g_out][:, both].bitcast(I32),
-                )
+            last = (half, g_out) == (1, 1)
+            if last:
+                emit_planes(nc.scalar.copy if c == 3 else nc.vector.tensor_copy, rows[:, :, local], g_out, agents, f"page{step % 2}")
+            elif c % 2 == 1:
+                emit_planes(nc.vector.tensor_copy, rows[:], g_out, both, f"page{step % 2}")
         for q in range(4):
-            nc.sync.dma_start(
+            nc.scalar.dma_start(
                 out_2[:, 4 * q : 4 * q + 4, :].rearrange("g r n -> r g n").bitcast(I32),
                 y_scales[32 * q : 32 * q + 4].bitcast(I32),
             )

@@ -20,7 +20,7 @@ K, K2, H, N, T, S, T2 = 1024, 512, 1024, 1024, 2048, 512, 1024
 FLOPS = 2 * K * H * S + 2 * K2 * H * S + 2 * H * N * T2
 CHUNK = 256
 CHUNKS = T2 // CHUNK
-TILES = H // P
+PAGES = H // P
 
 
 def tile_list_crowd_steering_features_kernel(
@@ -42,16 +42,18 @@ def tile_list_crowd_steering_features_kernel(
             nc.sync.dma_start(lst[:], src)
             return lst
 
-        def load_scale_rows(name, src):
-            passes, cols = src.shape[0], src.shape[2]
+        def zeroed_plane(engine, name, cols):
             plane = held(name, [P, cols], U8)
-            nc.vector.memset(plane[:].bitcast(I32), 0)
+            engine.memset(plane[:].bitcast(I32), 0)
+            return plane
+
+        def load_scale_rows(queue, plane, src):
+            passes = src.shape[0]
             for q in range(4):
-                nc.sync.dma_start(
+                queue.dma_start(
                     plane[32 * q : 32 * q + 4 * passes, :].bitcast(I32),
                     src[:, 4 * q : 4 * q + 4, :].bitcast(I32),
                 )
-            return plane
 
         def load_scale_rows_repeated(name, src):
             plane = held(name, [P, src.shape[2]], U8)
@@ -71,28 +73,31 @@ def tile_list_crowd_steering_features_kernel(
                 nc.sync.dma_start(gains[32 * q : 32 * q + 32], src.rearrange("(u t) j -> u t j", t=4)[:, t0:t1, :])
             return [gains[:, t, :] for t in range(t1 - t0)]
 
+        def load_weight(name, src, a, half, tag):
+            raw = held(f"{name}_raw{a}{half}", [P, 4, 512], F32, tag=tag)
+            rows = src[512 * a : 512 * (a + 1), 512 * half : 512 * (half + 1)]
+            nc.sync.dma_start(raw[:], rows.rearrange("(p j) c -> p j c", j=4))
+            return raw
+
+        def load_style(i):
+            g, t = divmod(i, 4)
+            st = held(f"style{i}", [P, T2], F32)
+            nc.sync.dma_start(st[:], style.rearrange("(g p t) n -> g t p n", g=2, t=4)[g, t])
+            return st
+
         def gather(name, window, lst, dtype):
             picked = held(name, [P, S], dtype)
             nc.vector.tensor_copy(picked[:], window[:].bitcast(dtype).indirect(lst[:]))
             return picked
 
-        def load_weight(name, src, a):
-            raws = []
-            for half in range(2):
-                raw = held(f"{name}_raw{half}{a}", [P, 4, 512], F32, tag=f"stage{2 * a + half}")
-                rows = src[512 * a : 512 * (a + 1), 512 * half : 512 * (half + 1)]
-                nc.sync.dma_start(raw[:], rows.rearrange("(p j) c -> p j c", j=4))
-                raws.append(raw)
-            return raws
-
-        def quantise_weight(name, raws, a, rounded):
-            for half in range(2):
+        def quantise_weight(name, raws, rounded):
+            for n, raw in enumerate(raws):
                 nc.scalar.copy(
-                    rounded[:, half, :].rearrange("p (t m u e) -> p m u t e", t=4, u=2, e=2),
-                    raws[a][half][:].rearrange("p (u e) (m t) -> p m u t e", e=2, t=4),
+                    rounded[:, n, :].rearrange("p (t m u e) -> p m u t e", t=4, u=2, e=2),
+                    raw[:].rearrange("p (u e) (m t) -> p m u t e", e=2, t=4),
                 )
-            codes = held(f"{name}_codes{a}", [P, 1024], U32)
-            scales = held(f"{name}_scales{a}", [P, 1024], U8)
+            codes = held(f"{name}_codes", [P, 1024], U32)
+            scales = held(f"{name}_scales", [P, 1024], U8)
             nc.vector.quantize_mx(codes[:].bitcast(FP8X4), scales[:], rounded[:].rearrange("p a c -> p (a c)"))
             return codes, scales
 
@@ -101,11 +106,7 @@ def tile_list_crowd_steering_features_kernel(
 
         zero = held("zero", [P, 1], F32)
         nc.vector.memset(zero[:], 0.0)
-        sin_zero = held("sin_zero", [P, 1], F32)
-        nc.scalar.activation(sin_zero[:], zero[:], ACT.Sin)
-        half_pi = held("half_pi", [P, 1], F32)
-        nc.vector.tensor_scalar(half_pi[:], sin_zero[:], 1.0, math.pi / 2, op0=MULT, op1=ADD)
-
+        tab_plane = zeroed_plane(nc.vector, "tab_plane", T)
         tab2_plane = load_scale_rows_repeated("tab2_plane", tab2_scales)
         list2 = load_list("list2", offs2)
         w2_raw = held("w2_raw", [P, 2 * H], U8)
@@ -113,24 +114,26 @@ def tile_list_crowd_steering_features_kernel(
         tab2 = load_words("tab2", tab2_words[0], "big0")
         w2_plane = load_scale_rows_repeated("w2_plane", w2_scales)
         list4 = load_list("list4", offs4)
-        gains2 = load_gains("gains2_first", wg2, 0, 2)
+        sin_zero = held("sin_zero", [P, 1], F32)
+        nc.scalar.activation(sin_zero[:], zero[:], ACT.Sin)
+        half_pi = held("half_pi", [P, 1], F32)
+        nc.vector.tensor_scalar(half_pi[:], sin_zero[:], 1.0, math.pi / 2, op0=MULT, op1=ADD)
+
+        gains2 = load_gains("gains2_first", wg2, 0, 1)
         list1 = load_list("list1", offs)
-        tab = [load_words("tab0", tab_words[0], "big1")]
-        gains2 = gains2 + load_gains("gains2_rest", wg2, 2, 4)
-        tab_plane = load_scale_rows("tab_plane", tab_scales)
-        w1_raw = [load_weight("w1", w1, 0)]
-        tab.append(load_words("tab1", tab_words[1], "big2"))
-        w1_raw.append(load_weight("w1", w1, 1))
+        gains2 = gains2 + load_gains("gains2_rest", wg2, 1, 4)
+        load_scale_rows(nc.sync, tab_plane, tab_scales)
+        tab, w1_raw = [], {}
+        for a in range(2):
+            tab.append(load_words(f"tab{a}", tab_words[a], f"big{1 + a}"))
+            w1_raw[a, 0] = load_weight("w1", w1, a, 0, f"stage{a}")
         centre = held("centre", [P, 2, 4], F32)
         nc.sync.dma_start(centre[:], ctr.rearrange("(g p t) -> p g t", g=2, t=4))
+        for a in range(2):
+            w1_raw[a, 1] = load_weight("w1", w1, a, 1, f"stage{2 + a}")
         list3 = load_list("list3", offs3)
         gains1 = load_gains("gains1", wg1, 0, 4)
-        styles = []
-        for i in range(TILES):
-            g, t = divmod(i, 4)
-            st = held(f"style{i}", [P, T2], F32)
-            nc.sync.dma_start(st[:], style.rearrange("(g p t) n -> g t p n", g=2, t=4)[g, t])
-            styles.append(st)
+        styles = [load_style(i) for i in range(2)]
 
         w2_dealt = held("w2_dealt", [P, 2, H], U8)
         w2_plane_dealt = held("w2_plane_dealt", [P, 2, 512], U8)
@@ -147,100 +150,140 @@ def tile_list_crowd_steering_features_kernel(
                 w2_plane[:, 512 * g : 512 * (g + 1)].rearrange("p (m t) -> p t m", t=4),
             )
 
+        halves = [slice(0, S // 2), slice(S // 2, S)]
+
+        def entries(cols):
+            return slice(cols.start // 16, cols.stop // 16)
+
         v2_scales = gather("v2_scales", tab2_plane, list2, U8)
         deal_words(0)
+        deal_scales(0)
         v2_words = held("v2_words", [P, S], U32)
-        halves = [slice(0, S // 2), slice(S // 2, S)]
         for cols in halves:
-            entries = slice(cols.start // 16, cols.stop // 16)
-            nc.vector.tensor_copy(v2_words[:, cols], tab2[:].bitcast(U32).indirect(list2[:, entries]))
-            if cols.start == 0:
-                deal_scales(0)
+            nc.vector.tensor_copy(v2_words[:, cols], tab2[:].bitcast(U32).indirect(list2[:, entries(cols)]))
         deal_words(1)
         deal_scales(1)
 
         h2, h1, pages = {}, {}, {}
 
-        def runners(i, pieces):
+        def angle(i, h, cols, acc):
             g, t = divmod(i, 4)
-            h = held(f"h2_{i}", [P, S], F32, tag="h", bufs=10)
+            nc.tensor.matmul_mx(
+                acc[:, cols],
+                lhsT=w2_dealt[:, g, 2 * P * t : 2 * P * (t + 1)].bitcast(FP4X4),
+                lhsT_scale=w2_plane_dealt[:, g, P * t : P * (t + 1)],
+                rhs=v2_words[:, cols].bitcast(FP8X4),
+                rhs_scale=v2_scales[:, cols],
+                start=True,
+                stop=True,
+            )
+            nc.scalar.activation(h[:, cols], acc[:, cols], ACT.Abs)
+
+        def cosine(h):
+            nc.scalar.activation(h, h, ACT.Sin, bias=half_pi[:], scale=-1.0)
+
+        def runners(first, count):
+            h = held(f"h2_{first}", [P, count, S], F32, tag="h", bufs=5)
+            for n in range(count):
+                angle(first + n, h[:, n, :], slice(0, S), bank(first + n, f"angle{first + n}"))
+                h2[first + n] = h[:, n, :]
+            cosine(h[:])
+
+        def walkers(first, w1_q):
+            h = held(f"h1_{first}", [P, 2, S], F32, tag="h", bufs=5)
+            codes, scales = w1_q
+            for n in range(2):
+                half, t = divmod(first + n, 4)
+                acc = bank(first + n, f"dist{first + n}")
+                for a in range(2):
+                    cols = slice(512 * a + P * t, 512 * a + P * (t + 1))
+                    nc.tensor.matmul_mx(
+                        acc[:],
+                        lhsT=codes[:, cols].bitcast(FP8X4),
+                        lhsT_scale=scales[:, cols],
+                        rhs=v_words[a][:].bitcast(FP8X4),
+                        rhs_scale=v_scales[4 * a : P, :],
+                        start=(a == 0),
+                        stop=(a == 1),
+                    )
+                nc.scalar.activation(h[:, n, :], acc[:], ACT.Square, bias=centre[:, half, t : t + 1], scale=-1.0)
+                h1[first + n] = h[:, n, :]
+            nc.scalar.activation(h[:], h[:], ACT.Exp, scale=-1.0)
+            for n in range(2):
+                nc.gpsimd.tensor_tensor(h[:, n, :], h[:, n, :], gains1[(first + n) % 4], MULT)
+
+        def weigh(name, h, gains):
+            weighed = held(name, [P, S], F32, tag="weighed", bufs=3)
+            nc.gpsimd.tensor_tensor(weighed[:], h, gains, MULT)
+            return weighed[:]
+
+        def place(i, lst, weighed):
+            nc.vector.tensor_copy(pages[i][:].indirect(lst[:]), weighed)
+
+        def new_page(i):
+            if 3 <= i <= 6:
+                pages[i] = shared.tile([P, T2], F32, name=f"page{i}", offset=4096 * (i - 3), align_bytes=64)
+            else:
+                pages[i] = held(f"page{i}", [P, T2], F32, tag={2: "big2", 7: "stage3"}.get(i))
+
+        def fused_features(i, pieces):
+            h = held(f"h2_{i}", [P, S], F32, tag="weighed", bufs=3)
             for n, cols in enumerate(pieces):
-                acc = bank(i + 7 * n, f"angle{i}_{n}")
-                nc.tensor.matmul_mx(
-                    acc[:, cols],
-                    lhsT=w2_dealt[:, g, 2 * P * t : 2 * P * (t + 1)].bitcast(FP4X4),
-                    lhsT_scale=w2_plane_dealt[:, g, P * t : P * (t + 1)],
-                    rhs=v2_words[:, cols].bitcast(FP8X4),
-                    rhs_scale=v2_scales[:, cols],
-                    start=True,
-                    stop=True,
-                )
-                nc.scalar.activation(h[:, cols], acc[:, cols], ACT.Abs)
-                nc.scalar.activation(h[:, cols], h[:, cols], ACT.Sin, bias=half_pi[:], scale=-1.0)
+                angle(i, h[:], cols, bank(i + 7 * n, f"angle{i}_{n}"))
+                cosine(h[:, cols])
             h2[i] = h
 
-        def weigh_runners(i):
-            nc.gpsimd.tensor_tensor(h2[i][:], h2[i][:], gains2[i % 4], MULT)
+        def place_fused(i, pieces):
+            new_page(i)
+            for cols in pieces:
+                nc.vector.tensor_tensor(
+                    pages[i][:].indirect(list4[:, entries(cols)]), h2[i][:, cols], gains2[i][:, cols], MULT
+                )
 
-        def place_runners(i, page):
-            pages[i] = page
-            nc.vector.tensor_copy(page[:].indirect(list4[:]), h2[i][:])
-
-        runners(0, halves)
-        pages[0] = held("page0", [P, T2], F32)
-        nc.vector.tensor_tensor(pages[0][:].indirect(list4[:]), h2[0][:], gains2[0], MULT)
-        for i in range(1, 3):
-            runners(i, [slice(0, S)])
-            weigh_runners(i)
-            place_runners(i, held(f"page{i}", [P, T2], F32))
-
-        v_words = [gather(f"v_words{a}", tab[a], list1, U32) for a in range(2)]
+        whole = [slice(0, S)]
+        for i in range(3):
+            fused_features(i, halves if i == 0 else whole)
+        for i in range(2):
+            place_fused(i, halves if i == 0 else whole)
+        runners(3, 2)
         v_scales = gather("v_scales", tab_plane, list1, U8)
-        w1_q = [
-            quantise_weight("w1", w1_raw, 0, held("w1_bf0", [P, 2, 2048], BF16, tag="round0")),
+        v_words = [gather(f"v_words{a}", tab[a], list1, U32) for a in range(2)]
+        place_fused(2, whole)
+        w1_q = []
+        for half in range(2):
+            rounded = shared.tile([P, 2, 2048], BF16, name=f"w1_bf{half}", offset=(2048, 12288)[half], align_bytes=64)
+            w1_q.append(quantise_weight(f"w1_{half}", [w1_raw[a, half] for a in range(2)], rounded))
+            if half == 0:
+                runners(5, 2)
+                runners(7, 1)
+        weighed = {i: weigh(f"weighed{i}", h2[i], gains2[i % 4]) for i in range(3, PAGES)}
+        for first in range(0, PAGES, 2):
+            walkers(first, w1_q[first // 4])
+
+        w3_raw = {}
+        for a in range(2):
+            for g in range(2):
+                w3_raw[a, g] = load_weight("w3", w3, a, g, f"stage{2 * a + g}")
+            styles += [load_style(i) for i in (2 + 2 * a, 3 + 2 * a)]
+        styles += [load_style(i) for i in (6, 7)]
+        w3_q = [
+            quantise_weight("w3_0", [w3_raw[0, g] for g in range(2)], held("w3_bf0", [P, 2, 2048], BF16, tag="big1")),
             quantise_weight(
-                "w1", w1_raw, 1, shared.tile([P, 2, 2048], BF16, name="w1_bf1", offset=0, align_bytes=64)
+                "w3_1", [w3_raw[1, g] for g in range(2)],
+                held("w3_bf1", [P, 2, 2048], BF16, tag="round2"),
             ),
         ]
-        for i in range(3, TILES):
-            runners(i, [slice(0, S)])
-            weigh_runners(i)
-        place_runners(3, held("page3", [P, T2], F32, tag="round0"))
-        for i in (4, 5):
-            place_runners(i, shared.tile([P, T2], F32, name=f"page{i}", offset=4096 * (i - 4), align_bytes=64))
-        for i in range(TILES):
-            half, t = divmod(i, 4)
-            acc = bank(i, f"dist{i}")
-            cols = slice(P * i, P * (i + 1))
-            for a in range(2):
-                codes, scales = w1_q[a]
-                nc.tensor.matmul_mx(
-                    acc[:],
-                    lhsT=codes[:, cols].bitcast(FP8X4),
-                    lhsT_scale=scales[:, cols],
-                    rhs=v_words[a][:].bitcast(FP8X4),
-                    rhs_scale=v_scales[4 * a : P, :],
-                    start=(a == 0),
-                    stop=(a == 1),
-                )
-            h = held(f"h1_{i}", [P, S], F32, tag="h", bufs=10)
-            nc.scalar.activation(h[:], acc[:], ACT.Square, bias=centre[:, half, t : t + 1], scale=-1.0)
-            nc.scalar.activation(h[:], h[:], ACT.Exp, scale=-1.0)
-            nc.gpsimd.tensor_tensor(h[:], h[:], gains1[t], MULT)
-            h1[i] = h
 
-        w3_raw = [load_weight("w3", w3, a) for a in range(2)]
-        z_rows = [held(f"z_rows{g}", [P, CHUNKS, 4, CHUNK], BF16, tag=("gains1", "big1")[g]) for g in range(2)]
-        z_woven = [None, None]
+        z_rows = [held(f"z_rows{g}", [P, CHUNKS, 4, CHUNK], BF16, tag=("big0", None)[g]) for g in range(2)]
+        z_woven = [
+            held("z_woven0", [P, CHUNKS, CHUNK, 4], BF16, tag="stage3"),
+            held("z_woven1", [P, CHUNKS, CHUNK, 4], BF16, tag="big1"),
+        ]
         z_codes = [held(f"z_codes{g}", [P, T2], U32) for g in range(2)]
         z_scales = [held(f"z_scales{g}", [P, T2], U8) for g in range(2)]
 
-        def place_walkers(i):
-            nc.vector.tensor_copy(pages[i][:].indirect(list3[:]), h1[i][:])
-
-        def apply_style(i, chunks):
+        def apply_style(engine, i, chunks):
             g, t = divmod(i, 4)
-            engine = nc.vector if i == 7 else nc.gpsimd
             engine.tensor_tensor(
                 z_rows[g][:, chunks, t, :],
                 pages[i][:].rearrange("p (c n) -> p c n", n=CHUNK)[:, chunks, :],
@@ -262,26 +305,6 @@ def tile_list_crowd_steering_features_kernel(
                 z_woven[g][:, c0:c1].rearrange("p c n t -> p (c n t)"),
             )
 
-        for i in range(6):
-            place_walkers(i)
-            apply_style(i, slice(0, 2))
-            apply_style(i, slice(2, 4))
-        w3_q = [
-            quantise_weight("w3", w3_raw, a, held(f"w3_bf{a}", [P, 2, 2048], BF16, tag=f"round{2 + a}"))
-            for a in range(2)
-        ]
-        z_woven[0] = held("z_woven0", [P, CHUNKS, CHUNK, 4], BF16, tag="stage3")
-        for c in range(CHUNKS):
-            weave(nc.scalar.copy, 0, c)
-        z_woven[1] = held("z_woven1", [P, CHUNKS, CHUNK, 4], BF16, tag="round3")
-        place_runners(6, held("page6", [P, T2], F32, tag="round2"))
-        place_walkers(6)
-        quantise_z(0, 0, CHUNKS)
-        apply_style(6, slice(0, 1))
-        apply_style(6, slice(1, 4))
-        place_runners(7, held("page7", [P, T2], F32, tag="stage3"))
-        place_walkers(7)
-
         def project(acc, c, g_out, pair, a):
             codes, scales = w3_q[a]
             for e in range(2):
@@ -298,8 +321,31 @@ def tile_list_crowd_steering_features_kernel(
                     stop=(a == 1 and e == 1),
                 )
 
+        order = [(c, g) for c in (0, 1) for g in range(2)] + [(c, g) for g in range(2) for c in (2, 3)]
+        early = {}
+        steps = ["r3", "r4", "r5", "w0", "w1", "w2", "w3", "r6", "w4", "w5", "w6", "r7", "w7"]
+        for n, step in enumerate(steps):
+            i = int(step[1])
+            if n > 0 and steps[n - 1][0] == "w":
+                done = int(steps[n - 1][1])
+                apply_style(nc.gpsimd, done, slice(0, 2))
+                apply_style(nc.gpsimd, done, slice(2, 4))
+                if done == 3:
+                    for c in range(CHUNKS):
+                        weave(nc.scalar.copy, 0, c)
+                    quantise_z(0, 0, CHUNKS)
+                    for k, (c, g_out) in enumerate(order[:4]):
+                        for pair in range(2):
+                            early[c, g_out, pair] = bank(2 * k + pair, f"y{c}{g_out}{pair}")
+                            project(early[c, g_out, pair], c, g_out, pair, 0)
+            if step[0] == "r":
+                new_page(i)
+                place(i, list4, weighed[i])
+            else:
+                place(i, list3, h1[i])
+
         for c in range(CHUNKS):
-            apply_style(7, slice(c, c + 1))
+            apply_style(nc.vector, 7, slice(c, c + 1))
             weave(nc.scalar.copy if c == 1 else nc.vector.tensor_copy, 1, c)
             quantise_z(1, c, c + 1)
 
@@ -324,9 +370,7 @@ def tile_list_crowd_steering_features_kernel(
                 y_codes[g_out][:, agents].bitcast(I32),
             )
 
-        y_tags = ("stage0", "stage1", "stage2", "big2")
-        y = {(half, g): held(f"y{half}{g}", [P, 4, 512], F32, tag=y_tags[2 * half + g]) for half in range(2) for g in range(2)}
-        order = [(c, g) for c in (0, 1) for g in range(2)] + [(c, g) for g in range(2) for c in (2, 3)]
+        y = {(half, g): held(f"y{half}{g}", [P, 4, 512], F32, tag=f"stage{2 * half + g}") for half in range(2) for g in range(2)}
         for step, (c, g_out) in enumerate(order):
             half = c // 2
             both = slice(512 * half, 512 * (half + 1))
@@ -335,9 +379,12 @@ def tile_list_crowd_steering_features_kernel(
             rows = y[half, g_out]
             for pair in range(2):
                 slots = slice(2 * pair, 2 * pair + 2)
-                acc = bank(2 * step + pair, f"y{c}{g_out}{pair}")
-                for a in range(2):
-                    project(acc, c, g_out, pair, a)
+                if half == 0:
+                    acc = early[c, g_out, pair]
+                else:
+                    acc = bank(2 * step + pair, f"y{c}{g_out}{pair}")
+                    project(acc, c, g_out, pair, 0)
+                project(acc, c, g_out, pair, 1)
                 nc.scalar.copy(rows[:, slots, local], acc[:].rearrange("p (t n) -> p t n", t=2))
                 if half == 0:
                     nc.sync.dma_start(y_rows[g_out][:, slots, agents], rows[:, slots, local])

@@ -21,6 +21,10 @@ FLOPS = 2 * K * H * S + 2 * K2 * H * S + 2 * H * N * T2
 CHUNK = 256
 CHUNKS = T2 // CHUNK
 PAGES = H // P
+ROUNDED = 0
+STAGE = ROUNDED + 2 * 8192
+RING = STAGE + 4 * 8192 + 960
+RING_SLOT = (0, 4096, 2048)
 
 
 def tile_list_crowd_steering_features_kernel(
@@ -30,9 +34,28 @@ def tile_list_crowd_steering_features_kernel(
     nc = tc.nc
     with ExitStack() as ctx:
         lists = ctx.enter_context(tc.tile_pool(name="lists", bufs=1))
+        first = ctx.enter_context(tc.tile_pool(name="first", bufs=1))
+        psum = ctx.enter_context(tc.psum_pool(name="psum", bufs=1))
+
+        def zeroed_plane(name, cols):
+            plane = first.tile([P, cols], U8, name=name, tag=name, align_bytes=64)
+            nc.vector.memset(plane[:].bitcast(I32), 0)
+            return plane
+
+        w2_plane = zeroed_plane("w2_plane", H)
+        zero = first.tile([P, 1], F32, name="zero")
+        nc.vector.memset(zero[:], 0.0)
+        sin_zero = first.tile([P, 1], F32, name="sin_zero")
+        nc.scalar.activation(sin_zero[:], zero[:], ACT.Sin)
+        half_pi = first.tile([P, 1], F32, name="half_pi")
+        nc.vector.tensor_scalar(half_pi[:], sin_zero[:], 1.0, math.pi / 2, op0=MULT, op1=ADD)
+        tab_plane = zeroed_plane("tab_plane", T)
+
         keep = ctx.enter_context(tc.tile_pool(name="keep", bufs=1))
         shared = ctx.enter_context(tc.tile_pool(name="shared", bufs=1))
-        psum = ctx.enter_context(tc.psum_pool(name="psum", bufs=1))
+
+        def placed(name, shape, dtype, offset):
+            return shared.tile(shape, dtype, name=name, offset=offset, align_bytes=64)
 
         def held(name, shape, dtype, tag=None, bufs=1):
             return keep.tile(shape, dtype, name=name, tag=tag or name, bufs=bufs, align_bytes=64)
@@ -42,11 +65,6 @@ def tile_list_crowd_steering_features_kernel(
             nc.sync.dma_start(lst[:], src)
             return lst
 
-        def zeroed_plane(engine, name, cols):
-            plane = held(name, [P, cols], U8)
-            engine.memset(plane[:].bitcast(I32), 0)
-            return plane
-
         def load_scale_rows(queue, plane, src):
             passes = src.shape[0]
             for q in range(4):
@@ -54,13 +72,6 @@ def tile_list_crowd_steering_features_kernel(
                     plane[32 * q : 32 * q + 4 * passes, :].bitcast(I32),
                     src[:, 4 * q : 4 * q + 4, :].bitcast(I32),
                 )
-
-        def load_scale_rows_repeated(name, src):
-            plane = held(name, [P, src.shape[2]], U8)
-            for q in range(4):
-                rows = src[0, 4 * q : 4 * q + 4, :].bitcast(I32)
-                nc.sync.dma_start(plane[32 * q : 32 * q + 32, :].bitcast(I32), rows.partition_broadcast(8))
-            return plane
 
         def load_words(name, src, tag):
             words = held(name, [P, T], I32, tag=tag)
@@ -73,8 +84,11 @@ def tile_list_crowd_steering_features_kernel(
                 nc.sync.dma_start(gains[32 * q : 32 * q + 32], src.rearrange("(u t) j -> u t j", t=4)[:, t0:t1, :])
             return [gains[:, t, :] for t in range(t1 - t0)]
 
-        def load_weight(name, src, a, half, tag):
-            raw = held(f"{name}_raw{a}{half}", [P, 4, 512], F32, tag=tag)
+        def staged(name, shape, dtype, slot, shift=0):
+            return placed(name, shape, dtype, STAGE + 8192 * slot + shift)
+
+        def load_weight(name, src, a, half, slot):
+            raw = staged(f"{name}_raw{a}{half}", [P, 4, 512], F32, slot)
             rows = src[512 * a : 512 * (a + 1), 512 * half : 512 * (half + 1)]
             nc.sync.dma_start(raw[:], rows.rearrange("(p j) c -> p j c", j=4))
             return raw
@@ -90,47 +104,37 @@ def tile_list_crowd_steering_features_kernel(
             nc.vector.tensor_copy(picked[:], window[:].bitcast(dtype).indirect(lst[:]))
             return picked
 
-        def quantise_weight(name, raws, rounded):
+        def quantise_weight(name, raws, rounded, scales):
             for n, raw in enumerate(raws):
                 nc.scalar.copy(
                     rounded[:, n, :].rearrange("p (t m u e) -> p m u t e", t=4, u=2, e=2),
                     raw[:].rearrange("p (u e) (m t) -> p m u t e", e=2, t=4),
                 )
             codes = held(f"{name}_codes", [P, 1024], U32)
-            scales = held(f"{name}_scales", [P, 1024], U8)
             nc.vector.quantize_mx(codes[:].bitcast(FP8X4), scales[:], rounded[:].rearrange("p a c -> p (a c)"))
             return codes, scales
 
         def bank(idx, name):
             return psum.tile([P, 512], F32, name=name, tag=f"bank{idx % 8}")
 
-        zero = held("zero", [P, 1], F32)
-        nc.vector.memset(zero[:], 0.0)
-        tab_plane = zeroed_plane(nc.vector, "tab_plane", T)
-        tab2_plane = load_scale_rows_repeated("tab2_plane", tab2_scales)
+        tab2_plane = held("tab2_plane", [P, T], U8)
+        for q in range(4):
+            rows = tab2_scales[0, 4 * q : 4 * q + 4, :].bitcast(I32)
+            nc.sync.dma_start(tab2_plane[32 * q : 32 * q + 32, :].bitcast(I32), rows.partition_broadcast(8))
         list2 = load_list("list2", offs2)
         w2_raw = held("w2_raw", [P, 2 * H], U8)
         nc.sync.dma_start(w2_raw[:].bitcast(I32), w2_words[0].bitcast(I32))
         tab2 = load_words("tab2", tab2_words[0], "big0")
-        w2_plane = load_scale_rows_repeated("w2_plane", w2_scales)
         list4 = load_list("list4", offs4)
-        sin_zero = held("sin_zero", [P, 1], F32)
-        nc.scalar.activation(sin_zero[:], zero[:], ACT.Sin)
-        half_pi = held("half_pi", [P, 1], F32)
-        nc.vector.tensor_scalar(half_pi[:], sin_zero[:], 1.0, math.pi / 2, op0=MULT, op1=ADD)
-
+        load_scale_rows(nc.sync, w2_plane, w2_scales)
         gains2 = load_gains("gains2_first", wg2, 0, 1)
         list1 = load_list("list1", offs)
         gains2 = gains2 + load_gains("gains2_rest", wg2, 1, 4)
         load_scale_rows(nc.sync, tab_plane, tab_scales)
-        tab, w1_raw = [], {}
-        for a in range(2):
-            tab.append(load_words(f"tab{a}", tab_words[a], f"big{1 + a}"))
-            w1_raw[a, 0] = load_weight("w1", w1, a, 0, f"stage{a}")
+        tab = [load_words(f"tab{a}", tab_words[a], f"big{1 + a}") for a in range(2)]
+        w1_raw = {(a, half): load_weight("w1", w1, a, half, 2 * half + a) for half in range(2) for a in range(2)}
         centre = held("centre", [P, 2, 4], F32)
         nc.sync.dma_start(centre[:], ctr.rearrange("(g p t) -> p g t", g=2, t=4))
-        for a in range(2):
-            w1_raw[a, 1] = load_weight("w1", w1, a, 1, f"stage{2 + a}")
         list3 = load_list("list3", offs3)
         gains1 = load_gains("gains1", wg1, 0, 4)
         styles = [load_style(i) for i in range(2)]
@@ -140,8 +144,8 @@ def tile_list_crowd_steering_features_kernel(
 
         def deal_words(g):
             nc.vector.tensor_copy(
-                w2_dealt[:, g, :].rearrange("p (t m e) -> p t m e", t=4, e=2),
-                w2_raw[:, H * g : H * (g + 1)].rearrange("p (m t e) -> p t m e", t=4, e=2),
+                w2_dealt[:, g, :].bitcast(U16).rearrange("p (t m) -> p t m", t=4),
+                w2_raw[:, H * g : H * (g + 1)].bitcast(U16).rearrange("p (m t) -> p t m", t=4),
             )
 
         def deal_scales(g):
@@ -156,13 +160,12 @@ def tile_list_crowd_steering_features_kernel(
             return slice(cols.start // 16, cols.stop // 16)
 
         v2_scales = gather("v2_scales", tab2_plane, list2, U8)
-        deal_words(0)
-        deal_scales(0)
+        for g in range(2):
+            deal_words(g)
         v2_words = held("v2_words", [P, S], U32)
-        for cols in halves:
+        for g, cols in enumerate(halves):
             nc.vector.tensor_copy(v2_words[:, cols], tab2[:].bitcast(U32).indirect(list2[:, entries(cols)]))
-        deal_words(1)
-        deal_scales(1)
+            deal_scales(g)
 
         h2, h1, pages = {}, {}, {}
 
@@ -183,14 +186,14 @@ def tile_list_crowd_steering_features_kernel(
             nc.scalar.activation(h, h, ACT.Sin, bias=half_pi[:], scale=-1.0)
 
         def runners(first, count):
-            h = held(f"h2_{first}", [P, count, S], F32, tag="h", bufs=5)
+            h = held(f"h2_{first}", [P, count, S], F32, tag=f"h{first}")
             for n in range(count):
                 angle(first + n, h[:, n, :], slice(0, S), bank(first + n, f"angle{first + n}"))
                 h2[first + n] = h[:, n, :]
             cosine(h[:])
 
         def walkers(first, w1_q):
-            h = held(f"h1_{first}", [P, 2, S], F32, tag="h", bufs=5)
+            h = held(f"h1_{first}", [P, 2, S], F32, tag=f"h{(0, 2, 3, 5)[first // 2]}")
             codes, scales = w1_q
             for n in range(2):
                 half, t = divmod(first + n, 4)
@@ -209,25 +212,29 @@ def tile_list_crowd_steering_features_kernel(
                 nc.scalar.activation(h[:, n, :], acc[:], ACT.Square, bias=centre[:, half, t : t + 1], scale=-1.0)
                 h1[first + n] = h[:, n, :]
             nc.scalar.activation(h[:], h[:], ACT.Exp, scale=-1.0)
-            for n in range(2):
+            for n in range(2 if first < 6 else 0):
                 nc.gpsimd.tensor_tensor(h[:, n, :], h[:, n, :], gains1[(first + n) % 4], MULT)
 
-        def weigh(name, h, gains):
-            weighed = held(name, [P, S], F32, tag="weighed", bufs=3)
-            nc.gpsimd.tensor_tensor(weighed[:], h, gains, MULT)
-            return weighed[:]
+        def ring(name, i):
+            return placed(name, [P, S], F32, RING + RING_SLOT[i % 3])
+
+        def weigh(weighed, h, gains):
+            nc.gpsimd.tensor_tensor(weighed, h, gains, MULT)
+            return weighed
 
         def place(i, lst, weighed):
             nc.vector.tensor_copy(pages[i][:].indirect(lst[:]), weighed)
 
         def new_page(i):
-            if 3 <= i <= 6:
-                pages[i] = shared.tile([P, T2], F32, name=f"page{i}", offset=4096 * (i - 3), align_bytes=64)
+            if 3 <= i <= 5:
+                pages[i] = placed(f"page{i}", [P, T2], F32, ROUNDED + 4096 * (i - 3))
+            elif i == 7:
+                pages[i] = staged("page7", [P, T2], F32, 3)
             else:
-                pages[i] = held(f"page{i}", [P, T2], F32, tag={2: "big2", 7: "stage3"}.get(i))
+                pages[i] = held(f"page{i}", [P, T2], F32, tag={2: "big2", 6: "h3"}.get(i))
 
         def fused_features(i, pieces):
-            h = held(f"h2_{i}", [P, S], F32, tag="weighed", bufs=3)
+            h = ring(f"h2_{i}", i)
             for n, cols in enumerate(pieces):
                 angle(i, h[:], cols, bank(i + 7 * n, f"angle{i}_{n}"))
                 cosine(h[:, cols])
@@ -251,36 +258,38 @@ def tile_list_crowd_steering_features_kernel(
         place_fused(2, whole)
         w1_q = []
         for half in range(2):
-            rounded = shared.tile([P, 2, 2048], BF16, name=f"w1_bf{half}", offset=(2048, 12288)[half], align_bytes=64)
-            w1_q.append(quantise_weight(f"w1_{half}", [w1_raw[a, half] for a in range(2)], rounded))
+            rounded = placed(f"w1_bf{half}", [P, 2, 2048], BF16, ROUNDED + 8192 * half)
+            scales = held(f"w1_scales{half}", [P, 1024], U8)
+            w1_q.append(quantise_weight(f"w1_{half}", [w1_raw[a, half] for a in range(2)], rounded, scales))
             if half == 0:
                 runners(5, 2)
                 runners(7, 1)
-        weighed = {i: weigh(f"weighed{i}", h2[i], gains2[i % 4]) for i in range(3, PAGES)}
+        weighed = {i: weigh(ring(f"weighed{i}", i)[:], h2[i], gains2[i % 4]) for i in range(3, PAGES)}
         for first in range(0, PAGES, 2):
             walkers(first, w1_q[first // 4])
 
         w3_raw = {}
         for a in range(2):
             for g in range(2):
-                w3_raw[a, g] = load_weight("w3", w3, a, g, f"stage{2 * a + g}")
+                w3_raw[a, g] = load_weight("w3", w3, a, g, 2 * a + g)
             styles += [load_style(i) for i in (2 + 2 * a, 3 + 2 * a)]
         styles += [load_style(i) for i in (6, 7)]
         w3_q = [
-            quantise_weight("w3_0", [w3_raw[0, g] for g in range(2)], held("w3_bf0", [P, 2, 2048], BF16, tag="big1")),
             quantise_weight(
-                "w3_1", [w3_raw[1, g] for g in range(2)],
-                held("w3_bf1", [P, 2, 2048], BF16, tag="round2"),
-            ),
+                f"w3_{a}", [w3_raw[a, g] for g in range(2)],
+                held(f"w3_bf{a}", [P, 2, 2048], BF16, tag=("big1", None)[a]),
+                placed(f"w3_scales{a}", [P, 1024], U8, RING + 64 + 1024 * a),
+            )
+            for a in range(2)
         ]
 
         z_rows = [held(f"z_rows{g}", [P, CHUNKS, 4, CHUNK], BF16, tag=("big0", None)[g]) for g in range(2)]
         z_woven = [
-            held("z_woven0", [P, CHUNKS, CHUNK, 4], BF16, tag="stage3"),
+            staged("z_woven0", [P, CHUNKS, CHUNK, 4], BF16, 3),
             held("z_woven1", [P, CHUNKS, CHUNK, 4], BF16, tag="big1"),
         ]
         z_codes = [held(f"z_codes{g}", [P, T2], U32) for g in range(2)]
-        z_scales = [held(f"z_scales{g}", [P, T2], U8) for g in range(2)]
+        z_scales = [placed("z_scales0", [P, T2], U8, RING - 960), held("z_scales1", [P, T2], U8)]
 
         def apply_style(engine, i, chunks):
             g, t = divmod(i, 4)
@@ -323,7 +332,7 @@ def tile_list_crowd_steering_features_kernel(
 
         order = [(c, g) for c in (0, 1) for g in range(2)] + [(c, g) for g in range(2) for c in (2, 3)]
         early = {}
-        steps = ["r3", "r4", "r5", "w0", "w1", "w2", "w3", "r6", "w4", "w5", "w6", "r7", "w7"]
+        steps = ["r3", "r4", "r5", "w0", "w1", "w2", "w3", "w4", "w5", "r6", "r7", "w6", "w7"]
         for n, step in enumerate(steps):
             i = int(step[1])
             if n > 0 and steps[n - 1][0] == "w":
@@ -333,11 +342,15 @@ def tile_list_crowd_steering_features_kernel(
                 if done == 3:
                     for c in range(CHUNKS):
                         weave(nc.scalar.copy, 0, c)
-                    quantise_z(0, 0, CHUNKS)
-                    for k, (c, g_out) in enumerate(order[:4]):
-                        for pair in range(2):
-                            early[c, g_out, pair] = bank(2 * k + pair, f"y{c}{g_out}{pair}")
-                            project(early[c, g_out, pair], c, g_out, pair, 0)
+            if step == "r7":
+                quantise_z(0, 0, CHUNKS)
+                for k, (c, g_out) in enumerate(order[:4]):
+                    for pair in range(2):
+                        early[c, g_out, pair] = bank(2 * k + pair, f"y{c}{g_out}{pair}")
+                        project(early[c, g_out, pair], c, g_out, pair, 0)
+                late = staged("weighed_late", [P, 2, S], F32, 3, 4096)
+                for m in range(2):
+                    h1[6 + m] = weigh(late[:, m, :], h1[6 + m], gains1[2 + m])
             if step[0] == "r":
                 new_page(i)
                 place(i, list4, weighed[i])
@@ -370,7 +383,7 @@ def tile_list_crowd_steering_features_kernel(
                 y_codes[g_out][:, agents].bitcast(I32),
             )
 
-        y = {(half, g): held(f"y{half}{g}", [P, 4, 512], F32, tag=f"stage{2 * half + g}") for half in range(2) for g in range(2)}
+        y = {(half, g): staged(f"y{half}{g}", [P, 4, 512], F32, 2 * half + g) for half in range(2) for g in range(2)}
         for step, (c, g_out) in enumerate(order):
             half = c // 2
             both = slice(512 * half, 512 * (half + 1))

@@ -22,7 +22,8 @@ CHUNK = 256
 CHUNKS = T2 // CHUNK
 PAGES = H // P
 ROUNDED = 0
-STAGE = ROUNDED + 2 * 8192
+TAB1 = ROUNDED + 2 * 8192
+STAGE = TAB1 + 8192
 RING = STAGE + 4 * 8192 + 960
 RING_SLOT = (0, 4096, 2048)
 
@@ -37,19 +38,19 @@ def tile_list_crowd_steering_features_kernel(
         first = ctx.enter_context(tc.tile_pool(name="first", bufs=1))
         psum = ctx.enter_context(tc.psum_pool(name="psum", bufs=1))
 
-        def zeroed_plane(name, cols):
+        def zeroed_plane(engine, name, cols):
             plane = first.tile([P, cols], U8, name=name, tag=name, align_bytes=64)
-            nc.vector.memset(plane[:].bitcast(I32), 0)
+            engine.memset(plane[:].bitcast(I32), 0)
             return plane
 
-        w2_plane = zeroed_plane("w2_plane", H)
+        w2_plane = zeroed_plane(nc.vector, "w2_plane", H)
         zero = first.tile([P, 1], F32, name="zero")
         nc.vector.memset(zero[:], 0.0)
         sin_zero = first.tile([P, 1], F32, name="sin_zero")
         nc.scalar.activation(sin_zero[:], zero[:], ACT.Sin)
         half_pi = first.tile([P, 1], F32, name="half_pi")
         nc.vector.tensor_scalar(half_pi[:], sin_zero[:], 1.0, math.pi / 2, op0=MULT, op1=ADD)
-        tab_plane = zeroed_plane("tab_plane", T)
+        tab_plane = zeroed_plane(nc.gpsimd, "tab_plane", T)
 
         keep = ctx.enter_context(tc.tile_pool(name="keep", bufs=1))
         shared = ctx.enter_context(tc.tile_pool(name="shared", bufs=1))
@@ -73,8 +74,7 @@ def tile_list_crowd_steering_features_kernel(
                     src[:, 4 * q : 4 * q + 4, :].bitcast(I32),
                 )
 
-        def load_words(name, src, tag):
-            words = held(name, [P, T], I32, tag=tag)
+        def load_words(words, src):
             nc.sync.dma_start(words[:], src.rearrange("p n i -> p (n i)").bitcast(I32))
             return words
 
@@ -124,14 +124,17 @@ def tile_list_crowd_steering_features_kernel(
         list2 = load_list("list2", offs2)
         w2_raw = held("w2_raw", [P, 2 * H], U8)
         nc.sync.dma_start(w2_raw[:].bitcast(I32), w2_words[0].bitcast(I32))
-        tab2 = load_words("tab2", tab2_words[0], "big0")
-        list4 = load_list("list4", offs4)
+        tab2 = load_words(held("tab2", [P, T], I32, tag="big0"), tab2_words[0])
+        list1 = load_list("list1", offs)
+        load_scale_rows(nc.gpsimd, tab_plane, tab_scales)
         load_scale_rows(nc.sync, w2_plane, w2_scales)
         gains2 = load_gains("gains2_first", wg2, 0, 1)
-        list1 = load_list("list1", offs)
+        list4 = load_list("list4", offs4)
         gains2 = gains2 + load_gains("gains2_rest", wg2, 1, 4)
-        load_scale_rows(nc.sync, tab_plane, tab_scales)
-        tab = [load_words(f"tab{a}", tab_words[a], f"big{1 + a}") for a in range(2)]
+        tab = [
+            load_words(held("tab0", [P, T], I32, tag="big1"), tab_words[0]),
+            load_words(placed("tab1", [P, T], I32, TAB1), tab_words[1]),
+        ]
         w1_raw = {(a, half): load_weight("w1", w1, a, half, 2 * half + a) for half in range(2) for a in range(2)}
         centre = held("centre", [P, 2, 4], F32)
         nc.sync.dma_start(centre[:], ctr.rearrange("(g p t) -> p g t", g=2, t=4))
@@ -166,6 +169,9 @@ def tile_list_crowd_steering_features_kernel(
         for g, cols in enumerate(halves):
             nc.vector.tensor_copy(v2_words[:, cols], tab2[:].bitcast(U32).indirect(list2[:, entries(cols)]))
             deal_scales(g)
+
+        v_scales = first.tile([P, S], U8, name="v_scales", tag="w2_plane", align_bytes=64)
+        nc.vector.tensor_copy(v_scales[:], tab_plane[:].indirect(list1[:]))
 
         h2, h1, pages = {}, {}, {}
 
@@ -226,12 +232,14 @@ def tile_list_crowd_steering_features_kernel(
             nc.vector.tensor_copy(pages[i][:].indirect(lst[:]), weighed)
 
         def new_page(i):
-            if 3 <= i <= 5:
-                pages[i] = placed(f"page{i}", [P, T2], F32, ROUNDED + 4096 * (i - 3))
+            if i in (2, 3):
+                pages[i] = placed(f"page{i}", [P, T2], F32, TAB1 + 4096 * (i - 2))
+            elif i in (4, 5):
+                pages[i] = placed(f"page{i}", [P, T2], F32, ROUNDED + 8192 * (i - 4))
             elif i == 7:
                 pages[i] = staged("page7", [P, T2], F32, 3)
             else:
-                pages[i] = held(f"page{i}", [P, T2], F32, tag={2: "big2", 6: "h3"}.get(i))
+                pages[i] = held(f"page{i}", [P, T2], F32, tag={6: "h3"}.get(i))
 
         def fused_features(i, pieces):
             h = ring(f"h2_{i}", i)
@@ -253,7 +261,6 @@ def tile_list_crowd_steering_features_kernel(
         for i in range(2):
             place_fused(i, halves if i == 0 else whole)
         runners(3, 2)
-        v_scales = gather("v_scales", tab_plane, list1, U8)
         v_words = [gather(f"v_words{a}", tab[a], list1, U32) for a in range(2)]
         place_fused(2, whole)
         w1_q = []

@@ -104,12 +104,14 @@ def tile_list_crowd_steering_features_kernel(
             nc.vector.tensor_copy(picked[:], window[:].bitcast(dtype).indirect(lst[:]))
             return picked
 
-        def quantise_weight(name, raws, rounded, scales):
+        def round_weight(raws, rounded):
             for n, raw in enumerate(raws):
                 nc.scalar.copy(
                     rounded[:, n, :].rearrange("p (t m u e) -> p m u t e", t=4, u=2, e=2),
                     raw[:].rearrange("p (u e) (m t) -> p m u t e", e=2, t=4),
                 )
+
+        def quantise_weight(name, rounded, scales):
             codes = held(f"{name}_codes", [P, 1024], U32)
             nc.vector.quantize_mx(codes[:].bitcast(FP8X4), scales[:], rounded[:].rearrange("p a c -> p (a c)"))
             return codes, scales
@@ -267,7 +269,8 @@ def tile_list_crowd_steering_features_kernel(
         for half in range(2):
             rounded = placed(f"w1_bf{half}", [P, 2, 2048], BF16, ROUNDED + 8192 * half)
             scales = held(f"w1_scales{half}", [P, 1024], U8)
-            w1_q.append(quantise_weight(f"w1_{half}", [w1_raw[a, half] for a in range(2)], rounded, scales))
+            round_weight([w1_raw[a, half] for a in range(2)], rounded)
+            w1_q.append(quantise_weight(f"w1_{half}", rounded, scales))
             if half == 0:
                 runners(5, 2)
                 runners(7, 1)
@@ -275,20 +278,14 @@ def tile_list_crowd_steering_features_kernel(
         for first in range(0, PAGES, 2):
             walkers(first, w1_q[first // 4])
 
-        w3_raw = {}
-        for a in range(2):
-            for g in range(2):
-                w3_raw[a, g] = load_weight("w3", w3, a, g, 2 * a + g)
-            styles += [load_style(i) for i in (2 + 2 * a, 3 + 2 * a)]
+        w3_bf = []
+        for g in range(2):
+            raws = [load_weight("w3", w3, a, g, 2 * g + a) for a in range(2)]
+            styles += [load_style(i) for i in (2 + 2 * g, 3 + 2 * g)]
+            w3_bf.append(held(f"w3_bf{g}", [P, 2, 2048], BF16, tag=("big1", None)[g]))
+            round_weight(raws, w3_bf[g])
         styles += [load_style(i) for i in (6, 7)]
-        w3_q = [
-            quantise_weight(
-                f"w3_{a}", [w3_raw[a, g] for g in range(2)],
-                held(f"w3_bf{a}", [P, 2, 2048], BF16, tag=("big1", None)[a]),
-                placed(f"w3_scales{a}", [P, 1024], U8, RING + 64 + 1024 * a),
-            )
-            for a in range(2)
-        ]
+        w3_q = [quantise_weight("w3_0", w3_bf[0], placed("w3_scales0", [P, 1024], U8, RING + 64))]
 
         z_rows = [held(f"z_rows{g}", [P, CHUNKS, 4, CHUNK], BF16, tag=("big0", None)[g]) for g in range(2)]
         z_woven = [
@@ -307,10 +304,10 @@ def tile_list_crowd_steering_features_kernel(
                 MULT,
             )
 
-        def weave(copy, g, c):
+        def weave(copy, g, c0, c1):
             copy(
-                z_woven[g][:, c].rearrange("p (n i) t -> p n t i", i=4),
-                z_rows[g][:, c].rearrange("p t (n i) -> p n t i", i=4),
+                z_woven[g][:, c0:c1].rearrange("p c (n i) t -> p c n t i", i=4),
+                z_rows[g][:, c0:c1].rearrange("p c t (n i) -> p c n t i", i=4),
             )
 
         def quantise_z(g, c0, c1):
@@ -321,23 +318,24 @@ def tile_list_crowd_steering_features_kernel(
                 z_woven[g][:, c0:c1].rearrange("p c n t -> p (c n t)"),
             )
 
-        def project(acc, c, g_out, pair, a):
-            codes, scales = w3_q[a]
-            for e in range(2):
-                t = 2 * pair + e
-                cols = slice(512 * g_out + P * t, 512 * g_out + P * (t + 1))
-                agents = slice(CHUNK * c, CHUNK * (c + 1))
+        def project(acc, agents, g_out, slots, a):
+            codes, scales = w3_q[g_out]
+            width = agents.stop - agents.start
+            for e, t in enumerate(slots):
+                cols = slice(512 * a + P * t, 512 * a + P * (t + 1))
                 nc.tensor.matmul_mx(
-                    acc[:, CHUNK * e : CHUNK * (e + 1)],
+                    acc[:, width * e : width * (e + 1)],
                     lhsT=codes[:, cols].bitcast(FP8X4),
                     lhsT_scale=scales[:, cols],
                     rhs=z_codes[a][:, agents].bitcast(FP8X4),
                     rhs_scale=z_scales[a][:, agents],
                     start=(a == 0 and e == 0),
-                    stop=(a == 1 and e == 1),
+                    stop=(a == 1 and e == len(slots) - 1),
                 )
 
-        order = [(c, g) for c in (0, 1) for g in range(2)] + [(c, g) for g in range(2) for c in (2, 3)]
+        def chunk(c):
+            return slice(CHUNK * c, CHUNK * (c + 1))
+
         early = {}
         steps = ["r3", "r4", "r5", "w0", "w1", "w2", "w3", "w4", "w5", "r6", "r7", "w6", "w7"]
         for n, step in enumerate(steps):
@@ -348,13 +346,13 @@ def tile_list_crowd_steering_features_kernel(
                 apply_style(nc.gpsimd, done, slice(2, 4))
                 if done == 3:
                     for c in range(CHUNKS):
-                        weave(nc.scalar.copy, 0, c)
+                        weave(nc.scalar.copy, 0, c, c + 1)
             if step == "r7":
                 quantise_z(0, 0, CHUNKS)
-                for k, (c, g_out) in enumerate(order[:4]):
+                for c in range(CHUNKS):
                     for pair in range(2):
-                        early[c, g_out, pair] = bank(2 * k + pair, f"y{c}{g_out}{pair}")
-                        project(early[c, g_out, pair], c, g_out, pair, 0)
+                        early[c, pair] = bank(2 * c + pair, f"y_first{c}{pair}")
+                        project(early[c, pair], chunk(c), 0, (2 * pair, 2 * pair + 1), 0)
                 late = staged("weighed_late", [P, 2, S], F32, 3, 4096)
                 for m in range(2):
                     h1[6 + m] = weigh(late[:, m, :], h1[6 + m], gains1[2 + m])
@@ -366,8 +364,9 @@ def tile_list_crowd_steering_features_kernel(
 
         for c in range(CHUNKS):
             apply_style(nc.vector, 7, slice(c, c + 1))
-            weave(nc.scalar.copy if c == 1 else nc.vector.tensor_copy, 1, c)
+            weave(nc.scalar.copy if c == 1 else nc.vector.tensor_copy, 1, c, c + 1)
             quantise_z(1, c, c + 1)
+        w3_q.append(quantise_weight("w3_1", w3_bf[1], staged("w3_scales1", [P, 1024], U8, 3, 4096 + 2048)))
 
         y_codes = [held(f"y_codes{g}", [P, T2], U32) for g in range(2)]
         y_scales = held("y_scales", [P, 2, T2], U8)
@@ -390,31 +389,40 @@ def tile_list_crowd_steering_features_kernel(
                 y_codes[g_out][:, agents].bitcast(I32),
             )
 
-        y = {(half, g): staged(f"y{half}{g}", [P, 4, 512], F32, 2 * half + g) for half in range(2) for g in range(2)}
-        for step, (c, g_out) in enumerate(order):
-            half = c // 2
-            both = slice(512 * half, 512 * (half + 1))
-            agents = slice(CHUNK * c, CHUNK * (c + 1))
-            local = slice(CHUNK * (c % 2), CHUNK * (c % 2 + 1))
-            rows = y[half, g_out]
+        y = {
+            (0, 0): staged("y00", [P, 4, 512], F32, 0),
+            (0, 1): staged("y01", [P, 4, 512], F32, 1),
+            (1, 0): staged("y10", [P, 4, 512], F32, 2),
+            (1, 1): held("y11", [P, 4, 512], F32, tag="big0"),
+        }
+        for c in range(CHUNKS):
+            half, local = c // 2, chunk(c % 2)
+            rows = y[0, half]
             for pair in range(2):
                 slots = slice(2 * pair, 2 * pair + 2)
+                project(early[c, pair], chunk(c), 0, (2 * pair, 2 * pair + 1), 1)
+                nc.scalar.copy(rows[:, slots, local], early[c, pair][:].rearrange("p (t n) -> p t n", t=2))
                 if half == 0:
-                    acc = early[c, g_out, pair]
-                else:
-                    acc = bank(2 * step + pair, f"y{c}{g_out}{pair}")
-                    project(acc, c, g_out, pair, 0)
-                project(acc, c, g_out, pair, 1)
-                nc.scalar.copy(rows[:, slots, local], acc[:].rearrange("p (t n) -> p t n", t=2))
-                if half == 0:
-                    nc.sync.dma_start(y_rows[g_out][:, slots, agents], rows[:, slots, local])
-                elif c % 2 == 1:
-                    nc.sync.dma_start(y_rows[g_out][:, slots, both], rows[:, slots, :])
-            last = (half, g_out) == (1, 1)
-            if last:
-                emit_planes(nc.scalar.copy if c == 3 else nc.vector.tensor_copy, rows[:, :, local], g_out, agents, f"page{step % 2}")
-            elif c % 2 == 1:
-                emit_planes(nc.vector.tensor_copy, rows[:], g_out, both, f"page{step % 2}")
+                    nc.sync.dma_start(y_rows[0][:, slots, chunk(c)], rows[:, slots, local])
+            if half == 1:
+                nc.sync.dma_start(y_rows[0][:, :, chunk(c)], rows[:, :, local])
+            if c % 2 == 1:
+                emit_planes(nc.vector.tensor_copy, rows[:], 0, slice(512 * half, 512 * (half + 1)), f"page{half}")
+        for half in range(2):
+            rows = y[1, half]
+            agents = slice(512 * half, 512 * (half + 1))
+            for t in range(4):
+                acc = bank(4 * half + t, f"y_second{half}{t}")
+                for a in range(2):
+                    project(acc, agents, 1, (t,), a)
+                nc.scalar.copy(rows[:, t, :], acc[:])
+                if t % 2 == 1:
+                    nc.sync.dma_start(y_rows[1][:, t - 1 : t + 1, agents], rows[:, t - 1 : t + 1, :])
+            if half == 0:
+                emit_planes(nc.vector.tensor_copy, rows[:], 1, agents, "page0")
+            else:
+                emit_planes(nc.vector.tensor_copy, rows[:, :, chunk(0)], 1, chunk(2), "page1")
+                emit_planes(nc.scalar.copy, rows[:, :, chunk(1)], 1, chunk(3), "h0")
         for q in range(4):
             nc.scalar.dma_start(
                 out_2[:, 4 * q : 4 * q + 4, :].rearrange("g r n -> r g n").bitcast(I32),

@@ -25,7 +25,7 @@ ROUNDED = 0
 TAB1 = ROUNDED + 2 * 8192
 STAGE = TAB1 + 8192
 RING = STAGE + 4 * 8192 + 960
-RING_SLOT = (0, 4096, 2048)
+RING_SLOT = (4096, 0, 2048)
 
 
 def tile_list_crowd_steering_features_kernel(
@@ -219,8 +219,9 @@ def tile_list_crowd_steering_features_kernel(
                     )
                 nc.scalar.activation(h[:, n, :], acc[:], ACT.Square, bias=centre[:, half, t : t + 1], scale=-1.0)
                 h1[first + n] = h[:, n, :]
-            nc.scalar.activation(h[:], h[:], ACT.Exp, scale=-1.0)
-            for n in range(2 if first < 6 else 0):
+            count = 2 if first < 6 else 1
+            nc.scalar.activation(h[:, :count, :], h[:, :count, :], ACT.Exp, scale=-1.0)
+            for n in range(count):
                 nc.gpsimd.tensor_tensor(h[:, n, :], h[:, n, :], gains1[(first + n) % 4], MULT)
 
         def ring(name, i):
@@ -236,12 +237,12 @@ def tile_list_crowd_steering_features_kernel(
         def new_page(i):
             if i in (2, 3):
                 pages[i] = placed(f"page{i}", [P, T2], F32, TAB1 + 4096 * (i - 2))
-            elif i in (4, 5):
-                pages[i] = placed(f"page{i}", [P, T2], F32, ROUNDED + 8192 * (i - 4))
+            elif i in (4, 5, 6):
+                pages[i] = placed(f"page{i}", [P, T2], F32, ROUNDED + (0, 8192, 12288)[i - 4])
             elif i == 7:
-                pages[i] = staged("page7", [P, T2], F32, 3)
+                pages[i] = held("page7", [P, T2], F32, tag="big0")
             else:
-                pages[i] = held(f"page{i}", [P, T2], F32, tag={6: "h3"}.get(i))
+                pages[i] = held(f"page{i}", [P, T2], F32)
 
         def fused_features(i, pieces):
             h = ring(f"h2_{i}", i)
@@ -290,32 +291,31 @@ def tile_list_crowd_steering_features_kernel(
         z_rows = [held(f"z_rows{g}", [P, CHUNKS, 4, CHUNK], BF16, tag=("big0", None)[g]) for g in range(2)]
         z_woven = [
             staged("z_woven0", [P, CHUNKS, CHUNK, 4], BF16, 3),
-            held("z_woven1", [P, CHUNKS, CHUNK, 4], BF16, tag="big1"),
+            staged("z_woven1", [P, CHUNKS, CHUNK, 4], BF16, 2),
         ]
         z_codes = [held(f"z_codes{g}", [P, T2], U32) for g in range(2)]
         z_scales = [placed("z_scales0", [P, T2], U8, RING - 960), held("z_scales1", [P, T2], U8)]
 
-        def apply_style(engine, i, chunks):
+        def apply_style(engine, i, chunks, cols=slice(0, CHUNK)):
             g, t = divmod(i, 4)
             engine.tensor_tensor(
-                z_rows[g][:, chunks, t, :],
-                pages[i][:].rearrange("p (c n) -> p c n", n=CHUNK)[:, chunks, :],
-                styles[i][:].rearrange("p (c n) -> p c n", n=CHUNK)[:, chunks, :],
+                z_rows[g][:, chunks, t, cols],
+                pages[i][:].rearrange("p (c n) -> p c n", n=CHUNK)[:, chunks, cols],
+                styles[i][:].rearrange("p (c n) -> p c n", n=CHUNK)[:, chunks, cols],
                 MULT,
             )
 
-        def weave(copy, g, c0, c1):
+        def weave(copy, g, chunks, slots, cols=slice(0, CHUNK)):
             copy(
-                z_woven[g][:, c0:c1].rearrange("p c (n i) t -> p c n t i", i=4),
-                z_rows[g][:, c0:c1].rearrange("p c t (n i) -> p c n t i", i=4),
+                z_woven[g][:, chunks, cols, slots].rearrange("p c (n i) t -> p c n t i", i=4),
+                z_rows[g][:, chunks, slots, cols].rearrange("p c t (n i) -> p c n t i", i=4),
             )
 
-        def quantise_z(g, c0, c1):
-            cols = slice(CHUNK * c0, CHUNK * c1)
+        def quantise_z(g, agents):
             nc.vector.quantize_mx(
-                z_codes[g][:, cols].bitcast(FP8X4),
-                z_scales[g][:, cols],
-                z_woven[g][:, c0:c1].rearrange("p c n t -> p (c n t)"),
+                z_codes[g][:, agents].bitcast(FP8X4),
+                z_scales[g][:, agents],
+                z_woven[g][:].rearrange("p c n t -> p (c n t)")[:, 4 * agents.start : 4 * agents.stop],
             )
 
         def project(acc, agents, g_out, slots, a):
@@ -336,8 +336,13 @@ def tile_list_crowd_steering_features_kernel(
         def chunk(c):
             return slice(CHUNK * c, CHUNK * (c + 1))
 
-        early = {}
-        steps = ["r3", "r4", "r5", "w0", "w1", "w2", "w3", "w4", "w5", "r6", "r7", "w6", "w7"]
+        pieces = [slice(0, 128), slice(128, 256)] + [chunk(c) for c in range(1, CHUNKS)]
+        first_banks = [
+            (agents, tuple(range(t, t + 512 // (agents.stop - agents.start))))
+            for agents in pieces
+            for t in range(0, 4, 512 // (agents.stop - agents.start))
+        ]
+        steps = ["r3", "r4", "r5", "r6", "w0", "w1", "w2", "w3", "w4", "w5", "w6", "r7"]
         for n, step in enumerate(steps):
             i = int(step[1])
             if n > 0 and steps[n - 1][0] == "w":
@@ -346,39 +351,43 @@ def tile_list_crowd_steering_features_kernel(
                 apply_style(nc.gpsimd, done, slice(2, 4))
                 if done == 3:
                     for c in range(CHUNKS):
-                        weave(nc.scalar.copy, 0, c, c + 1)
-            if step == "r7":
-                quantise_z(0, 0, CHUNKS)
-                for c in range(CHUNKS):
-                    for pair in range(2):
-                        early[c, pair] = bank(2 * c + pair, f"y_first{c}{pair}")
-                        project(early[c, pair], chunk(c), 0, (2 * pair, 2 * pair + 1), 0)
-                late = staged("weighed_late", [P, 2, S], F32, 3, 4096)
-                for m in range(2):
-                    h1[6 + m] = weigh(late[:, m, :], h1[6 + m], gains1[2 + m])
+                        weave(nc.scalar.copy, 0, slice(c, c + 1), slice(0, 4))
+                if done == 5:
+                    weave(nc.scalar.copy, 1, slice(0, CHUNKS), slice(0, 2))
             if step[0] == "r":
                 new_page(i)
                 place(i, list4, weighed[i])
             else:
                 place(i, list3, h1[i])
 
-        for c in range(CHUNKS):
-            apply_style(nc.vector, 7, slice(c, c + 1))
-            weave(nc.scalar.copy if c == 1 else nc.vector.tensor_copy, 1, c, c + 1)
-            quantise_z(1, c, c + 1)
-        w3_q.append(quantise_weight("w3_1", w3_bf[1], staged("w3_scales1", [P, 1024], U8, 3, 4096 + 2048)))
+        quantise_z(0, slice(0, T2))
+        early = [bank(n, f"y_first{n}") for n in range(8)]
+        for acc, (agents, slots) in zip(early, first_banks):
+            project(acc, agents, 0, slots, 0)
+        bump = held("bump7", [P, S], F32, tag="big1")
+        nc.scalar.activation(bump[:], h1[7], ACT.Exp, scale=-1.0)
+        nc.vector.tensor_tensor(pages[7][:].indirect(list3[:]), bump[:], gains1[3], MULT)
+
+        for agents in pieces:
+            c, start = divmod(agents.start, CHUNK)
+            cols = slice(start, start + agents.stop - agents.start)
+            apply_style(nc.vector, 7, slice(c, c + 1), cols)
+            weave(nc.vector.tensor_copy, 1, slice(c, c + 1), slice(2, 4), cols)
+            quantise_z(1, agents)
+        w3_q.append(quantise_weight("w3_1", w3_bf[1], held("w3_scales1", [P, 1024], U8, tag="big1")))
 
         y_codes = [held(f"y_codes{g}", [P, T2], U32) for g in range(2)]
         y_scales = held("y_scales", [P, 2, T2], U8)
         y_rows = out_0.rearrange("(g p t) n -> g p t n", g=2, t=4)
 
-        def emit_planes(copy, values, g_out, agents, tag):
+        def emit_planes(shares, values, g_out, agents, tag):
             width = agents.stop - agents.start
             woven = held(f"y_woven{g_out}_{agents.start}", [P, width, 4], BF16, tag=tag)
-            copy(
-                woven[:].rearrange("p (n i) t -> p n t i", i=4),
-                values.rearrange("p t (n i) -> p n t i", i=4),
-            )
+            for share, copy in zip(shares, (nc.vector.tensor_copy, nc.scalar.copy)):
+                copy(
+                    woven[:, share, :].rearrange("p (n i) t -> p n t i", i=4),
+                    values[:, :, share].rearrange("p t (n i) -> p n t i", i=4),
+                )
             nc.vector.quantize_mx(
                 y_codes[g_out][:, agents].bitcast(FP8X4),
                 y_scales[:, g_out, agents],
@@ -395,19 +404,16 @@ def tile_list_crowd_steering_features_kernel(
             (1, 0): staged("y10", [P, 4, 512], F32, 2),
             (1, 1): held("y11", [P, 4, 512], F32, tag="big0"),
         }
-        for c in range(CHUNKS):
-            half, local = c // 2, chunk(c % 2)
+        for acc, (agents, slots) in zip(early, first_banks):
+            half, start = divmod(agents.start, 512)
+            local = slice(start, start + agents.stop - agents.start)
             rows = y[0, half]
-            for pair in range(2):
-                slots = slice(2 * pair, 2 * pair + 2)
-                project(early[c, pair], chunk(c), 0, (2 * pair, 2 * pair + 1), 1)
-                nc.scalar.copy(rows[:, slots, local], early[c, pair][:].rearrange("p (t n) -> p t n", t=2))
-                if half == 0:
-                    nc.sync.dma_start(y_rows[0][:, slots, chunk(c)], rows[:, slots, local])
-            if half == 1:
-                nc.sync.dma_start(y_rows[0][:, :, chunk(c)], rows[:, :, local])
-            if c % 2 == 1:
-                emit_planes(nc.vector.tensor_copy, rows[:], 0, slice(512 * half, 512 * (half + 1)), f"page{half}")
+            project(acc, agents, 0, slots, 1)
+            nc.scalar.copy(rows[:, slots[0] : slots[-1] + 1, local], acc[:].rearrange("p (t n) -> p t n", t=len(slots)))
+            if slots[-1] == 3:
+                nc.sync.dma_start(y_rows[0][:, :, agents], rows[:, :, local])
+                if agents.stop % 512 == 0:
+                    emit_planes([slice(0, 512)], rows[:], 0, slice(512 * half, 512 * (half + 1)), f"page{half}")
         for half in range(2):
             rows = y[1, half]
             agents = slice(512 * half, 512 * (half + 1))
@@ -418,13 +424,10 @@ def tile_list_crowd_steering_features_kernel(
                 nc.scalar.copy(rows[:, t, :], acc[:])
                 if t % 2 == 1:
                     nc.sync.dma_start(y_rows[1][:, t - 1 : t + 1, agents], rows[:, t - 1 : t + 1, :])
-            if half == 0:
-                emit_planes(nc.vector.tensor_copy, rows[:], 1, agents, "page0")
-            else:
-                emit_planes(nc.vector.tensor_copy, rows[:, :, chunk(0)], 1, chunk(2), "page1")
-                emit_planes(nc.scalar.copy, rows[:, :, chunk(1)], 1, chunk(3), "h0")
+            shares = [slice(0, 512)] if half == 0 else [slice(0, 336), slice(336, 512)]
+            emit_planes(shares, rows[:], 1, agents, f"page{half}")
         for q in range(4):
-            nc.scalar.dma_start(
+            (nc.scalar, nc.sync)[q % 2].dma_start(
                 out_2[:, 4 * q : 4 * q + 4, :].rearrange("g r n -> r g n").bitcast(I32),
                 y_scales[32 * q : 32 * q + 4].bitcast(I32),
             )

@@ -113,7 +113,7 @@ def tile_list_crowd_steering_features_kernel(
 
         def quantise_weight(name, rounded, scales):
             codes = held(f"{name}_codes", [P, 1024], U32)
-            nc.vector.quantize_mx(codes[:].bitcast(FP8X4), scales[:], rounded[:].rearrange("p a c -> p (a c)"))
+            nc.vector.quantize_mx(codes[:].bitcast(FP8X4), scales, rounded[:].rearrange("p a c -> p (a c)"))
             return codes, scales
 
         def bank(idx, name):
@@ -124,10 +124,10 @@ def tile_list_crowd_steering_features_kernel(
             rows = tab2_scales[0, 4 * q : 4 * q + 4, :].bitcast(I32)
             nc.sync.dma_start(tab2_plane[32 * q : 32 * q + 32, :].bitcast(I32), rows.partition_broadcast(8))
         list2 = load_list("list2", offs2)
+        list1 = load_list("list1", offs)
         w2_raw = held("w2_raw", [P, 2 * H], U8)
         nc.sync.dma_start(w2_raw[:].bitcast(I32), w2_words[0].bitcast(I32))
         tab2 = load_words(held("tab2", [P, T], I32, tag="big0"), tab2_words[0])
-        list1 = load_list("list1", offs)
         load_scale_rows(nc.gpsimd, tab_plane, tab_scales)
         load_scale_rows(nc.sync, w2_plane, w2_scales)
         gains2 = load_gains("gains2_first", wg2, 0, 1)
@@ -269,7 +269,7 @@ def tile_list_crowd_steering_features_kernel(
         w1_q = []
         for half in range(2):
             rounded = placed(f"w1_bf{half}", [P, 2, 2048], BF16, ROUNDED + 8192 * half)
-            scales = held(f"w1_scales{half}", [P, 1024], U8)
+            scales = held(f"w1_scales{half}", [P, 1024], U8)[:]
             round_weight([w1_raw[a, half] for a in range(2)], rounded)
             w1_q.append(quantise_weight(f"w1_{half}", rounded, scales))
             if half == 0:
@@ -286,20 +286,35 @@ def tile_list_crowd_steering_features_kernel(
             w3_bf.append(held(f"w3_bf{g}", [P, 2, 2048], BF16, tag=("big1", None)[g]))
             round_weight(raws, w3_bf[g])
         styles += [load_style(i) for i in (6, 7)]
-        w3_q = [quantise_weight("w3_0", w3_bf[0], placed("w3_scales0", [P, 1024], U8, RING + 64))]
+        w3_q = [quantise_weight("w3_0", w3_bf[0], placed("w3_scales0", [P, 1024], U8, RING + 64)[:])]
 
-        z_rows = [held(f"z_rows{g}", [P, CHUNKS, 4, CHUNK], BF16, tag=("big0", None)[g]) for g in range(2)]
+        first_rows = held("z_rows0", [P, CHUNKS, 4, CHUNK], BF16, tag="big0")
+        pair_rows = [held(f"z_rows1_{pair}", [P, CHUNKS, 2, CHUNK], BF16) for pair in range(2)]
+
+        def z_rows(g, chunks, slots, cols):
+            if g == 0:
+                return first_rows[:, chunks, slots, cols]
+            return pair_rows[slots.start // 2][:, chunks, slots.start % 2 : slots.start % 2 + slots.stop - slots.start, cols]
+
         z_woven = [
             staged("z_woven0", [P, CHUNKS, CHUNK, 4], BF16, 3),
             staged("z_woven1", [P, CHUNKS, CHUNK, 4], BF16, 2),
         ]
         z_codes = [held(f"z_codes{g}", [P, T2], U32) for g in range(2)]
-        z_scales = [placed("z_scales0", [P, T2], U8, RING - 960), held("z_scales1", [P, T2], U8)]
+        z_scales = {
+            (0, 0): placed("z_scales00", [P, 512], U8, RING - 448)[:],
+            (1, 0): held("z_scales10", [P, 512], U8)[:],
+            (1, 1): held("z_scales11", [P, 512], U8)[:],
+        }
+
+        def z_plane(g, agents):
+            half, start = divmod(agents.start, 512)
+            return z_scales[g, half][:, start : start + agents.stop - agents.start]
 
         def apply_style(engine, i, chunks, cols=slice(0, CHUNK)):
             g, t = divmod(i, 4)
             engine.tensor_tensor(
-                z_rows[g][:, chunks, t, cols],
+                z_rows(g, chunks, slice(t, t + 1), cols).rearrange("p c t n -> p c (t n)"),
                 pages[i][:].rearrange("p (c n) -> p c n", n=CHUNK)[:, chunks, cols],
                 styles[i][:].rearrange("p (c n) -> p c n", n=CHUNK)[:, chunks, cols],
                 MULT,
@@ -308,13 +323,13 @@ def tile_list_crowd_steering_features_kernel(
         def weave(copy, g, chunks, slots, cols=slice(0, CHUNK)):
             copy(
                 z_woven[g][:, chunks, cols, slots].rearrange("p c (n i) t -> p c n t i", i=4),
-                z_rows[g][:, chunks, slots, cols].rearrange("p c t (n i) -> p c n t i", i=4),
+                z_rows(g, chunks, slots, cols).rearrange("p c t (n i) -> p c n t i", i=4),
             )
 
         def quantise_z(g, agents):
             nc.vector.quantize_mx(
                 z_codes[g][:, agents].bitcast(FP8X4),
-                z_scales[g][:, agents],
+                z_plane(g, agents),
                 z_woven[g][:].rearrange("p c n t -> p (c n t)")[:, 4 * agents.start : 4 * agents.stop],
             )
 
@@ -328,7 +343,7 @@ def tile_list_crowd_steering_features_kernel(
                     lhsT=codes[:, cols].bitcast(FP8X4),
                     lhsT_scale=scales[:, cols],
                     rhs=z_codes[a][:, agents].bitcast(FP8X4),
-                    rhs_scale=z_scales[a][:, agents],
+                    rhs_scale=z_plane(a, agents),
                     start=(a == 0 and e == 0),
                     stop=(a == 1 and e == len(slots) - 1),
                 )
@@ -347,8 +362,7 @@ def tile_list_crowd_steering_features_kernel(
             i = int(step[1])
             if n > 0 and steps[n - 1][0] == "w":
                 done = int(steps[n - 1][1])
-                apply_style(nc.gpsimd, done, slice(0, 2))
-                apply_style(nc.gpsimd, done, slice(2, 4))
+                apply_style(nc.gpsimd, done, slice(0, CHUNKS))
                 if done == 3:
                     for c in range(CHUNKS):
                         weave(nc.scalar.copy, 0, slice(c, c + 1), slice(0, 4))
@@ -360,21 +374,26 @@ def tile_list_crowd_steering_features_kernel(
             else:
                 place(i, list3, h1[i])
 
-        quantise_z(0, slice(0, T2))
-        early = [bank(n, f"y_first{n}") for n in range(8)]
+        quantise_z(0, slice(0, 512))
+        early = [bank(n, f"y_first{n}") for n in range(4)]
         for acc, (agents, slots) in zip(early, first_banks):
             project(acc, agents, 0, slots, 0)
-        bump = held("bump7", [P, S], F32, tag="big1")
+        bump = placed("bump7", [P, S], F32, RING + 1088)
         nc.scalar.activation(bump[:], h1[7], ACT.Exp, scale=-1.0)
         nc.vector.tensor_tensor(pages[7][:].indirect(list3[:]), bump[:], gains1[3], MULT)
 
+        late_scales = placed("late_scales", [P, 1024 + 512], U8, RING + 1088)
+        z_scales[0, 1] = late_scales[:, 1024:]
         for agents in pieces:
             c, start = divmod(agents.start, CHUNK)
             cols = slice(start, start + agents.stop - agents.start)
             apply_style(nc.vector, 7, slice(c, c + 1), cols)
             weave(nc.vector.tensor_copy, 1, slice(c, c + 1), slice(2, 4), cols)
             quantise_z(1, agents)
-        w3_q.append(quantise_weight("w3_1", w3_bf[1], held("w3_scales1", [P, 1024], U8, tag="big1")))
+            if agents.stop == 512:
+                w3_q.append(quantise_weight("w3_1", w3_bf[1], late_scales[:, :1024]))
+            if agents.start >= 512:
+                quantise_z(0, agents)
 
         y_codes = [held(f"y_codes{g}", [P, T2], U32) for g in range(2)]
         y_scales = held("y_scales", [P, 2, T2], U8)
@@ -400,32 +419,37 @@ def tile_list_crowd_steering_features_kernel(
 
         y = {
             (0, 0): staged("y00", [P, 4, 512], F32, 0),
-            (0, 1): staged("y01", [P, 4, 512], F32, 1),
-            (1, 0): staged("y10", [P, 4, 512], F32, 2),
-            (1, 1): held("y11", [P, 4, 512], F32, tag="big0"),
+            (1, 0): staged("y10", [P, 4, 512], F32, 1),
+            (0, 1): held("y01", [P, 4, 512], F32, tag="big0"),
+            (1, 1): staged("y11", [P, 4, 512], F32, 2),
         }
-        for acc, (agents, slots) in zip(early, first_banks):
-            half, start = divmod(agents.start, 512)
-            local = slice(start, start + agents.stop - agents.start)
-            rows = y[0, half]
-            project(acc, agents, 0, slots, 1)
-            nc.scalar.copy(rows[:, slots[0] : slots[-1] + 1, local], acc[:].rearrange("p (t n) -> p t n", t=len(slots)))
-            if slots[-1] == 3:
-                nc.sync.dma_start(y_rows[0][:, :, agents], rows[:, :, local])
-                if agents.stop % 512 == 0:
-                    emit_planes([slice(0, 512)], rows[:], 0, slice(512 * half, 512 * (half + 1)), f"page{half}")
         for half in range(2):
+            both = slice(512 * half, 512 * (half + 1))
+            rows = y[0, half]
+            for n, (agents, slots) in enumerate(first_banks[4 * half : 4 * half + 4]):
+                local = slice(agents.start - both.start, agents.stop - both.start)
+                if half == 0:
+                    acc = early[n]
+                else:
+                    acc = bank(n, f"y_third{n}")
+                    project(acc, agents, 0, slots, 0)
+                project(acc, agents, 0, slots, 1)
+                nc.scalar.copy(
+                    rows[:, slots[0] : slots[-1] + 1, local], acc[:].rearrange("p (t n) -> p t n", t=len(slots))
+                )
+                if slots[-1] == 3:
+                    nc.sync.dma_start(y_rows[0][:, :, agents], rows[:, :, local])
+            emit_planes([slice(0, 512)], rows[:], 0, both, "page0")
             rows = y[1, half]
-            agents = slice(512 * half, 512 * (half + 1))
             for t in range(4):
-                acc = bank(4 * half + t, f"y_second{half}{t}")
+                acc = bank(4 + t, f"y_second{half}{t}")
                 for a in range(2):
-                    project(acc, agents, 1, (t,), a)
+                    project(acc, both, 1, (t,), a)
                 nc.scalar.copy(rows[:, t, :], acc[:])
                 if t % 2 == 1:
-                    nc.sync.dma_start(y_rows[1][:, t - 1 : t + 1, agents], rows[:, t - 1 : t + 1, :])
+                    nc.sync.dma_start(y_rows[1][:, t - 1 : t + 1, both], rows[:, t - 1 : t + 1, :])
             shares = [slice(0, 512)] if half == 0 else [slice(0, 336), slice(336, 512)]
-            emit_planes(shares, rows[:], 1, agents, f"page{half}")
+            emit_planes(shares, rows[:], 1, both, "page1")
         for q in range(4):
             (nc.scalar, nc.sync)[q % 2].dma_start(
                 out_2[:, 4 * q : 4 * q + 4, :].rearrange("g r n -> r g n").bitcast(I32),

@@ -22,10 +22,11 @@ CHUNK = 256
 CHUNKS = T2 // CHUNK
 PAGES = H // P
 ROUNDED = 0
-TAB1 = ROUNDED + 2 * 8192
+LAST_RUNNER = ROUNDED + 6144
+TAB1 = ROUNDED + 12288 + 8192
 STAGE = TAB1 + 8192
-RING = STAGE + 4 * 8192 + 960
-RING_SLOT = (4096, 0, 2048)
+RING = STAGE + 4 * 8192
+RUNNER_BYTES = (RING + 2048, RING, RING + 4096, RING, RING + 2112, RING + 4160, ROUNDED + 4096, LAST_RUNNER)
 
 
 def tile_list_crowd_steering_features_kernel(
@@ -44,13 +45,13 @@ def tile_list_crowd_steering_features_kernel(
             return plane
 
         w2_plane = zeroed_plane(nc.vector, "w2_plane", H)
+        tab_plane = zeroed_plane(nc.gpsimd, "tab_plane", T)
         zero = first.tile([P, 1], F32, name="zero")
         nc.vector.memset(zero[:], 0.0)
         sin_zero = first.tile([P, 1], F32, name="sin_zero")
         nc.scalar.activation(sin_zero[:], zero[:], ACT.Sin)
         half_pi = first.tile([P, 1], F32, name="half_pi")
         nc.vector.tensor_scalar(half_pi[:], sin_zero[:], 1.0, math.pi / 2, op0=MULT, op1=ADD)
-        tab_plane = zeroed_plane(nc.gpsimd, "tab_plane", T)
 
         keep = ctx.enter_context(tc.tile_pool(name="keep", bufs=1))
         shared = ctx.enter_context(tc.tile_pool(name="shared", bufs=1))
@@ -66,9 +67,9 @@ def tile_list_crowd_steering_features_kernel(
             nc.sync.dma_start(lst[:], src)
             return lst
 
-        def load_scale_rows(queue, plane, src):
+        def load_scale_rows(queue, plane, src, quadrants):
             passes = src.shape[0]
-            for q in range(4):
+            for q in quadrants:
                 queue.dma_start(
                     plane[32 * q : 32 * q + 4 * passes, :].bitcast(I32),
                     src[:, 4 * q : 4 * q + 4, :].bitcast(I32),
@@ -128,8 +129,9 @@ def tile_list_crowd_steering_features_kernel(
         w2_raw = held("w2_raw", [P, 2 * H], U8)
         nc.sync.dma_start(w2_raw[:].bitcast(I32), w2_words[0].bitcast(I32))
         tab2 = load_words(held("tab2", [P, T], I32, tag="big0"), tab2_words[0])
-        load_scale_rows(nc.gpsimd, tab_plane, tab_scales)
-        load_scale_rows(nc.sync, w2_plane, w2_scales)
+        load_scale_rows(nc.gpsimd, tab_plane, tab_scales, (0, 2))
+        load_scale_rows(nc.sync, w2_plane, w2_scales, range(4))
+        load_scale_rows(nc.sync, tab_plane, tab_scales, (1, 3))
         gains2 = load_gains("gains2_first", wg2, 0, 1)
         list4 = load_list("list4", offs4)
         gains2 = gains2 + load_gains("gains2_rest", wg2, 1, 4)
@@ -225,7 +227,7 @@ def tile_list_crowd_steering_features_kernel(
                 nc.gpsimd.tensor_tensor(h[:, n, :], h[:, n, :], gains1[(first + n) % 4], MULT)
 
         def ring(name, i):
-            return placed(name, [P, S], F32, RING + RING_SLOT[i % 3])
+            return placed(name, [P, S], F32, RUNNER_BYTES[i])
 
         def weigh(weighed, h, gains):
             nc.gpsimd.tensor_tensor(weighed, h, gains, MULT)
@@ -268,7 +270,7 @@ def tile_list_crowd_steering_features_kernel(
         place_fused(2, whole)
         w1_q = []
         for half in range(2):
-            rounded = placed(f"w1_bf{half}", [P, 2, 2048], BF16, ROUNDED + 8192 * half)
+            rounded = placed(f"w1_bf{half}", [P, 2, 2048], BF16, ROUNDED + (64, 12288)[half])
             scales = held(f"w1_scales{half}", [P, 1024], U8)[:]
             round_weight([w1_raw[a, half] for a in range(2)], rounded)
             w1_q.append(quantise_weight(f"w1_{half}", rounded, scales))
@@ -286,7 +288,7 @@ def tile_list_crowd_steering_features_kernel(
             w3_bf.append(held(f"w3_bf{g}", [P, 2, 2048], BF16, tag=("big1", None)[g]))
             round_weight(raws, w3_bf[g])
         styles += [load_style(i) for i in (6, 7)]
-        w3_q = [quantise_weight("w3_0", w3_bf[0], placed("w3_scales0", [P, 1024], U8, RING + 64)[:])]
+        w3_q = [quantise_weight("w3_0", w3_bf[0], placed("w3_scales0", [P, 1024], U8, LAST_RUNNER + 64)[:])]
 
         first_rows = held("z_rows0", [P, CHUNKS, 4, CHUNK], BF16, tag="big0")
         pair_rows = [held(f"z_rows1_{pair}", [P, CHUNKS, 2, CHUNK], BF16) for pair in range(2)]
@@ -302,7 +304,7 @@ def tile_list_crowd_steering_features_kernel(
         ]
         z_codes = [held(f"z_codes{g}", [P, T2], U32) for g in range(2)]
         z_scales = {
-            (0, 0): placed("z_scales00", [P, 512], U8, RING - 448)[:],
+            (0, 0): placed("z_scales00", [P, 512], U8, LAST_RUNNER - 448)[:],
             (1, 0): held("z_scales10", [P, 512], U8)[:],
             (1, 1): held("z_scales11", [P, 512], U8)[:],
         }
@@ -378,11 +380,11 @@ def tile_list_crowd_steering_features_kernel(
         early = [bank(n, f"y_first{n}") for n in range(4)]
         for acc, (agents, slots) in zip(early, first_banks):
             project(acc, agents, 0, slots, 0)
-        bump = placed("bump7", [P, S], F32, RING + 1088)
+        bump = placed("bump7", [P, S], F32, LAST_RUNNER + 1088)
         nc.scalar.activation(bump[:], h1[7], ACT.Exp, scale=-1.0)
         nc.vector.tensor_tensor(pages[7][:].indirect(list3[:]), bump[:], gains1[3], MULT)
 
-        late_scales = placed("late_scales", [P, 1024 + 512], U8, RING + 1088)
+        late_scales = placed("late_scales", [P, 1024 + 512], U8, LAST_RUNNER + 1088)
         z_scales[0, 1] = late_scales[:, 1024:]
         for agents in pieces:
             c, start = divmod(agents.start, CHUNK)

@@ -18,15 +18,24 @@ ADD = mybir.AluOpType.add
 P = 128
 K, K2, H, N, T, S, T2 = 1024, 512, 1024, 1024, 2048, 512, 1024
 FLOPS = 2 * K * H * S + 2 * K2 * H * S + 2 * H * N * T2
-CHUNK = 256
-CHUNKS = T2 // CHUNK
 PAGES = H // P
-ROUNDED = 0
-LAST_RUNNER = ROUNDED + 6144
-TAB1 = ROUNDED + 12288 + 8192
-STAGE = TAB1 + 8192
-RING = STAGE + 4 * 8192
-RUNNER_BYTES = (RING + 2048, RING, RING + 4096, RING, RING + 2112, RING + 4160, ROUNDED + 4096, LAST_RUNNER)
+HALF = T2 // 2
+KIB = 1024
+FUSED = 3
+QUARTER = T2 // 4
+LAST_SHARE = 176
+
+TAB2 = 0
+TAB0 = TAB2 + 8 * KIB
+TAB1 = TAB0 + 8 * KIB
+GAINS2 = TAB1 + 8 * KIB
+RAW = GAINS2 + 8 * KIB
+W1_BF = RAW + 32 * KIB
+W1_CODES = W1_BF + 16 * KIB
+FEAT = W1_CODES + 8 * KIB
+STYLE = FEAT + 16 * KIB + 64
+PAGE = STYLE + 24 * KIB
+SHARED_END = PAGE + 20 * KIB
 
 
 def tile_list_crowd_steering_features_kernel(
@@ -59,8 +68,11 @@ def tile_list_crowd_steering_features_kernel(
         def placed(name, shape, dtype, offset):
             return shared.tile(shape, dtype, name=name, offset=offset, align_bytes=64)
 
-        def held(name, shape, dtype, tag=None, bufs=1):
-            return keep.tile(shape, dtype, name=name, tag=tag or name, bufs=bufs, align_bytes=64)
+        def held(name, shape, dtype):
+            return keep.tile(shape, dtype, name=name, tag=name, align_bytes=64)
+
+        def bank(idx, name):
+            return psum.tile([P, 512], F32, name=name, tag=f"bank{idx}")
 
         def load_list(name, src):
             lst = lists.tile([P, S // 16], U16, name=name, tag=name)
@@ -75,28 +87,27 @@ def tile_list_crowd_steering_features_kernel(
                     src[:, 4 * q : 4 * q + 4, :].bitcast(I32),
                 )
 
-        def load_words(words, src):
+        def load_words(name, offset, src):
+            words = placed(name, [P, T], I32, offset)
             nc.sync.dma_start(words[:], src.rearrange("p n i -> p (n i)").bitcast(I32))
             return words
 
-        def load_gains(name, src, t0, t1):
-            gains = held(name, [P, t1 - t0, S], F32)
+        def load_gains(gains, src, t0):
+            count = gains.shape[1]
             for q in (0, 2, 1, 3):
-                nc.sync.dma_start(gains[32 * q : 32 * q + 32], src.rearrange("(u t) j -> u t j", t=4)[:, t0:t1, :])
-            return [gains[:, t, :] for t in range(t1 - t0)]
+                nc.sync.dma_start(gains[32 * q : 32 * q + 32], src.rearrange("(u t) j -> u t j", t=4)[:, t0 : t0 + count, :])
+            return [gains[:, t, :] for t in range(count)]
 
-        def staged(name, shape, dtype, slot, shift=0):
-            return placed(name, shape, dtype, STAGE + 8192 * slot + shift)
-
-        def load_weight(name, src, a, half, slot):
-            raw = staged(f"{name}_raw{a}{half}", [P, 4, 512], F32, slot)
+        def load_weight(name, src, a, half):
+            raw = placed(f"{name}_raw{a}{half}", [P, 4, 512], F32, RAW + 8 * KIB * (2 * half + a))
             rows = src[512 * a : 512 * (a + 1), 512 * half : 512 * (half + 1)]
             nc.sync.dma_start(raw[:], rows.rearrange("(p j) c -> p j c", j=4))
             return raw
 
         def load_style(i):
             g, t = divmod(i, 4)
-            st = held(f"style{i}", [P, T2], F32)
+            offset = STYLE + 4 * KIB * i if i < 6 else W1_CODES + 4 * KIB * (i - 6)
+            st = placed(f"style{i}", [P, T2], F32, offset)
             nc.sync.dma_start(st[:], style.rearrange("(g p t) n -> g t p n", g=2, t=4)[g, t])
             return st
 
@@ -105,20 +116,16 @@ def tile_list_crowd_steering_features_kernel(
             nc.vector.tensor_copy(picked[:], window[:].bitcast(dtype).indirect(lst[:]))
             return picked
 
-        def round_weight(raws, rounded):
-            for n, raw in enumerate(raws):
+        def round_weight(raw, rounded):
+            count = 4 // len(rounded)
+            for s, part in enumerate(rounded):
                 nc.scalar.copy(
-                    rounded[:, n, :].rearrange("p (t m u e) -> p m u t e", t=4, u=2, e=2),
-                    raw[:].rearrange("p (u e) (m t) -> p m u t e", e=2, t=4),
+                    part.rearrange("p (t m u e) -> p m u t e", t=count, u=2, e=2),
+                    raw[:].rearrange("p (u e) (m t) -> p m u t e", e=2, t=4)[:, :, :, count * s : count * (s + 1), :],
                 )
 
-        def quantise_weight(name, rounded, scales):
-            codes = held(f"{name}_codes", [P, 1024], U32)
-            nc.vector.quantize_mx(codes[:].bitcast(FP8X4), scales, rounded[:].rearrange("p a c -> p (a c)"))
-            return codes, scales
-
-        def bank(idx, name):
-            return psum.tile([P, 512], F32, name=name, tag=f"bank{idx % 8}")
+        def quantise(codes, scales, rounded):
+            nc.vector.quantize_mx(codes.bitcast(FP8X4), scales, rounded)
 
         tab2_plane = held("tab2_plane", [P, T], U8)
         for q in range(4):
@@ -128,22 +135,19 @@ def tile_list_crowd_steering_features_kernel(
         list1 = load_list("list1", offs)
         w2_raw = held("w2_raw", [P, 2 * H], U8)
         nc.sync.dma_start(w2_raw[:].bitcast(I32), w2_words[0].bitcast(I32))
-        tab2 = load_words(held("tab2", [P, T], I32, tag="big0"), tab2_words[0])
+        tab2 = load_words("tab2", TAB2, tab2_words[0])
         load_scale_rows(nc.gpsimd, tab_plane, tab_scales, (0, 2))
         load_scale_rows(nc.sync, w2_plane, w2_scales, range(4))
         load_scale_rows(nc.sync, tab_plane, tab_scales, (1, 3))
-        gains2 = load_gains("gains2_first", wg2, 0, 1)
+        gains2 = load_gains(placed("gains2_first", [P, 1, S], F32, GAINS2), wg2, 0)
         list4 = load_list("list4", offs4)
-        gains2 = gains2 + load_gains("gains2_rest", wg2, 1, 4)
-        tab = [
-            load_words(held("tab0", [P, T], I32, tag="big1"), tab_words[0]),
-            load_words(placed("tab1", [P, T], I32, TAB1), tab_words[1]),
-        ]
-        w1_raw = {(a, half): load_weight("w1", w1, a, half, 2 * half + a) for half in range(2) for a in range(2)}
+        gains2 = gains2 + load_gains(placed("gains2_rest", [P, 3, S], F32, GAINS2 + 2 * KIB), wg2, 1)
+        tab = [load_words("tab0", TAB0, tab_words[0]), load_words("tab1", TAB1, tab_words[1])]
+        w1_raw = {(a, half): load_weight("w1", w1, a, half) for half in range(2) for a in range(2)}
         centre = held("centre", [P, 2, 4], F32)
         nc.sync.dma_start(centre[:], ctr.rearrange("(g p t) -> p g t", g=2, t=4))
         list3 = load_list("list3", offs3)
-        gains1 = load_gains("gains1", wg1, 0, 4)
+        gains1 = load_gains(held("gains1", [P, 4, S], F32), wg1, 0)
         styles = [load_style(i) for i in range(2)]
 
         w2_dealt = held("w2_dealt", [P, 2, H], U8)
@@ -162,6 +166,7 @@ def tile_list_crowd_steering_features_kernel(
             )
 
         halves = [slice(0, S // 2), slice(S // 2, S)]
+        whole = [slice(0, S)]
 
         def entries(cols):
             return slice(cols.start // 16, cols.stop // 16)
@@ -173,285 +178,301 @@ def tile_list_crowd_steering_features_kernel(
         for g, cols in enumerate(halves):
             nc.vector.tensor_copy(v2_words[:, cols], tab2[:].bitcast(U32).indirect(list2[:, entries(cols)]))
             deal_scales(g)
-
         v_scales = first.tile([P, S], U8, name="v_scales", tag="w2_plane", align_bytes=64)
         nc.vector.tensor_copy(v_scales[:], tab_plane[:].indirect(list1[:]))
 
-        h2, h1, pages = {}, {}, {}
+        def feature(name, offset):
+            return placed(name, [P, S], F32, offset)
 
-        def angle(i, h, cols, acc):
+        def slot(n):
+            return FEAT + 2 * KIB * n + (64 if n > 2 else 0)
+
+        page_bytes = {0: PAGE, 1: PAGE + 4 * KIB, 2: PAGE + 8 * KIB, 3: TAB1, 4: PAGE + 12 * KIB, 5: PAGE + 16 * KIB,
+                      6: W1_BF, 7: W1_BF + 8 * KIB}
+        pages = {}
+
+        def new_page(i):
+            pages[i] = placed(f"page{i}", [P, T2], F32, page_bytes[i])
+
+        def cosines(i, pieces):
             g, t = divmod(i, 4)
-            nc.tensor.matmul_mx(
-                acc[:, cols],
-                lhsT=w2_dealt[:, g, 2 * P * t : 2 * P * (t + 1)].bitcast(FP4X4),
-                lhsT_scale=w2_plane_dealt[:, g, P * t : P * (t + 1)],
-                rhs=v2_words[:, cols].bitcast(FP8X4),
-                rhs_scale=v2_scales[:, cols],
-                start=True,
-                stop=True,
-            )
-            nc.scalar.activation(h[:, cols], acc[:, cols], ACT.Abs)
-
-        def cosine(h):
-            nc.scalar.activation(h, h, ACT.Sin, bias=half_pi[:], scale=-1.0)
-
-        def runners(first, count):
-            h = held(f"h2_{first}", [P, count, S], F32, tag=f"h{first}")
-            for n in range(count):
-                angle(first + n, h[:, n, :], slice(0, S), bank(first + n, f"angle{first + n}"))
-                h2[first + n] = h[:, n, :]
-            cosine(h[:])
-
-        def walkers(first, w1_q):
-            h = held(f"h1_{first}", [P, 2, S], F32, tag=f"h{(0, 2, 3, 5)[first // 2]}")
-            codes, scales = w1_q
-            for n in range(2):
-                half, t = divmod(first + n, 4)
-                acc = bank(first + n, f"dist{first + n}")
-                for a in range(2):
-                    cols = slice(512 * a + P * t, 512 * a + P * (t + 1))
-                    nc.tensor.matmul_mx(
-                        acc[:],
-                        lhsT=codes[:, cols].bitcast(FP8X4),
-                        lhsT_scale=scales[:, cols],
-                        rhs=v_words[a][:].bitcast(FP8X4),
-                        rhs_scale=v_scales[4 * a : P, :],
-                        start=(a == 0),
-                        stop=(a == 1),
-                    )
-                nc.scalar.activation(h[:, n, :], acc[:], ACT.Square, bias=centre[:, half, t : t + 1], scale=-1.0)
-                h1[first + n] = h[:, n, :]
-            count = 2 if first < 6 else 1
-            nc.scalar.activation(h[:, :count, :], h[:, :count, :], ACT.Exp, scale=-1.0)
-            for n in range(count):
-                nc.gpsimd.tensor_tensor(h[:, n, :], h[:, n, :], gains1[(first + n) % 4], MULT)
-
-        def ring(name, i):
-            return placed(name, [P, S], F32, RUNNER_BYTES[i])
+            h = feature(f"h2_{i}", slot(i))
+            for n, cols in enumerate(pieces):
+                acc = bank((i + 7 * n) % 8, f"angle{i}_{n}")
+                nc.tensor.matmul_mx(
+                    acc[:, cols],
+                    lhsT=w2_dealt[:, g, 2 * P * t : 2 * P * (t + 1)].bitcast(FP4X4),
+                    lhsT_scale=w2_plane_dealt[:, g, P * t : P * (t + 1)],
+                    rhs=v2_words[:, cols].bitcast(FP8X4),
+                    rhs_scale=v2_scales[:, cols],
+                    start=True,
+                    stop=True,
+                )
+                nc.scalar.activation(h[:, cols], acc[:, cols], ACT.Abs)
+                nc.scalar.activation(h[:, cols], h[:, cols], ACT.Sin, bias=half_pi[:], scale=-1.0)
+            return h
 
         def weigh(weighed, h, gains):
-            nc.gpsimd.tensor_tensor(weighed, h, gains, MULT)
+            nc.gpsimd.tensor_tensor(weighed[:], h[:], gains, MULT)
             return weighed
 
         def place(i, lst, weighed):
-            nc.vector.tensor_copy(pages[i][:].indirect(lst[:]), weighed)
+            nc.vector.tensor_copy(pages[i][:].indirect(lst[:]), weighed[:])
 
-        def new_page(i):
-            if i in (2, 3):
-                pages[i] = placed(f"page{i}", [P, T2], F32, TAB1 + 4096 * (i - 2))
-            elif i in (4, 5, 6):
-                pages[i] = placed(f"page{i}", [P, T2], F32, ROUNDED + (0, 8192, 12288)[i - 4])
-            elif i == 7:
-                pages[i] = held("page7", [P, T2], F32, tag="big0")
-            else:
-                pages[i] = held(f"page{i}", [P, T2], F32)
-
-        def fused_features(i, pieces):
-            h = ring(f"h2_{i}", i)
-            for n, cols in enumerate(pieces):
-                angle(i, h[:], cols, bank(i + 7 * n, f"angle{i}_{n}"))
-                cosine(h[:, cols])
-            h2[i] = h
-
-        def place_fused(i, pieces):
+        h2 = [cosines(i, halves if i == 0 else whole) for i in range(PAGES)]
+        for i in range(FUSED):
             new_page(i)
-            for cols in pieces:
+            for cols in halves if i == 0 else whole:
                 nc.vector.tensor_tensor(
                     pages[i][:].indirect(list4[:, entries(cols)]), h2[i][:, cols], gains2[i][:, cols], MULT
                 )
-
-        whole = [slice(0, S)]
-        for i in range(3):
-            fused_features(i, halves if i == 0 else whole)
-        for i in range(2):
-            place_fused(i, halves if i == 0 else whole)
-        runners(3, 2)
         v_words = [gather(f"v_words{a}", tab[a], list1, U32) for a in range(2)]
-        place_fused(2, whole)
-        w1_q = []
-        for half in range(2):
-            rounded = placed(f"w1_bf{half}", [P, 2, 2048], BF16, ROUNDED + (64, 12288)[half])
-            scales = held(f"w1_scales{half}", [P, 1024], U8)[:]
-            round_weight([w1_raw[a, half] for a in range(2)], rounded)
-            w1_q.append(quantise_weight(f"w1_{half}", rounded, scales))
-            if half == 0:
-                runners(5, 2)
-                runners(7, 1)
-        weighed = {i: weigh(ring(f"weighed{i}", i)[:], h2[i], gains2[i % 4]) for i in range(3, PAGES)}
-        for first in range(0, PAGES, 2):
-            walkers(first, w1_q[first // 4])
-
-        w3_bf = []
-        for g in range(2):
-            raws = [load_weight("w3", w3, a, g, 2 * g + a) for a in range(2)]
-            styles += [load_style(i) for i in (2 + 2 * g, 3 + 2 * g)]
-            w3_bf.append(held(f"w3_bf{g}", [P, 2, 2048], BF16, tag=("big1", None)[g]))
-            round_weight(raws, w3_bf[g])
-        styles += [load_style(i) for i in (6, 7)]
-        w3_q = [quantise_weight("w3_0", w3_bf[0], placed("w3_scales0", [P, 1024], U8, LAST_RUNNER + 64)[:])]
-
-        first_rows = held("z_rows0", [P, CHUNKS, 4, CHUNK], BF16, tag="big0")
-        pair_rows = [held(f"z_rows1_{pair}", [P, CHUNKS, 2, CHUNK], BF16) for pair in range(2)]
-
-        def z_rows(g, chunks, slots, cols):
-            if g == 0:
-                return first_rows[:, chunks, slots, cols]
-            return pair_rows[slots.start // 2][:, chunks, slots.start % 2 : slots.start % 2 + slots.stop - slots.start, cols]
-
-        z_woven = [
-            staged("z_woven0", [P, CHUNKS, CHUNK, 4], BF16, 3),
-            staged("z_woven1", [P, CHUNKS, CHUNK, 4], BF16, 2),
-        ]
-        z_codes = [held(f"z_codes{g}", [P, T2], U32) for g in range(2)]
-        z_scales = {
-            (0, 0): placed("z_scales00", [P, 512], U8, LAST_RUNNER - 448)[:],
-            (1, 0): held("z_scales10", [P, 512], U8)[:],
-            (1, 1): held("z_scales11", [P, 512], U8)[:],
+        after_fused = {3: slot(2) + 64 - 2 * KIB, 4: slot(2) + 64}
+        runners = {
+            i: weigh(feature(f"runner{i}", after_fused[i]) if i in after_fused else h2[i], h2[i], gains2[i % 4])
+            for i in range(FUSED, PAGES)
         }
 
-        def z_plane(g, agents):
-            half, start = divmod(agents.start, 512)
-            return z_scales[g, half][:, start : start + agents.stop - agents.start]
+        w1_codes = placed("w1_codes", [P, 2, 1024], U32, W1_CODES)
+        w1_scales = held("w1_scales", [P, 2, 1024], U8)
+        w1_bf = []
+        for half in range(2):
+            w1_bf.append(placed(f"w1_bf{half}", [P, 2, 2048], BF16, W1_BF + 8 * KIB * half))
+            for a in range(2):
+                round_weight(w1_raw[a, half], [w1_bf[half][:, a, :]])
+        for i in range(FUSED, PAGES):
+            if i >= 6:
+                half = i - 6
+                quantise(w1_codes[:, half, :], w1_scales[:, half, :], w1_bf[half][:].rearrange("p a c -> p (a c)"))
+            new_page(i)
+            place(i, list4, runners[i])
 
-        def apply_style(engine, i, chunks, cols=slice(0, CHUNK)):
+        walker_bytes = (slot(3), slot(4), slot(0), after_fused[3], after_fused[4], slot(5), slot(6), slot(7))
+
+        def squares(i):
+            half, t = divmod(i, 4)
+            h = feature(f"h1_{i}", walker_bytes[i])
+            acc = bank(i, f"dist{i}")
+            for a in range(2):
+                cols = slice(512 * a + P * t, 512 * a + P * (t + 1))
+                nc.tensor.matmul_mx(
+                    acc[:],
+                    lhsT=w1_codes[:, half, cols].bitcast(FP8X4),
+                    lhsT_scale=w1_scales[:, half, cols],
+                    rhs=v_words[a][:].bitcast(FP8X4),
+                    rhs_scale=v_scales[4 * a : P, :],
+                    start=(a == 0),
+                    stop=(a == 1),
+                )
+            nc.scalar.activation(h[:], acc[:], ACT.Square, bias=centre[:, half, t : t + 1], scale=-1.0)
+            return h
+
+        def bump(out, h):
+            nc.scalar.activation(out[:], h[:], ACT.Exp, scale=-1.0)
+            return out
+
+        walkers = {}
+        for i in range(PAGES):
+            h = squares(i)
+            if i == PAGES - 1:
+                last_squares = h
+            else:
+                out = feature("walker0", W1_BF + 12 * KIB) if i == 0 else h
+                walkers[i] = weigh(out, bump(h, h), gains1[i % 4])
+
+        early_bf = placed("early_bf", [P, 2, 2048], BF16, RAW + 24 * KIB)
+        second_bf = held("second_bf", [P, 2048], BF16)
+        w3_late_bf = held("w3_late_bf", [P, 2, 2, 1024], BF16)
+        rounded_w3 = {
+            (0, 0): [early_bf[:, 0, :]],
+            (1, 0): [second_bf[:]],
+            (0, 1): [w3_late_bf[:, pair, 0, :] for pair in range(2)],
+            (1, 1): [w3_late_bf[:, pair, 1, :] for pair in range(2)],
+        }
+        for a, g in ((1, 0), (0, 1), (1, 1), (0, 0)):
+            round_weight(load_weight("w3", w3, a, g), rounded_w3[a, g])
+        styles += [load_style(i) for i in range(2, PAGES)]
+
+        z_rows0 = [placed(f"z_rows0_{half}", [P, 4, HALF], BF16, TAB2 + 4 * KIB * half) for half in range(2)]
+        z_rows1 = [placed(f"z_rows1_{pair}", [P, 2, 2, HALF], BF16, (TAB0, TAB2)[pair]) for pair in range(2)]
+        z1_first_bf = placed("z1_first_bf", [P, 2048], BF16, RAW + 4 * KIB)
+        z_late_bf = placed("z_late_bf", [P, 2, 2, 1024], BF16, RAW - 4 * KIB)
+        front, back = slice(0, HALF), slice(HALF, T2)
+        quarters = [slice(HALF + QUARTER * n, HALF + QUARTER * (n + 1)) for n in range(2)]
+
+        def z_woven(g, agents):
+            if agents.start < HALF:
+                tile, start = (early_bf[:, 1, :], z1_first_bf[:])[g], agents.start
+            else:
+                n, start = divmod(agents.start - HALF, QUARTER)
+                tile = z_late_bf[:, n, g, :]
+            return tile[:, 4 * start : 4 * (start + agents.stop - agents.start)]
+
+        def z_rows(g, halves, slots):
+            if g == 0:
+                return z_rows0[halves][:, slots, :]
+            return z_rows1[slots.start // 2][:, halves, slots.start % 2 : slots.start % 2 + slots.stop - slots.start, :]
+
+        def apply_style(i):
             g, t = divmod(i, 4)
-            engine.tensor_tensor(
-                z_rows(g, chunks, slice(t, t + 1), cols).rearrange("p c t n -> p c (t n)"),
-                pages[i][:].rearrange("p (c n) -> p c n", n=CHUNK)[:, chunks, cols],
-                styles[i][:].rearrange("p (c n) -> p c n", n=CHUNK)[:, chunks, cols],
+            if g == 0:
+                for half, agents in enumerate((front, back)):
+                    nc.gpsimd.tensor_tensor(z_rows0[half][:, t, :], pages[i][:, agents], styles[i][:, agents], MULT)
+                return
+            nc.gpsimd.tensor_tensor(
+                z_rows(g, slice(0, 2), slice(t, t + 1)).rearrange("p c t n -> p c (t n)"),
+                pages[i][:].rearrange("p (c n) -> p c n", c=2),
+                styles[i][:].rearrange("p (c n) -> p c n", c=2),
                 MULT,
             )
 
-        def weave(copy, g, chunks, slots, cols=slice(0, CHUNK)):
+        def weave(copy, g, agents, slots):
+            half, start = divmod(agents.start, HALF)
+            cols = slice(start, start + agents.stop - agents.start)
             copy(
-                z_woven[g][:, chunks, cols, slots].rearrange("p c (n i) t -> p c n t i", i=4),
-                z_rows(g, chunks, slots, cols).rearrange("p c t (n i) -> p c n t i", i=4),
+                z_woven(g, agents).rearrange("p (n i t) -> p n t i", i=4, t=4)[:, :, slots, :],
+                z_rows(g, half, slots)[:, :, cols].rearrange("p t (n i) -> p n t i", i=4),
             )
 
-        def quantise_z(g, agents):
-            nc.vector.quantize_mx(
-                z_codes[g][:, agents].bitcast(FP8X4),
-                z_plane(g, agents),
-                z_woven[g][:].rearrange("p c n t -> p (c n t)")[:, 4 * agents.start : 4 * agents.stop],
-            )
+        for i in range(PAGES - 1):
+            place(i, list3, walkers[i])
+            apply_style(i)
+            if i == 3:
+                weave(nc.scalar.copy, 0, front, slice(0, 4))
+                last_bump = bump(feature("last_bump", TAB2), last_squares)
+                for agents in quarters:
+                    weave(nc.scalar.copy, 0, agents, slice(0, 4))
+            if i == 4:
+                last_walker = weigh(feature("last_walker", slot(7)), last_bump, gains1[3])
+            if i == 5:
+                for agents in [front] + quarters:
+                    weave(nc.scalar.copy, 1, agents, slice(0, 2))
+
+        early_codes = held("early_codes", [P, 2, 512], U32)
+        early_scales = held("early_scales", [P, 2, 512], U8)
+        quantise(early_codes[:].rearrange("p a c -> p (a c)"), early_scales[:].rearrange("p a c -> p (a c)"),
+                 early_bf[:].rearrange("p a c -> p (a c)"))
+        second_codes = held("second_codes", [P, 512], U32)
+        w3_late_codes = held("w3_late_codes", [P, 2, 2, 256], U32)
+        z1_first_codes = held("z1_first_codes", [P, 512], U32)
+        z1_first_scales = held("z1_first_scales", [P, 512], U8)
+        z_late_codes = held("z_late_codes", [P, 2, 2, QUARTER], U32)
+        z_late_scales = held("z_late_scales", [P, 2, 2, QUARTER], U8)
+        late_scales = {}
+
+        def w3_operand(a, g_out, t):
+            if g_out == 1:
+                cols = slice(P * (t % 2), P * (t % 2 + 1))
+                return w3_late_codes[:, t // 2, a, cols], late_scales[1][:, t // 2, a, cols]
+            cols = slice(P * t, P * (t + 1))
+            if a == 0:
+                return early_codes[:, 0, cols], early_scales[:, 0, cols]
+            return second_codes[:, cols], late_scales[0][:, cols]
+
+        def z_operand(a, agents):
+            if agents.start >= HALF:
+                n = (agents.start - HALF) // QUARTER
+                return z_late_codes[:, n, a, :], z_late_scales[:, n, a, :]
+            if a == 0:
+                return early_codes[:, 1, agents], early_scales[:, 1, agents]
+            return z1_first_codes[:, agents], z1_first_scales[:, agents]
 
         def project(acc, agents, g_out, slots, a):
-            codes, scales = w3_q[g_out]
+            z_codes, z_scales = z_operand(a, agents)
             width = agents.stop - agents.start
             for e, t in enumerate(slots):
-                cols = slice(512 * a + P * t, 512 * a + P * (t + 1))
+                codes, scales = w3_operand(a, g_out, t)
                 nc.tensor.matmul_mx(
                     acc[:, width * e : width * (e + 1)],
-                    lhsT=codes[:, cols].bitcast(FP8X4),
-                    lhsT_scale=scales[:, cols],
-                    rhs=z_codes[a][:, agents].bitcast(FP8X4),
-                    rhs_scale=z_plane(a, agents),
+                    lhsT=codes.bitcast(FP8X4),
+                    lhsT_scale=scales,
+                    rhs=z_codes.bitcast(FP8X4),
+                    rhs_scale=z_scales,
                     start=(a == 0 and e == 0),
                     stop=(a == 1 and e == len(slots) - 1),
                 )
 
-        def chunk(c):
-            return slice(CHUNK * c, CHUNK * (c + 1))
-
-        pieces = [slice(0, 128), slice(128, 256)] + [chunk(c) for c in range(1, CHUNKS)]
-        first_banks = [
-            (agents, tuple(range(t, t + 512 // (agents.stop - agents.start))))
-            for agents in pieces
-            for t in range(0, 4, 512 // (agents.stop - agents.start))
-        ]
-        steps = ["r3", "r4", "r5", "r6", "w0", "w1", "w2", "w3", "w4", "w5", "w6", "r7"]
-        for n, step in enumerate(steps):
-            i = int(step[1])
-            if n > 0 and steps[n - 1][0] == "w":
-                done = int(steps[n - 1][1])
-                apply_style(nc.gpsimd, done, slice(0, CHUNKS))
-                if done == 3:
-                    for c in range(CHUNKS):
-                        weave(nc.scalar.copy, 0, slice(c, c + 1), slice(0, 4))
-                if done == 5:
-                    weave(nc.scalar.copy, 1, slice(0, CHUNKS), slice(0, 2))
-            if step[0] == "r":
-                new_page(i)
-                place(i, list4, weighed[i])
-            else:
-                place(i, list3, h1[i])
-
-        quantise_z(0, slice(0, 512))
+        pieces = [slice(P * n, P * (n + 1)) for n in range(4)]
         early = [bank(n, f"y_first{n}") for n in range(4)]
-        for acc, (agents, slots) in zip(early, first_banks):
-            project(acc, agents, 0, slots, 0)
-        bump = placed("bump7", [P, S], F32, LAST_RUNNER + 1088)
-        nc.scalar.activation(bump[:], h1[7], ACT.Exp, scale=-1.0)
-        nc.vector.tensor_tensor(pages[7][:].indirect(list3[:]), bump[:], gains1[3], MULT)
+        for acc, agents in zip(early, pieces):
+            project(acc, agents, 0, range(4), 0)
+        place(PAGES - 1, list3, last_walker)
 
-        late_scales = placed("late_scales", [P, 1024 + 512], U8, LAST_RUNNER + 1088)
-        z_scales[0, 1] = late_scales[:, 1024:]
-        for agents in pieces:
-            c, start = divmod(agents.start, CHUNK)
+        late_scales[0] = placed("second_scales", [P, 512], U8, slot(7))
+        late_scales[1] = placed("w3_late_scales", [P, 2, 2, 256], U8, slot(7) + 512)
+
+        def last_style(agents):
+            half, start = divmod(agents.start, HALF)
             cols = slice(start, start + agents.stop - agents.start)
-            apply_style(nc.vector, 7, slice(c, c + 1), cols)
-            weave(nc.vector.tensor_copy, 1, slice(c, c + 1), slice(2, 4), cols)
-            quantise_z(1, agents)
-            if agents.stop == 512:
-                w3_q.append(quantise_weight("w3_1", w3_bf[1], late_scales[:, :1024]))
-            if agents.start >= 512:
-                quantise_z(0, agents)
+            nc.vector.tensor_tensor(z_rows1[1][:, half, 1, cols], pages[7][:, agents], styles[7][:, agents], MULT)
+            weave(nc.vector.tensor_copy, 1, agents, slice(2, 4))
+
+        for n, agents in enumerate(pieces):
+            last_style(agents)
+            if n == 0:
+                quantise(second_codes[:], late_scales[0][:], second_bf[:])
+            quantise(z1_first_codes[:, agents], z1_first_scales[:, agents], z_woven(1, agents))
+        for pair in range(2):
+            quantise(*(tile[:, pair].rearrange("p a c -> p (a c)") for tile in (w3_late_codes, late_scales[1], w3_late_bf)))
+        for n, agents in enumerate(quarters):
+            last_style(agents)
+            quantise(*(tile[:, n].rearrange("p a c -> p (a c)") for tile in (z_late_codes, z_late_scales, z_late_bf)))
 
         y_codes = [held(f"y_codes{g}", [P, T2], U32) for g in range(2)]
         y_scales = held("y_scales", [P, 2, T2], U8)
         y_rows = out_0.rearrange("(g p t) n -> g p t n", g=2, t=4)
 
-        def emit_planes(shares, values, g_out, agents, tag):
+        def quantise_y(values, g_out, agents, on_vector):
             width = agents.stop - agents.start
-            woven = held(f"y_woven{g_out}_{agents.start}", [P, width, 4], BF16, tag=tag)
-            for share, copy in zip(shares, (nc.vector.tensor_copy, nc.scalar.copy)):
+            woven = placed(f"y_woven{g_out}_{agents.start}", [P, width, 4], BF16, PAGE + 8 * agents.start + 8 * KIB * g_out)
+            shares = ((slice(0, on_vector), nc.vector.tensor_copy), (slice(on_vector, width), nc.scalar.copy))
+            for share, copy in shares[: 1 if on_vector == width else 2]:
                 copy(
                     woven[:, share, :].rearrange("p (n i) t -> p n t i", i=4),
                     values[:, :, share].rearrange("p t (n i) -> p n t i", i=4),
                 )
-            nc.vector.quantize_mx(
-                y_codes[g_out][:, agents].bitcast(FP8X4),
-                y_scales[:, g_out, agents],
-                woven[:].rearrange("p n t -> p (n t)"),
-            )
+            quantise(y_codes[g_out][:, agents], y_scales[:, g_out, agents], woven[:].rearrange("p n t -> p (n t)"))
+
+        def store_codes(g_out, agents):
             nc.sync.dma_start(
                 out_1[g_out].rearrange("p n i -> p (n i)").bitcast(I32)[:, agents],
                 y_codes[g_out][:, agents].bitcast(I32),
             )
 
-        y = {
-            (0, 0): staged("y00", [P, 4, 512], F32, 0),
-            (1, 0): staged("y10", [P, 4, 512], F32, 1),
-            (0, 1): held("y01", [P, 4, 512], F32, tag="big0"),
-            (1, 1): staged("y11", [P, 4, 512], F32, 2),
-        }
-        for half in range(2):
-            both = slice(512 * half, 512 * (half + 1))
-            rows = y[0, half]
-            for n, (agents, slots) in enumerate(first_banks[4 * half : 4 * half + 4]):
-                local = slice(agents.start - both.start, agents.stop - both.start)
-                if half == 0:
-                    acc = early[n]
-                else:
-                    acc = bank(n, f"y_third{n}")
-                    project(acc, agents, 0, slots, 0)
-                project(acc, agents, 0, slots, 1)
-                nc.scalar.copy(
-                    rows[:, slots[0] : slots[-1] + 1, local], acc[:].rearrange("p (t n) -> p t n", t=len(slots))
-                )
-                if slots[-1] == 3:
-                    nc.sync.dma_start(y_rows[0][:, :, agents], rows[:, :, local])
-            emit_planes([slice(0, 512)], rows[:], 0, both, "page0")
-            rows = y[1, half]
-            for t in range(4):
-                acc = bank(4 + t, f"y_second{half}{t}")
-                for a in range(2):
-                    project(acc, both, 1, (t,), a)
-                nc.scalar.copy(rows[:, t, :], acc[:])
-                if t % 2 == 1:
-                    nc.sync.dma_start(y_rows[1][:, t - 1 : t + 1, both], rows[:, t - 1 : t + 1, :])
-            shares = [slice(0, 512)] if half == 0 else [slice(0, 336), slice(336, 512)]
-            emit_planes(shares, rows[:], 1, both, "page1")
+        def sums(g_out, half, layout, banks, passes, stores):
+            rows = placed(f"y{g_out}{half}", [P, 4, HALF], F32, (RAW + 8 * KIB, STYLE)[half] + 8 * KIB * g_out)
+
+            def local(agents):
+                return slice(agents.start - HALF * half, agents.stop - HALF * half)
+
+            for n, (acc, (agents, slots)) in enumerate(zip(banks, layout)):
+                for a in passes:
+                    project(acc, agents, g_out, range(slots.start, slots.stop), a)
+                width = agents.stop - agents.start
+                nc.scalar.copy(rows[:, slots, local(agents)], acc[:].rearrange("p (t n) -> p t n", n=width))
+                if n in stores:
+                    done, done_slots = stores[n]
+                    nc.sync.dma_start(y_rows[g_out][:, done_slots, done], rows[:, done_slots, local(done)])
+            return rows
+
+        def banks(g_out, half):
+            return [bank(4 * g_out + n, f"y{g_out}{half}{n}") for n in range(4)]
+
+        every, low, high = slice(0, 4), slice(0, 2), slice(2, 4)
+        by_piece = [(agents, every) for agents in pieces]
+        by_slot = [(front, slice(t, t + 1)) for t in range(4)]
+        by_quarter = [(agents, slots) for agents in quarters for slots in (low, high)]
+        first_stores = {0: (pieces[0], every), 1: (pieces[1], every), 3: (slice(QUARTER, HALF), every)}
+        y00 = sums(0, 0, by_piece, early, (1,), first_stores)
+        y10 = sums(1, 0, by_slot, banks(1, 0), (0, 1), {1: (front, low), 3: (front, high)})
+        y01 = sums(0, 1, by_quarter, banks(0, 1), (0, 1), {2: (back, low), 3: (back, high)})
+        y11 = sums(1, 1, by_quarter, banks(1, 1), (0, 1), {2: (back, low), 3: (back, high)})
+        for values, g_out, agents in ((y00, 0, front), (y10, 1, front), (y01, 0, back)):
+            quantise_y(values[:], g_out, agents, HALF)
+            store_codes(g_out, agents)
+        quantise_y(y11[:, :, :QUARTER], 1, quarters[0], QUARTER)
+        quantise_y(y11[:, :, QUARTER:], 1, quarters[1], LAST_SHARE)
+        store_codes(1, back)
         for q in range(4):
             (nc.scalar, nc.sync)[q % 2].dma_start(
                 out_2[:, 4 * q : 4 * q + 4, :].rearrange("g r n -> r g n").bitcast(I32),

@@ -23,7 +23,6 @@ HALF = T2 // 2
 KIB = 1024
 FUSED = 3
 QUARTER = T2 // 4
-LAST_SHARE = 176
 
 TAB2 = 0
 TAB0 = TAB2 + 8 * KIB
@@ -33,9 +32,8 @@ RAW = GAINS2 + 8 * KIB
 W1_BF = RAW + 32 * KIB
 W1_CODES = W1_BF + 16 * KIB
 FEAT = W1_CODES + 8 * KIB
-STYLE = FEAT + 16 * KIB + 64
+STYLE = FEAT + 18 * KIB + 64
 PAGE = STYLE + 24 * KIB
-SHARED_END = PAGE + 20 * KIB
 
 
 def tile_list_crowd_steering_features_kernel(
@@ -187,8 +185,8 @@ def tile_list_crowd_steering_features_kernel(
         def slot(n):
             return FEAT + 2 * KIB * n + (64 if n > 2 else 0)
 
-        page_bytes = {0: PAGE, 1: PAGE + 4 * KIB, 2: PAGE + 8 * KIB, 3: TAB1, 4: PAGE + 12 * KIB, 5: PAGE + 16 * KIB,
-                      6: W1_BF, 7: W1_BF + 8 * KIB}
+        page_bytes = {0: PAGE, 1: PAGE + 4 * KIB, 2: PAGE + 8 * KIB, 3: TAB1, 4: W1_BF, 5: W1_BF + 4 * KIB,
+                      6: W1_BF + 8 * KIB, 7: TAB2}
         pages = {}
 
         def new_page(i):
@@ -240,14 +238,14 @@ def tile_list_crowd_steering_features_kernel(
             w1_bf.append(placed(f"w1_bf{half}", [P, 2, 2048], BF16, W1_BF + 8 * KIB * half))
             for a in range(2):
                 round_weight(w1_raw[a, half], [w1_bf[half][:, a, :]])
-        for i in range(FUSED, PAGES):
-            if i >= 6:
-                half = i - 6
+        for i in range(FUSED, PAGES - 1):
+            if i in (4, 6):
+                half = i // 2 - 2
                 quantise(w1_codes[:, half, :], w1_scales[:, half, :], w1_bf[half][:].rearrange("p a c -> p (a c)"))
             new_page(i)
             place(i, list4, runners[i])
 
-        walker_bytes = (slot(3), slot(4), slot(0), after_fused[3], after_fused[4], slot(5), slot(6), slot(7))
+        walker_bytes = (slot(3), slot(4), slot(0), after_fused[3], after_fused[4], slot(5), slot(6), slot(8))
 
         def squares(i):
             half, t = divmod(i, 4)
@@ -274,11 +272,14 @@ def tile_list_crowd_steering_features_kernel(
         walkers = {}
         for i in range(PAGES):
             h = squares(i)
-            if i == PAGES - 1:
-                last_squares = h
-            else:
-                out = feature("walker0", W1_BF + 12 * KIB) if i == 0 else h
-                walkers[i] = weigh(out, bump(h, h), gains1[i % 4])
+            out = feature("walker0", W1_BF + 12 * KIB) if i == 0 else h
+            bump(h, h)
+            if i < PAGES - 1:
+                walkers[i] = weigh(out, h, gains1[i % 4])
+        last_walkers = []
+        for n, cols in enumerate(halves):
+            last_walkers.append(placed(f"last_walkers{n}", [P, S // 2], F32, GAINS2 + 2 * KIB * n))
+            nc.gpsimd.tensor_tensor(last_walkers[n][:], h[:, cols], gains1[3][:, cols], MULT)
 
         early_bf = placed("early_bf", [P, 2, 2048], BF16, RAW + 24 * KIB)
         second_bf = held("second_bf", [P, 2048], BF16)
@@ -293,8 +294,8 @@ def tile_list_crowd_steering_features_kernel(
             round_weight(load_weight("w3", w3, a, g), rounded_w3[a, g])
         styles += [load_style(i) for i in range(2, PAGES)]
 
-        z_rows0 = [placed(f"z_rows0_{half}", [P, 4, HALF], BF16, TAB2 + 4 * KIB * half) for half in range(2)]
-        z_rows1 = [placed(f"z_rows1_{pair}", [P, 2, 2, HALF], BF16, (TAB0, TAB2)[pair]) for pair in range(2)]
+        z_rows0 = placed("z_rows0", [P, 2, 4, HALF], BF16, TAB2)
+        z_rows1 = [placed(f"z_rows1_{pair}", [P, 2, 2, HALF], BF16, TAB0 + 4 * KIB * pair) for pair in range(2)]
         z1_first_bf = placed("z1_first_bf", [P, 2048], BF16, RAW + 4 * KIB)
         z_late_bf = placed("z_late_bf", [P, 2, 2, 1024], BF16, RAW - 4 * KIB)
         front, back = slice(0, HALF), slice(HALF, T2)
@@ -310,15 +311,11 @@ def tile_list_crowd_steering_features_kernel(
 
         def z_rows(g, halves, slots):
             if g == 0:
-                return z_rows0[halves][:, slots, :]
+                return z_rows0[:, halves, slots, :]
             return z_rows1[slots.start // 2][:, halves, slots.start % 2 : slots.start % 2 + slots.stop - slots.start, :]
 
         def apply_style(i):
             g, t = divmod(i, 4)
-            if g == 0:
-                for half, agents in enumerate((front, back)):
-                    nc.gpsimd.tensor_tensor(z_rows0[half][:, t, :], pages[i][:, agents], styles[i][:, agents], MULT)
-                return
             nc.gpsimd.tensor_tensor(
                 z_rows(g, slice(0, 2), slice(t, t + 1)).rearrange("p c t n -> p c (t n)"),
                 pages[i][:].rearrange("p (c n) -> p c n", c=2),
@@ -338,18 +335,21 @@ def tile_list_crowd_steering_features_kernel(
             place(i, list3, walkers[i])
             apply_style(i)
             if i == 3:
-                weave(nc.scalar.copy, 0, front, slice(0, 4))
-                last_bump = bump(feature("last_bump", TAB2), last_squares)
-                for agents in quarters:
+                for agents in [front] + quarters:
                     weave(nc.scalar.copy, 0, agents, slice(0, 4))
-            if i == 4:
-                last_walker = weigh(feature("last_walker", slot(7)), last_bump, gains1[3])
             if i == 5:
                 for agents in [front] + quarters:
                     weave(nc.scalar.copy, 1, agents, slice(0, 2))
 
         early_codes = held("early_codes", [P, 2, 512], U32)
-        early_scales = held("early_scales", [P, 2, 512], U8)
+        new_page(PAGES - 1)
+        place(PAGES - 1, list4, runners[PAGES - 1])
+
+        def place_last(n):
+            nc.vector.tensor_copy(pages[PAGES - 1][:].indirect(list3[:, entries(halves[n])]), last_walkers[n][:])
+
+        place_last(0)
+        early_scales = placed("early_scales", [P, 2, 512], U8, GAINS2)
         quantise(early_codes[:].rearrange("p a c -> p (a c)"), early_scales[:].rearrange("p a c -> p (a c)"),
                  early_bf[:].rearrange("p a c -> p (a c)"))
         second_codes = held("second_codes", [P, 512], U32)
@@ -396,10 +396,10 @@ def tile_list_crowd_steering_features_kernel(
         early = [bank(n, f"y_first{n}") for n in range(4)]
         for acc, agents in zip(early, pieces):
             project(acc, agents, 0, range(4), 0)
-        place(PAGES - 1, list3, last_walker)
+        place_last(1)
 
-        late_scales[0] = placed("second_scales", [P, 512], U8, slot(7))
-        late_scales[1] = placed("w3_late_scales", [P, 2, 2, 256], U8, slot(7) + 512)
+        late_scales[0] = placed("second_scales", [P, 512], U8, GAINS2 + 2 * KIB - 448)
+        late_scales[1] = placed("w3_late_scales", [P, 2, 2, 256], U8, GAINS2 + 2 * KIB + 64)
 
         def last_style(agents):
             half, start = divmod(agents.start, HALF)
@@ -422,15 +422,10 @@ def tile_list_crowd_steering_features_kernel(
         y_scales = held("y_scales", [P, 2, T2], U8)
         y_rows = out_0.rearrange("(g p t) n -> g p t n", g=2, t=4)
 
-        def quantise_y(values, g_out, agents, on_vector):
+        def quantise_y(copy, values, g_out, agents):
             width = agents.stop - agents.start
             woven = placed(f"y_woven{g_out}_{agents.start}", [P, width, 4], BF16, PAGE + 8 * agents.start + 8 * KIB * g_out)
-            shares = ((slice(0, on_vector), nc.vector.tensor_copy), (slice(on_vector, width), nc.scalar.copy))
-            for share, copy in shares[: 1 if on_vector == width else 2]:
-                copy(
-                    woven[:, share, :].rearrange("p (n i) t -> p n t i", i=4),
-                    values[:, :, share].rearrange("p t (n i) -> p n t i", i=4),
-                )
+            copy(woven[:].rearrange("p (n i) t -> p n t i", i=4), values.rearrange("p t (n i) -> p n t i", i=4))
             quantise(y_codes[g_out][:, agents], y_scales[:, g_out, agents], woven[:].rearrange("p n t -> p (n t)"))
 
         def store_codes(g_out, agents):
@@ -468,10 +463,10 @@ def tile_list_crowd_steering_features_kernel(
         y01 = sums(0, 1, by_quarter, banks(0, 1), (0, 1), {2: (back, low), 3: (back, high)})
         y11 = sums(1, 1, by_quarter, banks(1, 1), (0, 1), {2: (back, low), 3: (back, high)})
         for values, g_out, agents in ((y00, 0, front), (y10, 1, front), (y01, 0, back)):
-            quantise_y(values[:], g_out, agents, HALF)
+            quantise_y(nc.vector.tensor_copy, values[:], g_out, agents)
             store_codes(g_out, agents)
-        quantise_y(y11[:, :, :QUARTER], 1, quarters[0], QUARTER)
-        quantise_y(y11[:, :, QUARTER:], 1, quarters[1], LAST_SHARE)
+        quantise_y(nc.vector.tensor_copy, y11[:, :, :QUARTER], 1, quarters[0])
+        quantise_y(nc.scalar.copy, y11[:, :, QUARTER:], 1, quarters[1])
         store_codes(1, back)
         for q in range(4):
             (nc.scalar, nc.sync)[q % 2].dma_start(

@@ -185,7 +185,7 @@ def tile_list_crowd_steering_features_kernel(
         def slot(n):
             return FEAT + 2 * KIB * n + (64 if n > 2 else 0)
 
-        page_bytes = {0: PAGE, 1: PAGE + 4 * KIB, 2: PAGE + 8 * KIB, 3: TAB1, 4: W1_BF, 5: W1_BF + 4 * KIB,
+        page_bytes = {0: PAGE, 1: PAGE + 4 * KIB, 2: PAGE + 8 * KIB, 3: TAB1, 4: W1_BF, 5: PAGE + 12 * KIB,
                       6: W1_BF + 8 * KIB, 7: TAB2}
         pages = {}
 
@@ -238,7 +238,7 @@ def tile_list_crowd_steering_features_kernel(
             w1_bf.append(placed(f"w1_bf{half}", [P, 2, 2048], BF16, W1_BF + 8 * KIB * half))
             for a in range(2):
                 round_weight(w1_raw[a, half], [w1_bf[half][:, a, :]])
-        for i in range(FUSED, PAGES - 1):
+        for i in (3, 5, 4, 6):
             if i in (4, 6):
                 half = i // 2 - 2
                 quantise(w1_codes[:, half, :], w1_scales[:, half, :], w1_bf[half][:].rearrange("p a c -> p (a c)"))
@@ -276,10 +276,7 @@ def tile_list_crowd_steering_features_kernel(
             bump(h, h)
             if i < PAGES - 1:
                 walkers[i] = weigh(out, h, gains1[i % 4])
-        last_walkers = []
-        for n, cols in enumerate(halves):
-            last_walkers.append(placed(f"last_walkers{n}", [P, S // 2], F32, GAINS2 + 2 * KIB * n))
-            nc.gpsimd.tensor_tensor(last_walkers[n][:], h[:, cols], gains1[3][:, cols], MULT)
+        last_bumps = h
 
         early_bf = placed("early_bf", [P, 2, 2048], BF16, RAW + 24 * KIB)
         second_bf = held("second_bf", [P, 2048], BF16)
@@ -294,7 +291,7 @@ def tile_list_crowd_steering_features_kernel(
             round_weight(load_weight("w3", w3, a, g), rounded_w3[a, g])
         styles += [load_style(i) for i in range(2, PAGES)]
 
-        z_rows0 = placed("z_rows0", [P, 2, 4, HALF], BF16, TAB2)
+        z_rows0 = [placed(f"z_rows0_{half}", [P, 4, HALF], BF16, TAB2 + 4 * KIB * half) for half in range(2)]
         z_rows1 = [placed(f"z_rows1_{pair}", [P, 2, 2, HALF], BF16, TAB0 + 4 * KIB * pair) for pair in range(2)]
         z1_first_bf = placed("z1_first_bf", [P, 2048], BF16, RAW + 4 * KIB)
         z_late_bf = placed("z_late_bf", [P, 2, 2, 1024], BF16, RAW - 4 * KIB)
@@ -311,11 +308,15 @@ def tile_list_crowd_steering_features_kernel(
 
         def z_rows(g, halves, slots):
             if g == 0:
-                return z_rows0[:, halves, slots, :]
+                return z_rows0[halves][:, slots, :]
             return z_rows1[slots.start // 2][:, halves, slots.start % 2 : slots.start % 2 + slots.stop - slots.start, :]
 
         def apply_style(i):
             g, t = divmod(i, 4)
+            if g == 0:
+                for half, agents in enumerate((front, back)):
+                    nc.gpsimd.tensor_tensor(z_rows0[half][:, t, :], pages[i][:, agents], styles[i][:, agents], MULT)
+                return
             nc.gpsimd.tensor_tensor(
                 z_rows(g, slice(0, 2), slice(t, t + 1)).rearrange("p c t n -> p c (t n)"),
                 pages[i][:].rearrange("p (c n) -> p c n", c=2),
@@ -335,6 +336,10 @@ def tile_list_crowd_steering_features_kernel(
             place(i, list3, walkers[i])
             apply_style(i)
             if i == 3:
+                last_walkers = []
+                for n, cols in enumerate(halves):
+                    last_walkers.append(placed(f"last_walkers{n}", [P, S // 2], F32, TAB1 + 2 * KIB * n))
+                    nc.gpsimd.tensor_tensor(last_walkers[n][:], last_bumps[:, cols], gains1[3][:, cols], MULT)
                 for agents in [front] + quarters:
                     weave(nc.scalar.copy, 0, agents, slice(0, 4))
             if i == 5:
@@ -349,7 +354,7 @@ def tile_list_crowd_steering_features_kernel(
             nc.vector.tensor_copy(pages[PAGES - 1][:].indirect(list3[:, entries(halves[n])]), last_walkers[n][:])
 
         place_last(0)
-        early_scales = placed("early_scales", [P, 2, 512], U8, GAINS2)
+        early_scales = placed("early_scales", [P, 2, 512], U8, TAB1)
         quantise(early_codes[:].rearrange("p a c -> p (a c)"), early_scales[:].rearrange("p a c -> p (a c)"),
                  early_bf[:].rearrange("p a c -> p (a c)"))
         second_codes = held("second_codes", [P, 512], U32)
@@ -398,8 +403,8 @@ def tile_list_crowd_steering_features_kernel(
             project(acc, agents, 0, range(4), 0)
         place_last(1)
 
-        late_scales[0] = placed("second_scales", [P, 512], U8, GAINS2 + 2 * KIB - 448)
-        late_scales[1] = placed("w3_late_scales", [P, 2, 2, 256], U8, GAINS2 + 2 * KIB + 64)
+        late_scales[0] = placed("second_scales", [P, 512], U8, TAB1 + 2 * KIB - 448)
+        late_scales[1] = placed("w3_late_scales", [P, 2, 2, 256], U8, TAB1 + 2 * KIB + 64)
 
         def last_style(agents):
             half, start = divmod(agents.start, HALF)

@@ -465,8 +465,9 @@ def tile_list_crowd_steering_features_kernel(
         first_stores = {0: (pieces[0], every), 1: (pieces[1], every), 3: (slice(QUARTER, HALF), every)}
         y00 = sums(0, 0, by_piece, early, (1,), first_stores)
         y10 = sums(1, 0, by_slot, banks(1, 0), (0, 1), {1: (front, low), 3: (front, high)})
-        y01 = sums(0, 1, by_quarter, banks(0, 1), (0, 1), {2: (back, low), 3: (back, high)})
-        y11 = sums(1, 1, by_quarter, banks(1, 1), (0, 1), {2: (back, low), 3: (back, high)})
+        quarter_stores = {1: (quarters[0], every), 3: (quarters[1], every)}
+        y01 = sums(0, 1, by_quarter, banks(0, 1), (0, 1), quarter_stores)
+        y11 = sums(1, 1, by_quarter, banks(1, 1), (0, 1), quarter_stores)
         for values, g_out, agents in ((y00, 0, front), (y10, 1, front), (y01, 0, back)):
             quantise_y(nc.vector.tensor_copy, values[:], g_out, agents)
             store_codes(g_out, agents)

@@ -185,7 +185,7 @@ def tile_list_crowd_steering_features_kernel(
         def slot(n):
             return FEAT + 2 * KIB * n + (64 if n > 2 else 0)
 
-        page_bytes = {0: PAGE, 1: PAGE + 4 * KIB, 2: PAGE + 8 * KIB, 3: TAB1, 4: W1_BF, 5: PAGE + 12 * KIB,
+        page_bytes = {0: PAGE, 1: PAGE + 4 * KIB, 2: PAGE + 8 * KIB, 3: TAB1, 4: W1_BF, 5: TAB1 + 4 * KIB,
                       6: W1_BF + 8 * KIB, 7: TAB2}
         pages = {}
 
@@ -225,11 +225,8 @@ def tile_list_crowd_steering_features_kernel(
                     pages[i][:].indirect(list4[:, entries(cols)]), h2[i][:, cols], gains2[i][:, cols], MULT
                 )
         v_words = [gather(f"v_words{a}", tab[a], list1, U32) for a in range(2)]
-        after_fused = {3: slot(2) + 64 - 2 * KIB, 4: slot(2) + 64}
-        runners = {
-            i: weigh(feature(f"runner{i}", after_fused[i]) if i in after_fused else h2[i], h2[i], gains2[i % 4])
-            for i in range(FUSED, PAGES)
-        }
+        runner_bytes = {3: slot(2) + 64 - 2 * KIB, 4: slot(2) + 64, 5: slot(3), 6: slot(4), 7: slot(5)}
+        runners = {i: weigh(feature(f"runner{i}", runner_bytes[i]), h2[i], gains2[i % 4]) for i in range(FUSED, PAGES)}
 
         w1_codes = placed("w1_codes", [P, 2, 1024], U32, W1_CODES)
         w1_scales = held("w1_scales", [P, 2, 1024], U8)
@@ -245,7 +242,7 @@ def tile_list_crowd_steering_features_kernel(
             new_page(i)
             place(i, list4, runners[i])
 
-        walker_bytes = (slot(3), slot(4), slot(0), after_fused[3], after_fused[4], slot(5), slot(6), slot(8))
+        walker_bytes = (slot(6), slot(7), slot(0), runner_bytes[3], slot(3), runner_bytes[4], slot(4), slot(8))
 
         def squares(i):
             half, t = divmod(i, 4)

@@ -23,6 +23,7 @@ HALF = T2 // 2
 KIB = 1024
 FUSED = 3
 QUARTER = T2 // 4
+LAST_SHARE = 336
 
 TAB2 = 0
 TAB0 = TAB2 + 8 * KIB
@@ -96,8 +97,8 @@ def tile_list_crowd_steering_features_kernel(
                 nc.sync.dma_start(gains[32 * q : 32 * q + 32], src.rearrange("(u t) j -> u t j", t=4)[:, t0 : t0 + count, :])
             return [gains[:, t, :] for t in range(count)]
 
-        def load_weight(name, src, a, half):
-            raw = placed(f"{name}_raw{a}{half}", [P, 4, 512], F32, RAW + 8 * KIB * (2 * half + a))
+        def load_weight(name, src, a, half, offset):
+            raw = placed(f"{name}_raw{a}{half}", [P, 4, 512], F32, offset)
             rows = src[512 * a : 512 * (a + 1), 512 * half : 512 * (half + 1)]
             nc.sync.dma_start(raw[:], rows.rearrange("(p j) c -> p j c", j=4))
             return raw
@@ -141,7 +142,8 @@ def tile_list_crowd_steering_features_kernel(
         list4 = load_list("list4", offs4)
         gains2 = gains2 + load_gains(placed("gains2_rest", [P, 3, S], F32, GAINS2 + 2 * KIB), wg2, 1)
         tab = [load_words("tab0", TAB0, tab_words[0]), load_words("tab1", TAB1, tab_words[1])]
-        w1_raw = {(a, half): load_weight("w1", w1, a, half) for half in range(2) for a in range(2)}
+        w1_bytes = {(0, 0): RAW, (1, 0): RAW + 8 * KIB, (0, 1): RAW + 16 * KIB, (1, 1): STYLE + 16 * KIB}
+        w1_raw = {part: load_weight("w1", w1, *part, offset) for part, offset in w1_bytes.items()}
         centre = held("centre", [P, 2, 4], F32)
         nc.sync.dma_start(centre[:], ctr.rearrange("(g p t) -> p g t", g=2, t=4))
         list3 = load_list("list3", offs3)
@@ -186,7 +188,7 @@ def tile_list_crowd_steering_features_kernel(
             return FEAT + 2 * KIB * n + (64 if n > 2 else 0)
 
         page_bytes = {0: PAGE, 1: PAGE + 4 * KIB, 2: PAGE + 8 * KIB, 3: TAB1, 4: W1_BF, 5: TAB1 + 4 * KIB,
-                      6: W1_BF + 8 * KIB, 7: TAB2}
+                      6: W1_BF + 4 * KIB, 7: TAB2}
         pages = {}
 
         def new_page(i):
@@ -229,16 +231,16 @@ def tile_list_crowd_steering_features_kernel(
         runners = {i: weigh(feature(f"runner{i}", runner_bytes[i]), h2[i], gains2[i % 4]) for i in range(FUSED, PAGES)}
 
         w1_codes = placed("w1_codes", [P, 2, 1024], U32, W1_CODES)
-        w1_scales = held("w1_scales", [P, 2, 1024], U8)
         w1_bf = []
         for half in range(2):
             w1_bf.append(placed(f"w1_bf{half}", [P, 2, 2048], BF16, W1_BF + 8 * KIB * half))
             for a in range(2):
                 round_weight(w1_raw[a, half], [w1_bf[half][:, a, :]])
+        w1_scales = placed("w1_scales", [P, 2, 1024], U8, w1_bytes[1, 1])
         for i in (3, 5, 4, 6):
-            if i in (4, 6):
-                half = i // 2 - 2
-                quantise(w1_codes[:, half, :], w1_scales[:, half, :], w1_bf[half][:].rearrange("p a c -> p (a c)"))
+            if i == 4:
+                for half in range(2):
+                    quantise(w1_codes[:, half, :], w1_scales[:, half, :], w1_bf[half][:].rearrange("p a c -> p (a c)"))
             new_page(i)
             place(i, list4, runners[i])
 
@@ -269,23 +271,22 @@ def tile_list_crowd_steering_features_kernel(
         walkers = {}
         for i in range(PAGES):
             h = squares(i)
-            out = feature("walker0", W1_BF + 12 * KIB) if i == 0 else h
             bump(h, h)
             if i < PAGES - 1:
-                walkers[i] = weigh(out, h, gains1[i % 4])
+                walkers[i] = weigh(h, h, gains1[i % 4])
         last_bumps = h
 
         early_bf = placed("early_bf", [P, 2, 2048], BF16, RAW + 24 * KIB)
         second_bf = held("second_bf", [P, 2048], BF16)
-        w3_late_bf = held("w3_late_bf", [P, 2, 2, 1024], BF16)
+        w3_late_bf = held("w3_late_bf", [P, 2, 2048], BF16)
         rounded_w3 = {
             (0, 0): [early_bf[:, 0, :]],
             (1, 0): [second_bf[:]],
-            (0, 1): [w3_late_bf[:, pair, 0, :] for pair in range(2)],
-            (1, 1): [w3_late_bf[:, pair, 1, :] for pair in range(2)],
+            (0, 1): [w3_late_bf[:, 0, :]],
+            (1, 1): [w3_late_bf[:, 1, :]],
         }
         for a, g in ((1, 0), (0, 1), (1, 1), (0, 0)):
-            round_weight(load_weight("w3", w3, a, g), rounded_w3[a, g])
+            round_weight(load_weight("w3", w3, a, g, RAW + 8 * KIB * (2 * g + a)), rounded_w3[a, g])
         styles += [load_style(i) for i in range(2, PAGES)]
 
         z_rows0 = [placed(f"z_rows0_{half}", [P, 4, HALF], BF16, TAB2 + 4 * KIB * half) for half in range(2)]
@@ -333,10 +334,7 @@ def tile_list_crowd_steering_features_kernel(
             place(i, list3, walkers[i])
             apply_style(i)
             if i == 3:
-                last_walkers = []
-                for n, cols in enumerate(halves):
-                    last_walkers.append(placed(f"last_walkers{n}", [P, S // 2], F32, TAB1 + 2 * KIB * n))
-                    nc.gpsimd.tensor_tensor(last_walkers[n][:], last_bumps[:, cols], gains1[3][:, cols], MULT)
+                last_walker = weigh(feature("last_walker", TAB1), last_bumps, gains1[3])
                 for agents in [front] + quarters:
                     weave(nc.scalar.copy, 0, agents, slice(0, 4))
             if i == 5:
@@ -346,16 +344,11 @@ def tile_list_crowd_steering_features_kernel(
         early_codes = held("early_codes", [P, 2, 512], U32)
         new_page(PAGES - 1)
         place(PAGES - 1, list4, runners[PAGES - 1])
-
-        def place_last(n):
-            nc.vector.tensor_copy(pages[PAGES - 1][:].indirect(list3[:, entries(halves[n])]), last_walkers[n][:])
-
-        place_last(0)
-        early_scales = placed("early_scales", [P, 2, 512], U8, TAB1)
+        early_scales = held("early_scales", [P, 2, 512], U8)
         quantise(early_codes[:].rearrange("p a c -> p (a c)"), early_scales[:].rearrange("p a c -> p (a c)"),
                  early_bf[:].rearrange("p a c -> p (a c)"))
         second_codes = held("second_codes", [P, 512], U32)
-        w3_late_codes = held("w3_late_codes", [P, 2, 2, 256], U32)
+        w3_late_codes = held("w3_late_codes", [P, 2, 512], U32)
         z1_first_codes = held("z1_first_codes", [P, 512], U32)
         z1_first_scales = held("z1_first_scales", [P, 512], U8)
         z_late_codes = held("z_late_codes", [P, 2, 2, QUARTER], U32)
@@ -363,10 +356,9 @@ def tile_list_crowd_steering_features_kernel(
         late_scales = {}
 
         def w3_operand(a, g_out, t):
-            if g_out == 1:
-                cols = slice(P * (t % 2), P * (t % 2 + 1))
-                return w3_late_codes[:, t // 2, a, cols], late_scales[1][:, t // 2, a, cols]
             cols = slice(P * t, P * (t + 1))
+            if g_out == 1:
+                return w3_late_codes[:, a, cols], late_scales[1][:, a, cols]
             if a == 0:
                 return early_codes[:, 0, cols], early_scales[:, 0, cols]
             return second_codes[:, cols], late_scales[0][:, cols]
@@ -379,10 +371,11 @@ def tile_list_crowd_steering_features_kernel(
                 return early_codes[:, 1, agents], early_scales[:, 1, agents]
             return z1_first_codes[:, agents], z1_first_scales[:, agents]
 
-        def project(acc, agents, g_out, slots, a):
-            z_codes, z_scales = z_operand(a, agents)
-            width = agents.stop - agents.start
-            for e, t in enumerate(slots):
+        def project(acc, runs, g_out, slots, a):
+            cells = [(t, agents) for t in range(slots.start, slots.stop) for agents in runs]
+            width = 512 // len(cells)
+            for e, (t, agents) in enumerate(cells):
+                z_codes, z_scales = z_operand(a, agents)
                 codes, scales = w3_operand(a, g_out, t)
                 nc.tensor.matmul_mx(
                     acc[:, width * e : width * (e + 1)],
@@ -391,17 +384,19 @@ def tile_list_crowd_steering_features_kernel(
                     rhs=z_codes.bitcast(FP8X4),
                     rhs_scale=z_scales,
                     start=(a == 0 and e == 0),
-                    stop=(a == 1 and e == len(slots) - 1),
+                    stop=(a == 1 and e == len(cells) - 1),
                 )
 
-        pieces = [slice(P * n, P * (n + 1)) for n in range(4)]
+        every, low, high = slice(0, 4), slice(0, 2), slice(2, 4)
+        pieces = [slice(0, P), slice(P, QUARTER), slice(QUARTER, HALF)]
+        by_piece = [([pieces[0]], every), ([pieces[1]], every), ([pieces[2]], low), ([pieces[2]], high)]
         early = [bank(n, f"y_first{n}") for n in range(4)]
-        for acc, agents in zip(early, pieces):
-            project(acc, agents, 0, range(4), 0)
-        place_last(1)
+        for acc, (runs, slots) in zip(early, by_piece):
+            project(acc, runs, 0, slots, 0)
+        place(PAGES - 1, list3, last_walker)
 
-        late_scales[0] = placed("second_scales", [P, 512], U8, TAB1 + 2 * KIB - 448)
-        late_scales[1] = placed("w3_late_scales", [P, 2, 2, 256], U8, TAB1 + 2 * KIB + 64)
+        late_scales[0] = placed("second_scales", [P, 512], U8, TAB1)
+        late_scales[1] = placed("w3_late_scales", [P, 2, 512], U8, TAB1 + 512)
 
         def last_style(agents):
             half, start = divmod(agents.start, HALF)
@@ -414,8 +409,7 @@ def tile_list_crowd_steering_features_kernel(
             if n == 0:
                 quantise(second_codes[:], late_scales[0][:], second_bf[:])
             quantise(z1_first_codes[:, agents], z1_first_scales[:, agents], z_woven(1, agents))
-        for pair in range(2):
-            quantise(*(tile[:, pair].rearrange("p a c -> p (a c)") for tile in (w3_late_codes, late_scales[1], w3_late_bf)))
+        quantise(*(tile[:].rearrange("p a c -> p (a c)") for tile in (w3_late_codes, late_scales[1], w3_late_bf)))
         for n, agents in enumerate(quarters):
             last_style(agents)
             quantise(*(tile[:, n].rearrange("p a c -> p (a c)") for tile in (z_late_codes, z_late_scales, z_late_bf)))
@@ -424,10 +418,15 @@ def tile_list_crowd_steering_features_kernel(
         y_scales = held("y_scales", [P, 2, T2], U8)
         y_rows = out_0.rearrange("(g p t) n -> g p t n", g=2, t=4)
 
-        def quantise_y(copy, values, g_out, agents):
+        def quantise_y(values, g_out, agents, on_vector):
             width = agents.stop - agents.start
             woven = placed(f"y_woven{g_out}_{agents.start}", [P, width, 4], BF16, PAGE + 8 * agents.start + 8 * KIB * g_out)
-            copy(woven[:].rearrange("p (n i) t -> p n t i", i=4), values.rearrange("p t (n i) -> p n t i", i=4))
+            shares = ((slice(0, on_vector), nc.vector.tensor_copy), (slice(on_vector, width), nc.scalar.copy))
+            for share, copy in shares[: 1 if on_vector == width else 2]:
+                copy(
+                    woven[:, share, :].rearrange("p (n i) t -> p n t i", i=4),
+                    values[:, :, share].rearrange("p t (n i) -> p n t i", i=4),
+                )
             quantise(y_codes[g_out][:, agents], y_scales[:, g_out, agents], woven[:].rearrange("p n t -> p (n t)"))
 
         def store_codes(g_out, agents):
@@ -442,9 +441,10 @@ def tile_list_crowd_steering_features_kernel(
             def local(agents):
                 return slice(agents.start - HALF * half, agents.stop - HALF * half)
 
-            for n, (acc, (agents, slots)) in enumerate(zip(banks, layout)):
+            for n, (acc, (runs, slots)) in enumerate(zip(banks, layout)):
                 for a in passes:
-                    project(acc, agents, g_out, range(slots.start, slots.stop), a)
+                    project(acc, runs, g_out, slots, a)
+                agents = slice(runs[0].start, runs[-1].stop)
                 width = agents.stop - agents.start
                 nc.scalar.copy(rows[:, slots, local(agents)], acc[:].rearrange("p (t n) -> p t n", n=width))
                 if n in stores:
@@ -455,21 +455,19 @@ def tile_list_crowd_steering_features_kernel(
         def banks(g_out, half):
             return [bank(4 * g_out + n, f"y{g_out}{half}{n}") for n in range(4)]
 
-        every, low, high = slice(0, 4), slice(0, 2), slice(2, 4)
-        by_piece = [(agents, every) for agents in pieces]
-        by_slot = [(front, slice(t, t + 1)) for t in range(4)]
-        by_quarter = [(agents, slots) for agents in quarters for slots in (low, high)]
-        first_stores = {0: (pieces[0], every), 1: (pieces[1], every), 3: (slice(QUARTER, HALF), every)}
+        by_slot = [([front], slice(t, t + 1)) for t in range(4)]
+        by_quarter = [([agents], slots) for agents in quarters for slots in (low, high)]
+        last_by_slot = [(quarters, slice(t, t + 1)) for t in range(4)]
+        first_stores = {0: (pieces[0], every), 1: (pieces[1], every), 3: (pieces[2], every)}
         y00 = sums(0, 0, by_piece, early, (1,), first_stores)
         y10 = sums(1, 0, by_slot, banks(1, 0), (0, 1), {1: (front, low), 3: (front, high)})
         quarter_stores = {1: (quarters[0], every), 3: (quarters[1], every)}
         y01 = sums(0, 1, by_quarter, banks(0, 1), (0, 1), quarter_stores)
-        y11 = sums(1, 1, by_quarter, banks(1, 1), (0, 1), quarter_stores)
+        y11 = sums(1, 1, last_by_slot, banks(1, 1), (0, 1), {1: (back, low), 3: (back, high)})
         for values, g_out, agents in ((y00, 0, front), (y10, 1, front), (y01, 0, back)):
-            quantise_y(nc.vector.tensor_copy, values[:], g_out, agents)
+            quantise_y(values[:], g_out, agents, HALF)
             store_codes(g_out, agents)
-        quantise_y(nc.vector.tensor_copy, y11[:, :, :QUARTER], 1, quarters[0])
-        quantise_y(nc.scalar.copy, y11[:, :, QUARTER:], 1, quarters[1])
+        quantise_y(y11[:], 1, back, LAST_SHARE)
         store_codes(1, back)
         for q in range(4):
             (nc.scalar, nc.sync)[q % 2].dma_start(

@@ -23,7 +23,7 @@ HALF = T2 // 2
 KIB = 1024
 FUSED = 3
 QUARTER = T2 // 4
-LAST_SHARE = 336
+LAST_SHARE = 256
 
 TAB2 = 0
 TAB0 = TAB2 + 8 * KIB
@@ -97,8 +97,8 @@ def tile_list_crowd_steering_features_kernel(
                 nc.sync.dma_start(gains[32 * q : 32 * q + 32], src.rearrange("(u t) j -> u t j", t=4)[:, t0 : t0 + count, :])
             return [gains[:, t, :] for t in range(count)]
 
-        def load_weight(name, src, a, half, offset):
-            raw = placed(f"{name}_raw{a}{half}", [P, 4, 512], F32, offset)
+        def load_weight(name, src, a, half):
+            raw = placed(f"{name}_raw{a}{half}", [P, 4, 512], F32, RAW + 8 * KIB * (2 * half + a))
             rows = src[512 * a : 512 * (a + 1), 512 * half : 512 * (half + 1)]
             nc.sync.dma_start(raw[:], rows.rearrange("(p j) c -> p j c", j=4))
             return raw
@@ -142,8 +142,7 @@ def tile_list_crowd_steering_features_kernel(
         list4 = load_list("list4", offs4)
         gains2 = gains2 + load_gains(placed("gains2_rest", [P, 3, S], F32, GAINS2 + 2 * KIB), wg2, 1)
         tab = [load_words("tab0", TAB0, tab_words[0]), load_words("tab1", TAB1, tab_words[1])]
-        w1_bytes = {(0, 0): RAW, (1, 0): RAW + 8 * KIB, (0, 1): RAW + 16 * KIB, (1, 1): STYLE + 16 * KIB}
-        w1_raw = {part: load_weight("w1", w1, *part, offset) for part, offset in w1_bytes.items()}
+        w1_raw = {(a, half): load_weight("w1", w1, a, half) for half in range(2) for a in range(2)}
         centre = held("centre", [P, 2, 4], F32)
         nc.sync.dma_start(centre[:], ctr.rearrange("(g p t) -> p g t", g=2, t=4))
         list3 = load_list("list3", offs3)
@@ -187,8 +186,8 @@ def tile_list_crowd_steering_features_kernel(
         def slot(n):
             return FEAT + 2 * KIB * n + (64 if n > 2 else 0)
 
-        page_bytes = {0: PAGE, 1: PAGE + 4 * KIB, 2: PAGE + 8 * KIB, 3: TAB1, 4: W1_BF, 5: TAB1 + 4 * KIB,
-                      6: W1_BF + 4 * KIB, 7: TAB2}
+        page_bytes = {0: PAGE, 1: PAGE + 4 * KIB, 2: PAGE + 8 * KIB, 3: TAB1, 4: W1_BF + 8 * KIB, 5: W1_BF,
+                      6: W1_BF + 12 * KIB, 7: TAB2}
         pages = {}
 
         def new_page(i):
@@ -236,11 +235,11 @@ def tile_list_crowd_steering_features_kernel(
             w1_bf.append(placed(f"w1_bf{half}", [P, 2, 2048], BF16, W1_BF + 8 * KIB * half))
             for a in range(2):
                 round_weight(w1_raw[a, half], [w1_bf[half][:, a, :]])
-        w1_scales = placed("w1_scales", [P, 2, 1024], U8, w1_bytes[1, 1])
+        w1_scales = held("w1_scales", [P, 2, 1024], U8)
         for i in (3, 5, 4, 6):
-            if i == 4:
-                for half in range(2):
-                    quantise(w1_codes[:, half, :], w1_scales[:, half, :], w1_bf[half][:].rearrange("p a c -> p (a c)"))
+            if i in (5, 4):
+                half = 5 - i
+                quantise(w1_codes[:, half, :], w1_scales[:, half, :], w1_bf[half][:].rearrange("p a c -> p (a c)"))
             new_page(i)
             place(i, list4, runners[i])
 
@@ -285,8 +284,9 @@ def tile_list_crowd_steering_features_kernel(
             (0, 1): [w3_late_bf[:, 0, :]],
             (1, 1): [w3_late_bf[:, 1, :]],
         }
-        for a, g in ((1, 0), (0, 1), (1, 1), (0, 0)):
-            round_weight(load_weight("w3", w3, a, g, RAW + 8 * KIB * (2 * g + a)), rounded_w3[a, g])
+        w3_raw = {(a, g): load_weight("w3", w3, a, g) for g in range(2) for a in range(2)}
+        for part in ((1, 0), (0, 1), (1, 1), (0, 0)):
+            round_weight(w3_raw[part], rounded_w3[part])
         styles += [load_style(i) for i in range(2, PAGES)]
 
         z_rows0 = [placed(f"z_rows0_{half}", [P, 4, HALF], BF16, TAB2 + 4 * KIB * half) for half in range(2)]
@@ -334,7 +334,6 @@ def tile_list_crowd_steering_features_kernel(
             place(i, list3, walkers[i])
             apply_style(i)
             if i == 3:
-                last_walker = weigh(feature("last_walker", TAB1), last_bumps, gains1[3])
                 for agents in [front] + quarters:
                     weave(nc.scalar.copy, 0, agents, slice(0, 4))
             if i == 5:
@@ -393,25 +392,26 @@ def tile_list_crowd_steering_features_kernel(
         early = [bank(n, f"y_first{n}") for n in range(4)]
         for acc, (runs, slots) in zip(early, by_piece):
             project(acc, runs, 0, slots, 0)
-        place(PAGES - 1, list3, last_walker)
+        nc.vector.tensor_tensor(pages[PAGES - 1][:].indirect(list3[:]), last_bumps[:], gains1[3], MULT)
 
-        late_scales[0] = placed("second_scales", [P, 512], U8, TAB1)
-        late_scales[1] = placed("w3_late_scales", [P, 2, 512], U8, TAB1 + 512)
+        late_scales[0] = placed("second_scales", [P, 512], U8, slot(8))
+        late_scales[1] = placed("w3_late_scales", [P, 2, 512], U8, slot(8) + 512)
 
         def last_style(agents):
             half, start = divmod(agents.start, HALF)
             cols = slice(start, start + agents.stop - agents.start)
             nc.vector.tensor_tensor(z_rows1[1][:, half, 1, cols], pages[7][:, agents], styles[7][:, agents], MULT)
-            weave(nc.vector.tensor_copy, 1, agents, slice(2, 4))
 
         for n, agents in enumerate(pieces):
             last_style(agents)
+            weave(nc.vector.tensor_copy, 1, agents, high)
             if n == 0:
                 quantise(second_codes[:], late_scales[0][:], second_bf[:])
             quantise(z1_first_codes[:, agents], z1_first_scales[:, agents], z_woven(1, agents))
+        last_style(back)
         quantise(*(tile[:].rearrange("p a c -> p (a c)") for tile in (w3_late_codes, late_scales[1], w3_late_bf)))
         for n, agents in enumerate(quarters):
-            last_style(agents)
+            weave(nc.vector.tensor_copy, 1, agents, high)
             quantise(*(tile[:, n].rearrange("p a c -> p (a c)") for tile in (z_late_codes, z_late_scales, z_late_bf)))
 
         y_codes = [held(f"y_codes{g}", [P, T2], U32) for g in range(2)]

@@ -97,8 +97,8 @@ def tile_list_crowd_steering_features_kernel(
                 nc.sync.dma_start(gains[32 * q : 32 * q + 32], src.rearrange("(u t) j -> u t j", t=4)[:, t0 : t0 + count, :])
             return [gains[:, t, :] for t in range(count)]
 
-        def load_weight(name, src, a, half):
-            raw = placed(f"{name}_raw{a}{half}", [P, 4, 512], F32, RAW + 8 * KIB * (2 * half + a))
+        def load_weight(name, src, a, half, offset):
+            raw = placed(f"{name}_raw{a}{half}", [P, 4, 512], F32, offset)
             rows = src[512 * a : 512 * (a + 1), 512 * half : 512 * (half + 1)]
             nc.sync.dma_start(raw[:], rows.rearrange("(p j) c -> p j c", j=4))
             return raw
@@ -142,7 +142,8 @@ def tile_list_crowd_steering_features_kernel(
         list4 = load_list("list4", offs4)
         gains2 = gains2 + load_gains(placed("gains2_rest", [P, 3, S], F32, GAINS2 + 2 * KIB), wg2, 1)
         tab = [load_words("tab0", TAB0, tab_words[0]), load_words("tab1", TAB1, tab_words[1])]
-        w1_raw = {(a, half): load_weight("w1", w1, a, half) for half in range(2) for a in range(2)}
+        w1_bytes = {(a, half): (RAW, STYLE + 8 * KIB)[a] + 8 * KIB * half for half in range(2) for a in range(2)}
+        w1_raw = {part: load_weight("w1", w1, *part, offset) for part, offset in w1_bytes.items()}
         centre = held("centre", [P, 2, 4], F32)
         nc.sync.dma_start(centre[:], ctr.rearrange("(g p t) -> p g t", g=2, t=4))
         list3 = load_list("list3", offs3)
@@ -187,7 +188,7 @@ def tile_list_crowd_steering_features_kernel(
             return FEAT + 2 * KIB * n + (64 if n > 2 else 0)
 
         page_bytes = {0: PAGE, 1: PAGE + 4 * KIB, 2: PAGE + 8 * KIB, 3: TAB1, 4: W1_BF + 8 * KIB, 5: W1_BF,
-                      6: W1_BF + 12 * KIB, 7: TAB2}
+                      6: W1_BF + 12 * KIB, 7: STYLE + 12 * KIB}
         pages = {}
 
         def new_page(i):
@@ -226,24 +227,37 @@ def tile_list_crowd_steering_features_kernel(
                     pages[i][:].indirect(list4[:, entries(cols)]), h2[i][:, cols], gains2[i][:, cols], MULT
                 )
         v_words = [gather(f"v_words{a}", tab[a], list1, U32) for a in range(2)]
-        runner_bytes = {3: slot(2) + 64 - 2 * KIB, 4: slot(2) + 64, 5: slot(3), 6: slot(4), 7: slot(5)}
-        runners = {i: weigh(feature(f"runner{i}", runner_bytes[i]), h2[i], gains2[i % 4]) for i in range(FUSED, PAGES)}
+        runner_bytes = {3: slot(2) + 64 - 2 * KIB, 5: TAB1 + 4 * KIB, 4: TAB1 + 6 * KIB, 6: W1_BF + 4 * KIB, 7: W1_BF + 6 * KIB}
+        runners = {}
+
+        def weigh_runners(indices):
+            for i in indices:
+                runners[i] = weigh(feature(f"runner{i}", runner_bytes[i]), h2[i], gains2[i % 4])
+
+        weigh_runners((3, 5, 4))
 
         w1_codes = placed("w1_codes", [P, 2, 1024], U32, W1_CODES)
-        w1_bf = []
+        w1_bf = {}
         for half in range(2):
-            w1_bf.append(placed(f"w1_bf{half}", [P, 2, 2048], BF16, W1_BF + 8 * KIB * half))
             for a in range(2):
-                round_weight(w1_raw[a, half], [w1_bf[half][:, a, :]])
-        w1_scales = held("w1_scales", [P, 2, 1024], U8)
+                w1_bf[a, half] = placed(f"w1_bf{a}{half}", [P, 2048], BF16, W1_BF + 4 * KIB * (2 * half + a))
+                round_weight(w1_raw[a, half], [w1_bf[a, half][:]])
+        w1_scales = {}
         for i in (3, 5, 4, 6):
             if i in (5, 4):
                 half = 5 - i
-                quantise(w1_codes[:, half, :], w1_scales[:, half, :], w1_bf[half][:].rearrange("p a c -> p (a c)"))
+                for a in range(2):
+                    cols = slice(512 * a, 512 * (a + 1))
+                    name = f"w1_scales{a}{half}"
+                    w1_scales[a, half] = held(name, [P, 512], U8) if a else placed(name, [P, 512], U8, w1_bytes[1, half])
+                    quantise(w1_codes[:, half, cols], w1_scales[a, half][:], w1_bf[a, half][:])
+            if i == 5:
+                weigh_runners((6, 7))
             new_page(i)
             place(i, list4, runners[i])
 
-        walker_bytes = (slot(6), slot(7), slot(0), runner_bytes[3], slot(3), runner_bytes[4], slot(4), slot(8))
+        walker_bytes = (slot(6), slot(7), slot(0), slot(3), slot(4), slot(5), slot(1), slot(8))
+        weighed_bytes = {2: runner_bytes[4], 3: walker_bytes[2], 4: runner_bytes[6], 5: walker_bytes[4]}
 
         def squares(i):
             half, t = divmod(i, 4)
@@ -254,7 +268,7 @@ def tile_list_crowd_steering_features_kernel(
                 nc.tensor.matmul_mx(
                     acc[:],
                     lhsT=w1_codes[:, half, cols].bitcast(FP8X4),
-                    lhsT_scale=w1_scales[:, half, cols],
+                    lhsT_scale=w1_scales[a, half][:, P * t : P * (t + 1)],
                     rhs=v_words[a][:].bitcast(FP8X4),
                     rhs_scale=v_scales[4 * a : P, :],
                     start=(a == 0),
@@ -267,13 +281,14 @@ def tile_list_crowd_steering_features_kernel(
             nc.scalar.activation(out[:], h[:], ACT.Exp, scale=-1.0)
             return out
 
-        walkers = {}
+        walkers, bumps = {}, {}
         for i in range(PAGES):
-            h = squares(i)
-            bump(h, h)
+            bumps[i] = squares(i)
             if i < PAGES - 1:
-                walkers[i] = weigh(h, h, gains1[i % 4])
-        last_bumps = h
+                bump(bumps[i], bumps[i])
+            if i < 6:
+                out = feature(f"walker{i}", weighed_bytes[i]) if i in weighed_bytes else bumps[i]
+                walkers[i] = weigh(out, bumps[i], gains1[i % 4])
 
         early_bf = placed("early_bf", [P, 2, 2048], BF16, RAW + 24 * KIB)
         second_bf = held("second_bf", [P, 2048], BF16)
@@ -284,15 +299,15 @@ def tile_list_crowd_steering_features_kernel(
             (0, 1): [w3_late_bf[:, 0, :]],
             (1, 1): [w3_late_bf[:, 1, :]],
         }
-        w3_raw = {(a, g): load_weight("w3", w3, a, g) for g in range(2) for a in range(2)}
+        w3_raw = {(a, g): load_weight("w3", w3, a, g, RAW + 8 * KIB * (2 * g + a)) for g in range(2) for a in range(2)}
         for part in ((1, 0), (0, 1), (1, 1), (0, 0)):
             round_weight(w3_raw[part], rounded_w3[part])
         styles += [load_style(i) for i in range(2, PAGES)]
 
-        z_rows0 = [placed(f"z_rows0_{half}", [P, 4, HALF], BF16, TAB2 + 4 * KIB * half) for half in range(2)]
+        z_rows0 = placed("z_rows0", [P, 2, 4, HALF], BF16, TAB2)
         z_rows1 = [placed(f"z_rows1_{pair}", [P, 2, 2, HALF], BF16, TAB0 + 4 * KIB * pair) for pair in range(2)]
-        z1_first_bf = placed("z1_first_bf", [P, 2048], BF16, RAW + 4 * KIB)
-        z_late_bf = placed("z_late_bf", [P, 2, 2, 1024], BF16, RAW - 4 * KIB)
+        z1_first_bf = placed("z1_first_bf", [P, 2048], BF16, RAW + 2 * KIB)
+        z_late_bf = placed("z_late_bf", [P, 2, 2, 1024], BF16, RAW - 6 * KIB)
         front, back = slice(0, HALF), slice(HALF, T2)
         quarters = [slice(HALF + QUARTER * n, HALF + QUARTER * (n + 1)) for n in range(2)]
 
@@ -306,21 +321,18 @@ def tile_list_crowd_steering_features_kernel(
 
         def z_rows(g, halves, slots):
             if g == 0:
-                return z_rows0[halves][:, slots, :]
+                return z_rows0[:, halves, slots, :]
             return z_rows1[slots.start // 2][:, halves, slots.start % 2 : slots.start % 2 + slots.stop - slots.start, :]
 
         def apply_style(i):
             g, t = divmod(i, 4)
-            if g == 0:
-                for half, agents in enumerate((front, back)):
-                    nc.gpsimd.tensor_tensor(z_rows0[half][:, t, :], pages[i][:, agents], styles[i][:, agents], MULT)
-                return
-            nc.gpsimd.tensor_tensor(
-                z_rows(g, slice(0, 2), slice(t, t + 1)).rearrange("p c t n -> p c (t n)"),
-                pages[i][:].rearrange("p (c n) -> p c n", c=2),
-                styles[i][:].rearrange("p (c n) -> p c n", c=2),
-                MULT,
-            )
+            for parts in (slice(0, 1), slice(1, 2)) if i == PAGES - 2 else (slice(0, 2),):
+                nc.gpsimd.tensor_tensor(
+                    z_rows(g, parts, slice(t, t + 1)).rearrange("p c t n -> p c (t n)"),
+                    pages[i][:].rearrange("p (c n) -> p c n", c=2)[:, parts, :],
+                    styles[i][:].rearrange("p (c n) -> p c n", c=2)[:, parts, :],
+                    MULT,
+                )
 
         def weave(copy, g, agents, slots):
             half, start = divmod(agents.start, HALF)
@@ -333,17 +345,21 @@ def tile_list_crowd_steering_features_kernel(
         for i in range(PAGES - 1):
             place(i, list3, walkers[i])
             apply_style(i)
+            if i == 0:
+                walkers[6] = weigh(feature("walker6", STYLE), bumps[6], gains1[2])
             if i == 3:
-                for agents in [front] + quarters:
+                weave(nc.scalar.copy, 0, front, slice(0, 4))
+                for agents in quarters:
                     weave(nc.scalar.copy, 0, agents, slice(0, 4))
             if i == 5:
+                last_bumps = bump(feature("last_bumps", page_bytes[5]), bumps[PAGES - 1])
                 for agents in [front] + quarters:
                     weave(nc.scalar.copy, 1, agents, slice(0, 2))
 
         early_codes = held("early_codes", [P, 2, 512], U32)
         new_page(PAGES - 1)
         place(PAGES - 1, list4, runners[PAGES - 1])
-        early_scales = held("early_scales", [P, 2, 512], U8)
+        early_scales = placed("early_scales", [P, 2, 512], U8, page_bytes[5] + 2 * KIB)
         quantise(early_codes[:].rearrange("p a c -> p (a c)"), early_scales[:].rearrange("p a c -> p (a c)"),
                  early_bf[:].rearrange("p a c -> p (a c)"))
         second_codes = held("second_codes", [P, 512], U32)
@@ -394,8 +410,7 @@ def tile_list_crowd_steering_features_kernel(
             project(acc, runs, 0, slots, 0)
         nc.vector.tensor_tensor(pages[PAGES - 1][:].indirect(list3[:]), last_bumps[:], gains1[3], MULT)
 
-        late_scales[0] = placed("second_scales", [P, 512], U8, slot(8))
-        late_scales[1] = placed("w3_late_scales", [P, 2, 512], U8, slot(8) + 512)
+        late_scales[0] = placed("second_scales", [P, 512], U8, page_bytes[5])
 
         def last_style(agents):
             half, start = divmod(agents.start, HALF)
@@ -409,6 +424,7 @@ def tile_list_crowd_steering_features_kernel(
                 quantise(second_codes[:], late_scales[0][:], second_bf[:])
             quantise(z1_first_codes[:, agents], z1_first_scales[:, agents], z_woven(1, agents))
         last_style(back)
+        late_scales[1] = placed("w3_late_scales", [P, 2, 512], U8, page_bytes[5] + 512)
         quantise(*(tile[:].rearrange("p a c -> p (a c)") for tile in (w3_late_codes, late_scales[1], w3_late_bf)))
         for n, agents in enumerate(quarters):
             weave(nc.vector.tensor_copy, 1, agents, high)

@@ -33,7 +33,7 @@ RAW = GAINS2 + 8 * KIB
 W1_BF = RAW + 32 * KIB
 W1_CODES = W1_BF + 16 * KIB
 FEAT = W1_CODES + 8 * KIB
-STYLE = FEAT + 18 * KIB + 64
+STYLE = FEAT + 18 * KIB
 PAGE = STYLE + 24 * KIB
 
 
@@ -185,9 +185,9 @@ def tile_list_crowd_steering_features_kernel(
             return placed(name, [P, S], F32, offset)
 
         def slot(n):
-            return FEAT + 2 * KIB * n + (64 if n > 2 else 0)
+            return FEAT + 2 * KIB * n
 
-        page_bytes = {0: PAGE, 1: PAGE + 4 * KIB, 2: PAGE + 8 * KIB, 3: TAB1, 4: W1_BF + 8 * KIB, 5: W1_BF,
+        page_bytes = {0: PAGE, 1: PAGE + 4 * KIB, 2: TAB1, 3: TAB1 + 4 * KIB, 4: W1_BF + 8 * KIB, 5: W1_BF,
                       6: W1_BF + 12 * KIB, 7: STYLE + 12 * KIB}
         pages = {}
 
@@ -221,13 +221,14 @@ def tile_list_crowd_steering_features_kernel(
 
         h2 = [cosines(i, halves if i == 0 else whole) for i in range(PAGES)]
         for i in range(FUSED):
+            if i == FUSED - 1:
+                v_words = [gather(f"v_words{a}", tab[a], list1, U32) for a in range(2)]
             new_page(i)
             for cols in halves if i == 0 else whole:
                 nc.vector.tensor_tensor(
                     pages[i][:].indirect(list4[:, entries(cols)]), h2[i][:, cols], gains2[i][:, cols], MULT
                 )
-        v_words = [gather(f"v_words{a}", tab[a], list1, U32) for a in range(2)]
-        runner_bytes = {3: slot(2) + 64 - 2 * KIB, 5: TAB1 + 4 * KIB, 4: TAB1 + 6 * KIB, 6: W1_BF + 4 * KIB, 7: W1_BF + 6 * KIB}
+        runner_bytes = {3: slot(1), 5: slot(2), 4: slot(5), 6: W1_BF + 4 * KIB, 7: W1_BF + 6 * KIB}
         runners = {}
 
         def weigh_runners(indices):
@@ -256,7 +257,7 @@ def tile_list_crowd_steering_features_kernel(
             new_page(i)
             place(i, list4, runners[i])
 
-        walker_bytes = (slot(6), slot(7), slot(0), slot(3), slot(4), slot(5), slot(1), slot(8))
+        walker_bytes = (slot(6), slot(7), slot(0), slot(3), slot(4), slot(2), slot(1), slot(8))
         weighed_bytes = {2: runner_bytes[4], 3: walker_bytes[2], 4: runner_bytes[6], 5: walker_bytes[4]}
 
         def squares(i):
@@ -477,7 +478,7 @@ def tile_list_crowd_steering_features_kernel(
         first_stores = {0: (pieces[0], every), 1: (pieces[1], every), 3: (pieces[2], every)}
         y00 = sums(0, 0, by_piece, early, (1,), first_stores)
         y10 = sums(1, 0, by_slot, banks(1, 0), (0, 1), {1: (front, low), 3: (front, high)})
-        quarter_stores = {1: (quarters[0], every), 3: (quarters[1], every)}
+        quarter_stores = {2: (back, low), 3: (back, high)}
         y01 = sums(0, 1, by_quarter, banks(0, 1), (0, 1), quarter_stores)
         y11 = sums(1, 1, last_by_slot, banks(1, 1), (0, 1), {1: (back, low), 3: (back, high)})
         for values, g_out, agents in ((y00, 0, front), (y10, 1, front), (y01, 0, back)):

@@ -53,6 +53,7 @@ def tile_list_crowd_steering_features_kernel(
             return plane
 
         w2_plane = zeroed_plane(nc.vector, "w2_plane", H)
+        tab2_plane = zeroed_plane(nc.gpsimd, "tab2_plane", T)
         tab_plane = zeroed_plane(nc.gpsimd, "tab_plane", T)
         zero = first.tile([P, 1], F32, name="zero")
         nc.vector.memset(zero[:], 0.0)
@@ -126,20 +127,19 @@ def tile_list_crowd_steering_features_kernel(
         def quantise(codes, scales, rounded):
             nc.vector.quantize_mx(codes.bitcast(FP8X4), scales, rounded)
 
-        tab2_plane = held("tab2_plane", [P, T], U8)
-        for q in range(4):
-            rows = tab2_scales[0, 4 * q : 4 * q + 4, :].bitcast(I32)
-            nc.sync.dma_start(tab2_plane[32 * q : 32 * q + 32, :].bitcast(I32), rows.partition_broadcast(8))
         list2 = load_list("list2", offs2)
         list1 = load_list("list1", offs)
+        list4 = load_list("list4", offs4)
+        load_scale_rows(nc.sync, tab2_plane, tab2_scales, range(4))
+        tab2 = load_words("tab2", TAB2, tab2_words[0])
         w2_raw = held("w2_raw", [P, 2 * H], U8)
         nc.sync.dma_start(w2_raw[:].bitcast(I32), w2_words[0].bitcast(I32))
-        tab2 = load_words("tab2", TAB2, tab2_words[0])
-        load_scale_rows(nc.gpsimd, tab_plane, tab_scales, (0, 2))
+        load_scale_rows(nc.gpsimd, tab_plane, tab_scales, (0, 2, 1))
         load_scale_rows(nc.sync, w2_plane, w2_scales, range(4))
-        load_scale_rows(nc.sync, tab_plane, tab_scales, (1, 3))
-        gains2 = load_gains(placed("gains2_first", [P, 1, S], F32, GAINS2), wg2, 0)
-        list4 = load_list("list4", offs4)
+        gains2_first = placed("gains2_first", [P, S], F32, GAINS2)
+        nc.sync.dma_start(gains2_first[:], wg2.rearrange("(u t) j -> u t j", t=4)[:, 0, :].partition_broadcast(4))
+        load_scale_rows(nc.sync, tab_plane, tab_scales, (3,))
+        gains2 = [gains2_first[:]]
         gains2 = gains2 + load_gains(placed("gains2_rest", [P, 3, S], F32, GAINS2 + 2 * KIB), wg2, 1)
         tab = [load_words("tab0", TAB0, tab_words[0]), load_words("tab1", TAB1, tab_words[1])]
         w1_bytes = {(a, half): (RAW, STYLE + 8 * KIB)[a] + 8 * KIB * half for half in range(2) for a in range(2)}
@@ -150,20 +150,26 @@ def tile_list_crowd_steering_features_kernel(
         gains1 = load_gains(held("gains1", [P, 4, S], F32), wg1, 0)
         styles = [load_style(i) for i in range(2)]
 
-        w2_dealt = held("w2_dealt", [P, 2, H], U8)
-        w2_plane_dealt = held("w2_plane_dealt", [P, 2, 512], U8)
+        deals = ((0, slice(0, 1)), (0, slice(1, 4)), (1, slice(0, 4)))
+        w2_dealt, w2_plane_dealt = {}, {}
 
-        def deal_words(g):
-            nc.vector.tensor_copy(
-                w2_dealt[:, g, :].bitcast(U16).rearrange("p (t m) -> p t m", t=4),
-                w2_raw[:, H * g : H * (g + 1)].bitcast(U16).rearrange("p (m t) -> p t m", t=4),
+        def deal_words(g, slots):
+            dealt = held(f"w2_dealt{g}{slots.start}", [P, 2 * P * (slots.stop - slots.start)], U8)
+            nc.scalar.copy(
+                dealt[:].bitcast(U16).rearrange("p (t m) -> p t m", m=P),
+                w2_raw[:, H * g : H * (g + 1)].bitcast(U16).rearrange("p (m t) -> p t m", t=4)[:, slots, :],
             )
+            for n, t in enumerate(range(slots.start, slots.stop)):
+                w2_dealt[4 * g + t] = dealt[:, 2 * P * n : 2 * P * (n + 1)]
 
         def deal_scales(g):
+            dealt = held(f"w2_plane_dealt{g}", [P, 512], U8)
             nc.vector.tensor_copy(
-                w2_plane_dealt[:, g, :].rearrange("p (t m) -> p t m", t=4),
+                dealt[:].rearrange("p (t m) -> p t m", t=4),
                 w2_plane[:, 512 * g : 512 * (g + 1)].rearrange("p (m t) -> p t m", t=4),
             )
+            for t in range(4):
+                w2_plane_dealt[4 * g + t] = dealt[:, P * t : P * (t + 1)]
 
         halves = [slice(0, S // 2), slice(S // 2, S)]
         whole = [slice(0, S)]
@@ -172,8 +178,8 @@ def tile_list_crowd_steering_features_kernel(
             return slice(cols.start // 16, cols.stop // 16)
 
         v2_scales = gather("v2_scales", tab2_plane, list2, U8)
-        for g in range(2):
-            deal_words(g)
+        for g, slots in deals:
+            deal_words(g, slots)
         v2_words = held("v2_words", [P, S], U32)
         for g, cols in enumerate(halves):
             nc.vector.tensor_copy(v2_words[:, cols], tab2[:].bitcast(U32).indirect(list2[:, entries(cols)]))
@@ -195,14 +201,13 @@ def tile_list_crowd_steering_features_kernel(
             pages[i] = placed(f"page{i}", [P, T2], F32, page_bytes[i])
 
         def cosines(i, pieces):
-            g, t = divmod(i, 4)
             h = feature(f"h2_{i}", slot(i))
             for n, cols in enumerate(pieces):
                 acc = bank((i + 7 * n) % 8, f"angle{i}_{n}")
                 nc.tensor.matmul_mx(
                     acc[:, cols],
-                    lhsT=w2_dealt[:, g, 2 * P * t : 2 * P * (t + 1)].bitcast(FP4X4),
-                    lhsT_scale=w2_plane_dealt[:, g, P * t : P * (t + 1)],
+                    lhsT=w2_dealt[i].bitcast(FP4X4),
+                    lhsT_scale=w2_plane_dealt[i],
                     rhs=v2_words[:, cols].bitcast(FP8X4),
                     rhs_scale=v2_scales[:, cols],
                     start=True,

@@ -129,17 +129,15 @@ def tile_list_crowd_steering_features_kernel(
 
         list2 = load_list("list2", offs2)
         list1 = load_list("list1", offs)
-        list4 = load_list("list4", offs4)
         load_scale_rows(nc.sync, tab2_plane, tab2_scales, range(4))
         tab2 = load_words("tab2", TAB2, tab2_words[0])
         w2_raw = held("w2_raw", [P, 2 * H], U8)
         nc.sync.dma_start(w2_raw[:].bitcast(I32), w2_words[0].bitcast(I32))
-        load_scale_rows(nc.gpsimd, tab_plane, tab_scales, (0, 2, 1))
+        load_scale_rows(nc.gpsimd, tab_plane, tab_scales, (0, 2))
         load_scale_rows(nc.sync, w2_plane, w2_scales, range(4))
-        gains2_first = placed("gains2_first", [P, S], F32, GAINS2)
-        nc.sync.dma_start(gains2_first[:], wg2.rearrange("(u t) j -> u t j", t=4)[:, 0, :].partition_broadcast(4))
-        load_scale_rows(nc.sync, tab_plane, tab_scales, (3,))
-        gains2 = [gains2_first[:]]
+        load_scale_rows(nc.sync, tab_plane, tab_scales, (1, 3))
+        list4 = load_list("list4", offs4)
+        gains2 = load_gains(placed("gains2_first", [P, 1, S], F32, GAINS2), wg2, 0)
         gains2 = gains2 + load_gains(placed("gains2_rest", [P, 3, S], F32, GAINS2 + 2 * KIB), wg2, 1)
         tab = [load_words("tab0", TAB0, tab_words[0]), load_words("tab1", TAB1, tab_words[1])]
         w1_bytes = {(a, half): (RAW, STYLE + 8 * KIB)[a] + 8 * KIB * half for half in range(2) for a in range(2)}

@@ -138,8 +138,8 @@ def tile_list_crowd_steering_features_kernel(
         load_scale_rows(nc.sync, tab_plane, tab_scales, (1, 3))
         list4 = load_list("list4", offs4)
         gains2 = load_gains(placed("gains2_first", [P, 1, S], F32, GAINS2), wg2, 0)
-        gains2 = gains2 + load_gains(placed("gains2_rest", [P, 3, S], F32, GAINS2 + 2 * KIB), wg2, 1)
         tab = [load_words("tab0", TAB0, tab_words[0]), load_words("tab1", TAB1, tab_words[1])]
+        gains2 = gains2 + load_gains(placed("gains2_rest", [P, 3, S], F32, GAINS2 + 2 * KIB), wg2, 1)
         w1_bytes = {(a, half): (RAW, STYLE + 8 * KIB)[a] + 8 * KIB * half for half in range(2) for a in range(2)}
         w1_raw = {part: load_weight("w1", w1, *part, offset) for part, offset in w1_bytes.items()}
         centre = held("centre", [P, 2, 4], F32)
@@ -148,17 +148,18 @@ def tile_list_crowd_steering_features_kernel(
         gains1 = load_gains(held("gains1", [P, 4, S], F32), wg1, 0)
         styles = [load_style(i) for i in range(2)]
 
-        deals = ((0, slice(0, 1)), (0, slice(1, 4)), (1, slice(0, 4)))
         w2_dealt, w2_plane_dealt = {}, {}
 
-        def deal_words(g, slots):
-            dealt = held(f"w2_dealt{g}{slots.start}", [P, 2 * P * (slots.stop - slots.start)], U8)
+        def deal_words(slots):
+            count = slots.stop - slots.start
+            dealt = held(f"w2_dealt{slots.start}", [P, 2, count, 2 * P], U8)
             nc.scalar.copy(
-                dealt[:].bitcast(U16).rearrange("p (t m) -> p t m", m=P),
-                w2_raw[:, H * g : H * (g + 1)].bitcast(U16).rearrange("p (m t) -> p t m", t=4)[:, slots, :],
+                dealt[:].bitcast(U16),
+                w2_raw[:].bitcast(U16).rearrange("p (g m t) -> p g t m", g=2, t=4)[:, :, slots, :],
             )
-            for n, t in enumerate(range(slots.start, slots.stop)):
-                w2_dealt[4 * g + t] = dealt[:, 2 * P * n : 2 * P * (n + 1)]
+            for g in range(2):
+                for n in range(count):
+                    w2_dealt[4 * g + slots.start + n] = dealt[:, g, n, :]
 
         def deal_scales(g):
             dealt = held(f"w2_plane_dealt{g}", [P, 512], U8)
@@ -176,8 +177,8 @@ def tile_list_crowd_steering_features_kernel(
             return slice(cols.start // 16, cols.stop // 16)
 
         v2_scales = gather("v2_scales", tab2_plane, list2, U8)
-        for g, slots in deals:
-            deal_words(g, slots)
+        for slots in (slice(0, 1), slice(1, 4)):
+            deal_words(slots)
         v2_words = held("v2_words", [P, S], U32)
         for g, cols in enumerate(halves):
             nc.vector.tensor_copy(v2_words[:, cols], tab2[:].bitcast(U32).indirect(list2[:, entries(cols)]))
@@ -191,17 +192,17 @@ def tile_list_crowd_steering_features_kernel(
         def slot(n):
             return FEAT + 2 * KIB * n
 
-        page_bytes = {0: PAGE, 1: PAGE + 4 * KIB, 2: TAB1, 3: TAB1 + 4 * KIB, 4: W1_BF + 8 * KIB, 5: W1_BF,
+        page_bytes = {0: PAGE, 4: PAGE + 4 * KIB, 1: TAB1, 2: TAB1 + 4 * KIB, 5: W1_BF + 8 * KIB, 3: W1_BF,
                       6: W1_BF + 12 * KIB, 7: STYLE + 12 * KIB}
         pages = {}
 
         def new_page(i):
             pages[i] = placed(f"page{i}", [P, T2], F32, page_bytes[i])
 
-        def cosines(i, pieces):
-            h = feature(f"h2_{i}", slot(i))
+        def cosines(turn, i, pieces):
+            h = feature(f"h2_{i}", slot(turn))
             for n, cols in enumerate(pieces):
-                acc = bank((i + 7 * n) % 8, f"angle{i}_{n}")
+                acc = bank((turn + 7 * n) % 8, f"angle{i}_{n}")
                 nc.tensor.matmul_mx(
                     acc[:, cols],
                     lhsT=w2_dealt[i].bitcast(FP4X4),
@@ -222,23 +223,24 @@ def tile_list_crowd_steering_features_kernel(
         def place(i, lst, weighed):
             nc.vector.tensor_copy(pages[i][:].indirect(lst[:]), weighed[:])
 
-        h2 = [cosines(i, halves if i == 0 else whole) for i in range(PAGES)]
-        for i in range(FUSED):
-            if i == FUSED - 1:
+        made = (0, 4, 1, 2, 5, 3, 6, 7)
+        h2 = {i: cosines(turn, i, halves if i == 0 else whole) for turn, i in enumerate(made)}
+        for i in made[:FUSED]:
+            if i == made[FUSED - 1]:
                 v_words = [gather(f"v_words{a}", tab[a], list1, U32) for a in range(2)]
             new_page(i)
             for cols in halves if i == 0 else whole:
                 nc.vector.tensor_tensor(
-                    pages[i][:].indirect(list4[:, entries(cols)]), h2[i][:, cols], gains2[i][:, cols], MULT
+                    pages[i][:].indirect(list4[:, entries(cols)]), h2[i][:, cols], gains2[i % 4][:, cols], MULT
                 )
-        runner_bytes = {3: slot(1), 5: slot(2), 4: slot(5), 6: W1_BF + 4 * KIB, 7: W1_BF + 6 * KIB}
+        runner_bytes = {2: slot(1), 3: slot(2), 5: slot(5), 6: W1_BF + 4 * KIB, 7: W1_BF + 6 * KIB}
         runners = {}
 
         def weigh_runners(indices):
             for i in indices:
                 runners[i] = weigh(feature(f"runner{i}", runner_bytes[i]), h2[i], gains2[i % 4])
 
-        weigh_runners((3, 5, 4))
+        weigh_runners((2, 3, 5))
 
         w1_codes = placed("w1_codes", [P, 2, 1024], U32, W1_CODES)
         w1_bf = {}
@@ -247,21 +249,21 @@ def tile_list_crowd_steering_features_kernel(
                 w1_bf[a, half] = placed(f"w1_bf{a}{half}", [P, 2048], BF16, W1_BF + 4 * KIB * (2 * half + a))
                 round_weight(w1_raw[a, half], [w1_bf[a, half][:]])
         w1_scales = {}
-        for i in (3, 5, 4, 6):
-            if i in (5, 4):
-                half = 5 - i
+        for i in (2, 3, 5, 6):
+            if i in (3, 5):
+                half = i // 4
                 for a in range(2):
                     cols = slice(512 * a, 512 * (a + 1))
                     name = f"w1_scales{a}{half}"
                     w1_scales[a, half] = held(name, [P, 512], U8) if a else placed(name, [P, 512], U8, w1_bytes[1, half])
                     quantise(w1_codes[:, half, cols], w1_scales[a, half][:], w1_bf[a, half][:])
-            if i == 5:
+            if i == 3:
                 weigh_runners((6, 7))
             new_page(i)
             place(i, list4, runners[i])
 
         walker_bytes = (slot(6), slot(7), slot(0), slot(3), slot(4), slot(2), slot(1), slot(8))
-        weighed_bytes = {2: runner_bytes[4], 3: walker_bytes[2], 4: runner_bytes[6], 5: walker_bytes[4]}
+        weighed_bytes = {2: runner_bytes[5], 3: walker_bytes[2], 4: runner_bytes[6], 5: walker_bytes[4]}
 
         def squares(i):
             half, t = divmod(i, 4)

@@ -54,7 +54,9 @@ def tile_list_crowd_steering_features_kernel(
 
         w2_plane = zeroed_plane(nc.vector, "w2_plane", H)
         tab2_plane = zeroed_plane(nc.gpsimd, "tab2_plane", T)
-        tab_plane = zeroed_plane(nc.gpsimd, "tab_plane", T)
+        tab_plane = first.tile([P, T], U8, name="tab_plane", align_bytes=64)
+        for rows in (slice(32, 64), slice(64, P)):
+            nc.gpsimd.memset(tab_plane[rows, :].bitcast(I32), 0)
         zero = first.tile([P, 1], F32, name="zero")
         nc.vector.memset(zero[:], 0.0)
         sin_zero = first.tile([P, 1], F32, name="sin_zero")
@@ -79,13 +81,9 @@ def tile_list_crowd_steering_features_kernel(
             nc.sync.dma_start(lst[:], src)
             return lst
 
-        def load_scale_rows(queue, plane, src, quadrants):
-            passes = src.shape[0]
-            for q in quadrants:
-                queue.dma_start(
-                    plane[32 * q : 32 * q + 4 * passes, :].bitcast(I32),
-                    src[:, 4 * q : 4 * q + 4, :].bitcast(I32),
-                )
+        def load_scale_rows(plane, src):
+            for q in range(4):
+                nc.sync.dma_start(plane[32 * q : 32 * q + 4, :].bitcast(I32), src[0, 4 * q : 4 * q + 4, :].bitcast(I32))
 
         def load_words(name, offset, src):
             words = placed(name, [P, T], I32, offset)
@@ -129,13 +127,13 @@ def tile_list_crowd_steering_features_kernel(
 
         list2 = load_list("list2", offs2)
         list1 = load_list("list1", offs)
-        load_scale_rows(nc.sync, tab2_plane, tab2_scales, range(4))
+        load_scale_rows(tab2_plane, tab2_scales)
         tab2 = load_words("tab2", TAB2, tab2_words[0])
         w2_raw = held("w2_raw", [P, 2 * H], U8)
         nc.sync.dma_start(w2_raw[:].bitcast(I32), w2_words[0].bitcast(I32))
-        load_scale_rows(nc.gpsimd, tab_plane, tab_scales, (0, 2))
-        load_scale_rows(nc.sync, w2_plane, w2_scales, range(4))
-        load_scale_rows(nc.sync, tab_plane, tab_scales, (1, 3))
+        load_scale_rows(w2_plane, w2_scales)
+        for a in range(2):
+            nc.sync.dma_start(tab_plane[a:32:2, :].bitcast(I32), tab_scales[a].bitcast(I32))
         list4 = load_list("list4", offs4)
         gains2 = load_gains(placed("gains2_first", [P, 1, S], F32, GAINS2), wg2, 0)
         tab = [load_words("tab0", TAB0, tab_words[0]), load_words("tab1", TAB1, tab_words[1])]
@@ -183,8 +181,10 @@ def tile_list_crowd_steering_features_kernel(
         for g, cols in enumerate(halves):
             nc.vector.tensor_copy(v2_words[:, cols], tab2[:].bitcast(U32).indirect(list2[:, entries(cols)]))
             deal_scales(g)
-        v_scales = first.tile([P, S], U8, name="v_scales", tag="w2_plane", align_bytes=64)
-        nc.vector.tensor_copy(v_scales[:], tab_plane[:].indirect(list1[:]))
+        v_scale_rows = gather("v_scale_rows", tab_plane, list1, U8)
+        v_scales = zeroed_plane(nc.vector, "v_scales", 2 * S)
+        for q in range(4):
+            nc.gpsimd.dma_start(v_scales[32 * q : 32 * q + 4, :].bitcast(I32), v_scale_rows[8 * q : 8 * q + 8, :].bitcast(I32))
 
         def feature(name, offset):
             return placed(name, [P, S], F32, offset)
@@ -276,7 +276,7 @@ def tile_list_crowd_steering_features_kernel(
                     lhsT=w1_codes[:, half, cols].bitcast(FP8X4),
                     lhsT_scale=w1_scales[a, half][:, P * t : P * (t + 1)],
                     rhs=v_words[a][:].bitcast(FP8X4),
-                    rhs_scale=v_scales[4 * a : P, :],
+                    rhs_scale=v_scales[:, S * a : S * (a + 1)],
                     start=(a == 0),
                     stop=(a == 1),
                 )

@@ -24,6 +24,7 @@ KIB = 1024
 FUSED = 3
 QUARTER = T2 // 4
 LAST_SHARE = 256
+WARM_UPS = 5
 
 TAB2 = 0
 TAB0 = TAB2 + 8 * KIB
@@ -414,6 +415,12 @@ def tile_list_crowd_steering_features_kernel(
         early = [bank(n, f"y_first{n}") for n in range(4)]
         for acc, (runs, slots) in zip(early, by_piece):
             project(acc, runs, 0, slots, 0)
+        warm = bank(7, "warm")
+        for n in range(WARM_UPS):
+            codes, scales = w3_operand(0, 0, 0)
+            z_codes, z_scales = z_operand(0, front)
+            nc.tensor.matmul_mx(warm[:], lhsT=codes.bitcast(FP8X4), lhsT_scale=scales, rhs=z_codes.bitcast(FP8X4),
+                                rhs_scale=z_scales, start=True, stop=True)
         nc.vector.tensor_tensor(pages[PAGES - 1][:].indirect(list3[:]), last_bumps[:], gains1[3], MULT)
 
         late_scales[0] = placed("second_scales", [P, 512], U8, page_bytes[5])

@@ -456,7 +456,8 @@ def tile_list_crowd_steering_features_kernel(
                     woven[:, share, :].rearrange("p (n i) t -> p n t i", i=4),
                     values[:, :, share].rearrange("p t (n i) -> p n t i", i=4),
                 )
-            quantise(y_codes[g_out][:, agents], y_scales[:, g_out, agents], woven[:].rearrange("p n t -> p (n t)"))
+                done = slice(agents.start + share.start, agents.start + share.stop)
+                quantise(y_codes[g_out][:, done], y_scales[:, g_out, done], woven[:, share, :].rearrange("p n t -> p (n t)"))
 
         def store_codes(g_out, agents):
             nc.sync.dma_start(

import math
from contextlib import ExitStack

import concourse.mybir as mybir

F32 = mybir.dt.float32
BF16 = mybir.dt.bfloat16
I32 = mybir.dt.int32
U32 = mybir.dt.uint32
U16 = mybir.dt.uint16
U8 = mybir.dt.uint8
FP8X4 = mybir.dt.float8_e4m3fn_x4
FP4X4 = mybir.dt.float4_e2m1fn_x4
ACT = mybir.ActivationFunctionType
MULT = mybir.AluOpType.mult
ADD = mybir.AluOpType.add

P = 128
K, K2, H, N, T, S, T2 = 1024, 512, 1024, 1024, 2048, 512, 1024
FLOPS = 2 * K * H * S + 2 * K2 * H * S + 2 * H * N * T2
PAGES = H // P
HALF = T2 // 2
KIB = 1024
FUSED = 3
QUARTER = T2 // 4
LAST_SHARE = 256
WARM_UPS = 5

TAB2 = 0
TAB0 = TAB2 + 8 * KIB
TAB1 = TAB0 + 8 * KIB
GAINS2 = TAB1 + 8 * KIB
RAW = GAINS2 + 8 * KIB
W1_BF = RAW + 32 * KIB
W1_CODES = W1_BF + 16 * KIB
FEAT = W1_CODES + 8 * KIB
STYLE = FEAT + 18 * KIB
PAGE = STYLE + 24 * KIB


def tile_list_crowd_steering_features_kernel(
    tc, tab_words, tab_scales, offs, tab2_words, tab2_scales, offs2, w1, ctr, w2_words, w2_scales,
    offs3, offs4, wg1, wg2, style, w3, out_0, out_1, out_2,
):
    nc = tc.nc
    with ExitStack() as ctx:
        lists = ctx.enter_context(tc.tile_pool(name="lists", bufs=1))
        first = ctx.enter_context(tc.tile_pool(name="first", bufs=1))
        psum = ctx.enter_context(tc.psum_pool(name="psum", bufs=1))

        def zeroed_plane(engine, name, cols):
            plane = first.tile([P, cols], U8, name=name, tag=name, align_bytes=64)
            engine.memset(plane[:].bitcast(I32), 0)
            return plane

        w2_plane = zeroed_plane(nc.vector, "w2_plane", H)
        tab2_plane = zeroed_plane(nc.gpsimd, "tab2_plane", T)
        tab_plane = first.tile([P, T], U8, name="tab_plane", align_bytes=64)
        for rows in (slice(32, 64), slice(64, P)):
            nc.gpsimd.memset(tab_plane[rows, :].bitcast(I32), 0)
        zero = first.tile([P, 1], F32, name="zero")
        nc.vector.memset(zero[:], 0.0)
        sin_zero = first.tile([P, 1], F32, name="sin_zero")
        nc.scalar.activation(sin_zero[:], zero[:], ACT.Sin)
        half_pi = first.tile([P, 1], F32, name="half_pi")
        nc.vector.tensor_scalar(half_pi[:], sin_zero[:], 1.0, math.pi / 2, op0=MULT, op1=ADD)

        keep = ctx.enter_context(tc.tile_pool(name="keep", bufs=1))
        shared = ctx.enter_context(tc.tile_pool(name="shared", bufs=1))

        def placed(name, shape, dtype, offset):
            return shared.tile(shape, dtype, name=name, offset=offset, align_bytes=64)

        def held(name, shape, dtype):
            return keep.tile(shape, dtype, name=name, tag=name, align_bytes=64)

        def bank(idx, name):
            return psum.tile([P, 512], F32, name=name, tag=f"bank{idx}")

        def load_list(name, src):
            lst = lists.tile([P, S // 16], U16, name=name, tag=name)
            nc.sync.dma_start(lst[:], src)
            return lst

        def load_scale_rows(plane, src):
            for q in range(4):
                nc.sync.dma_start(plane[32 * q : 32 * q + 4, :].bitcast(I32), src[0, 4 * q : 4 * q + 4, :].bitcast(I32))

        def load_words(name, offset, src):
            words = placed(name, [P, T], I32, offset)
            nc.sync.dma_start(words[:], src.rearrange("p n i -> p (n i)").bitcast(I32))
            return words

        def load_gains(gains, src, t0):
            count = gains.shape[1]
            for q in (0, 2, 1, 3):
                nc.sync.dma_start(gains[32 * q : 32 * q + 32], src.rearrange("(u t) j -> u t j", t=4)[:, t0 : t0 + count, :])
            return [gains[:, t, :] for t in range(count)]

        def load_weight(name, src, a, half, offset):
            raw = placed(f"{name}_raw{a}{half}", [P, 4, 512], F32, offset)
            rows = src[512 * a : 512 * (a + 1), 512 * half : 512 * (half + 1)]
            nc.sync.dma_start(raw[:], rows.rearrange("(p j) c -> p j c", j=4))
            return raw

        def load_style(i):
            g, t = divmod(i, 4)
            offset = STYLE + 4 * KIB * i if i < 6 else W1_CODES + 4 * KIB * (i - 6)
            st = placed(f"style{i}", [P, T2], F32, offset)
            nc.sync.dma_start(st[:], style.rearrange("(g p t) n -> g t p n", g=2, t=4)[g, t])
            return st

        def gather(name, window, lst, dtype):
            picked = held(name, [P, S], dtype)
            nc.vector.tensor_copy(picked[:], window[:].bitcast(dtype).indirect(lst[:]))
            return picked

        def round_weight(raw, rounded):
            count = 4 // len(rounded)
            for s, part in enumerate(rounded):
                nc.scalar.copy(
                    part.rearrange("p (t m u e) -> p m u t e", t=count, u=2, e=2),
                    raw[:].rearrange("p (u e) (m t) -> p m u t e", e=2, t=4)[:, :, :, count * s : count * (s + 1), :],
                )

        def quantise(codes, scales, rounded):
            nc.vector.quantize_mx(codes.bitcast(FP8X4), scales, rounded)

        list2 = load_list("list2", offs2)
        list1 = load_list("list1", offs)
        load_scale_rows(tab2_plane, tab2_scales)
        tab2 = load_words("tab2", TAB2, tab2_words[0])
        w2_raw = held("w2_raw", [P, 2 * H], U8)
        nc.sync.dma_start(w2_raw[:].bitcast(I32), w2_words[0].bitcast(I32))
        load_scale_rows(w2_plane, w2_scales)
        for a in range(2):
            nc.sync.dma_start(tab_plane[a:32:2, :].bitcast(I32), tab_scales[a].bitcast(I32))
        list4 = load_list("list4", offs4)
        gains2 = load_gains(placed("gains2_first", [P, 1, S], F32, GAINS2), wg2, 0)
        tab = [load_words("tab0", TAB0, tab_words[0]), load_words("tab1", TAB1, tab_words[1])]
        gains2 = gains2 + load_gains(placed("gains2_rest", [P, 3, S], F32, GAINS2 + 2 * KIB), wg2, 1)
        w1_bytes = {(a, half): (RAW, STYLE + 8 * KIB)[a] + 8 * KIB * half for half in range(2) for a in range(2)}
        w1_raw = {part: load_weight("w1", w1, *part, offset) for part, offset in w1_bytes.items()}
        centre = held("centre", [P, 2, 4], F32)
        nc.sync.dma_start(centre[:], ctr.rearrange("(g p t) -> p g t", g=2, t=4))
        list3 = load_list("list3", offs3)
        gains1 = load_gains(held("gains1", [P, 4, S], F32), wg1, 0)
        styles = [load_style(i) for i in range(2)]

        w2_dealt, w2_plane_dealt = {}, {}

        def deal_words(slots):
            count = slots.stop - slots.start
            dealt = held(f"w2_dealt{slots.start}", [P, 2, count, 2 * P], U8)
            nc.scalar.copy(
                dealt[:].bitcast(U16),
                w2_raw[:].bitcast(U16).rearrange("p (g m t) -> p g t m", g=2, t=4)[:, :, slots, :],
            )
            for g in range(2):
                for n in range(count):
                    w2_dealt[4 * g + slots.start + n] = dealt[:, g, n, :]

        def deal_scales(g):
            dealt = held(f"w2_plane_dealt{g}", [P, 512], U8)
            nc.vector.tensor_copy(
                dealt[:].rearrange("p (t m) -> p t m", t=4),
                w2_plane[:, 512 * g : 512 * (g + 1)].rearrange("p (m t) -> p t m", t=4),
            )
            for t in range(4):
                w2_plane_dealt[4 * g + t] = dealt[:, P * t : P * (t + 1)]

        halves = [slice(0, S // 2), slice(S // 2, S)]
        whole = [slice(0, S)]

        def entries(cols):
            return slice(cols.start // 16, cols.stop // 16)

        v2_scales = gather("v2_scales", tab2_plane, list2, U8)
        for slots in (slice(0, 1), slice(1, 4)):
            deal_words(slots)
        v2_words = held("v2_words", [P, S], U32)
        for g, cols in enumerate(halves):
            nc.vector.tensor_copy(v2_words[:, cols], tab2[:].bitcast(U32).indirect(list2[:, entries(cols)]))
            deal_scales(g)
        v_scale_rows = gather("v_scale_rows", tab_plane, list1, U8)
        v_scales = zeroed_plane(nc.vector, "v_scales", 2 * S)
        for q in range(4):
            nc.gpsimd.dma_start(v_scales[32 * q : 32 * q + 4, :].bitcast(I32), v_scale_rows[8 * q : 8 * q + 8, :].bitcast(I32))

        def feature(name, offset):
            return placed(name, [P, S], F32, offset)

        def slot(n):
            return FEAT + 2 * KIB * n

        page_bytes = {0: PAGE, 4: PAGE + 4 * KIB, 1: TAB1, 2: TAB1 + 4 * KIB, 5: W1_BF + 8 * KIB, 3: W1_BF,
                      6: W1_BF + 12 * KIB, 7: STYLE + 12 * KIB}
        pages = {}

        def new_page(i):
            pages[i] = placed(f"page{i}", [P, T2], F32, page_bytes[i])

        def cosines(turn, i, pieces):
            h = feature(f"h2_{i}", slot(turn))
            for n, cols in enumerate(pieces):
                acc = bank((turn + 7 * n) % 8, f"angle{i}_{n}")
                nc.tensor.matmul_mx(
                    acc[:, cols],
                    lhsT=w2_dealt[i].bitcast(FP4X4),
                    lhsT_scale=w2_plane_dealt[i],
                    rhs=v2_words[:, cols].bitcast(FP8X4),
                    rhs_scale=v2_scales[:, cols],
                    start=True,
                    stop=True,
                )
                nc.scalar.activation(h[:, cols], acc[:, cols], ACT.Abs)
                nc.scalar.activation(h[:, cols], h[:, cols], ACT.Sin, bias=half_pi[:], scale=-1.0)
            return h

        def weigh(weighed, h, gains):
            nc.gpsimd.tensor_tensor(weighed[:], h[:], gains, MULT)
            return weighed

        def place(i, lst, weighed):
            nc.vector.tensor_copy(pages[i][:].indirect(lst[:]), weighed[:])

        made = (0, 4, 1, 2, 5, 3, 6, 7)
        h2 = {i: cosines(turn, i, halves if i == 0 else whole) for turn, i in enumerate(made)}
        for i in made[:FUSED]:
            if i == made[FUSED - 1]:
                v_words = [gather(f"v_words{a}", tab[a], list1, U32) for a in range(2)]
            new_page(i)
            for cols in halves if i == 0 else whole:
                nc.vector.tensor_tensor(
                    pages[i][:].indirect(list4[:, entries(cols)]), h2[i][:, cols], gains2[i % 4][:, cols], MULT
                )
        runner_bytes = {2: slot(1), 3: slot(2), 5: slot(5), 6: W1_BF + 4 * KIB, 7: W1_BF + 6 * KIB}
        runners = {}

        def weigh_runners(indices):
            for i in indices:
                runners[i] = weigh(feature(f"runner{i}", runner_bytes[i]), h2[i], gains2[i % 4])

        weigh_runners((2, 3, 5))

        w1_codes = placed("w1_codes", [P, 2, 1024], U32, W1_CODES)
        w1_bf = {}
        for half in range(2):
            for a in range(2):
                w1_bf[a, half] = placed(f"w1_bf{a}{half}", [P, 2048], BF16, W1_BF + 4 * KIB * (2 * half + a))
                round_weight(w1_raw[a, half], [w1_bf[a, half][:]])
        w1_scales = {}
        for i in (2, 3, 5, 6):
            if i in (3, 5):
                half = i // 4
                for a in range(2):
                    cols = slice(512 * a, 512 * (a + 1))
                    name = f"w1_scales{a}{half}"
                    w1_scales[a, half] = held(name, [P, 512], U8) if a else placed(name, [P, 512], U8, w1_bytes[1, half])
                    quantise(w1_codes[:, half, cols], w1_scales[a, half][:], w1_bf[a, half][:])
            if i == 3:
                weigh_runners((6, 7))
            new_page(i)
            place(i, list4, runners[i])

        walker_bytes = (slot(6), slot(7), slot(0), slot(3), slot(4), slot(2), slot(1), slot(8))
        weighed_bytes = {2: runner_bytes[5], 3: walker_bytes[2], 4: runner_bytes[6], 5: walker_bytes[4]}

        def squares(i):
            half, t = divmod(i, 4)
            h = feature(f"h1_{i}", walker_bytes[i])
            acc = bank(i, f"dist{i}")
            for a in range(2):
                cols = slice(512 * a + P * t, 512 * a + P * (t + 1))
                nc.tensor.matmul_mx(
                    acc[:],
                    lhsT=w1_codes[:, half, cols].bitcast(FP8X4),
                    lhsT_scale=w1_scales[a, half][:, P * t : P * (t + 1)],
                    rhs=v_words[a][:].bitcast(FP8X4),
                    rhs_scale=v_scales[:, S * a : S * (a + 1)],
                    start=(a == 0),
                    stop=(a == 1),
                )
            nc.scalar.activation(h[:], acc[:], ACT.Square, bias=centre[:, half, t : t + 1], scale=-1.0)
            return h

        def bump(out, h):
            nc.scalar.activation(out[:], h[:], ACT.Exp, scale=-1.0)
            return out

        walkers, bumps = {}, {}
        for i in range(PAGES):
            bumps[i] = squares(i)
            if i < PAGES - 1:
                bump(bumps[i], bumps[i])
            if i < 6:
                out = feature(f"walker{i}", weighed_bytes[i]) if i in weighed_bytes else bumps[i]
                walkers[i] = weigh(out, bumps[i], gains1[i % 4])

        early_bf = placed("early_bf", [P, 2, 2048], BF16, RAW + 24 * KIB)
        second_bf = held("second_bf", [P, 2048], BF16)
        w3_late_bf = held("w3_late_bf", [P, 2, 2048], BF16)
        rounded_w3 = {
            (0, 0): [early_bf[:, 0, :]],
            (1, 0): [second_bf[:]],
            (0, 1): [w3_late_bf[:, 0, :]],
            (1, 1): [w3_late_bf[:, 1, :]],
        }
        w3_raw = {(a, g): load_weight("w3", w3, a, g, RAW + 8 * KIB * (2 * g + a)) for g in range(2) for a in range(2)}
        for part in ((1, 0), (0, 1), (1, 1), (0, 0)):
            round_weight(w3_raw[part], rounded_w3[part])
        styles += [load_style(i) for i in range(2, PAGES)]

        z_rows0 = placed("z_rows0", [P, 2, 4, HALF], BF16, TAB2)
        z_rows1 = [placed(f"z_rows1_{pair}", [P, 2, 2, HALF], BF16, TAB0 + 4 * KIB * pair) for pair in range(2)]
        z1_first_bf = placed("z1_first_bf", [P, 2048], BF16, RAW + 2 * KIB)
        z_late_bf = placed("z_late_bf", [P, 2, 2, 1024], BF16, RAW - 6 * KIB)
        front, back = slice(0, HALF), slice(HALF, T2)
        quarters = [slice(HALF + QUARTER * n, HALF + QUARTER * (n + 1)) for n in range(2)]

        def z_woven(g, agents):
            if agents.start < HALF:
                tile, start = (early_bf[:, 1, :], z1_first_bf[:])[g], agents.start
            else:
                n, start = divmod(agents.start - HALF, QUARTER)
                tile = z_late_bf[:, n, g, :]
            return tile[:, 4 * start : 4 * (start + agents.stop - agents.start)]

        def z_rows(g, halves, slots):
            if g == 0:
                return z_rows0[:, halves, slots, :]
            return z_rows1[slots.start // 2][:, halves, slots.start % 2 : slots.start % 2 + slots.stop - slots.start, :]

        def apply_style(i):
            g, t = divmod(i, 4)
            for parts in (slice(0, 1), slice(1, 2)) if i == PAGES - 2 else (slice(0, 2),):
                nc.gpsimd.tensor_tensor(
                    z_rows(g, parts, slice(t, t + 1)).rearrange("p c t n -> p c (t n)"),
                    pages[i][:].rearrange("p (c n) -> p c n", c=2)[:, parts, :],
                    styles[i][:].rearrange("p (c n) -> p c n", c=2)[:, parts, :],
                    MULT,
                )

        def weave(copy, g, agents, slots):
            half, start = divmod(agents.start, HALF)
            cols = slice(start, start + agents.stop - agents.start)
            copy(
                z_woven(g, agents).rearrange("p (n i t) -> p n t i", i=4, t=4)[:, :, slots, :],
                z_rows(g, half, slots)[:, :, cols].rearrange("p t (n i) -> p n t i", i=4),
            )

        for i in range(PAGES - 1):
            place(i, list3, walkers[i])
            apply_style(i)
            if i == 0:
                walkers[6] = weigh(feature("walker6", STYLE), bumps[6], gains1[2])
            if i == 3:
                weave(nc.scalar.copy, 0, front, slice(0, 4))
                for agents in quarters:
                    weave(nc.scalar.copy, 0, agents, slice(0, 4))
            if i == 5:
                last_bumps = bump(feature("last_bumps", page_bytes[5]), bumps[PAGES - 1])
                for agents in [front] + quarters:
                    weave(nc.scalar.copy, 1, agents, slice(0, 2))

        early_codes = held("early_codes", [P, 2, 512], U32)
        new_page(PAGES - 1)
        place(PAGES - 1, list4, runners[PAGES - 1])
        early_scales = placed("early_scales", [P, 2, 512], U8, page_bytes[5] + 2 * KIB)
        quantise(early_codes[:].rearrange("p a c -> p (a c)"), early_scales[:].rearrange("p a c -> p (a c)"),
                 early_bf[:].rearrange("p a c -> p (a c)"))
        second_codes = held("second_codes", [P, 512], U32)
        w3_late_codes = held("w3_late_codes", [P, 2, 512], U32)
        z1_first_codes = held("z1_first_codes", [P, 512], U32)
        z1_first_scales = held("z1_first_scales", [P, 512], U8)
        z_late_codes = held("z_late_codes", [P, 2, 2, QUARTER], U32)
        z_late_scales = held("z_late_scales", [P, 2, 2, QUARTER], U8)
        late_scales = {}

        def w3_operand(a, g_out, t):
            cols = slice(P * t, P * (t + 1))
            if g_out == 1:
                return w3_late_codes[:, a, cols], late_scales[1][:, a, cols]
            if a == 0:
                return early_codes[:, 0, cols], early_scales[:, 0, cols]
            return second_codes[:, cols], late_scales[0][:, cols]

        def z_operand(a, agents):
            if agents.start >= HALF:
                n = (agents.start - HALF) // QUARTER
                return z_late_codes[:, n, a, :], z_late_scales[:, n, a, :]
            if a == 0:
                return early_codes[:, 1, agents], early_scales[:, 1, agents]
            return z1_first_codes[:, agents], z1_first_scales[:, agents]

        def project(acc, runs, g_out, slots, a):
            cells = [(t, agents) for t in range(slots.start, slots.stop) for agents in runs]
            width = 512 // len(cells)
            for e, (t, agents) in enumerate(cells):
                z_codes, z_scales = z_operand(a, agents)
                codes, scales = w3_operand(a, g_out, t)
                nc.tensor.matmul_mx(
                    acc[:, width * e : width * (e + 1)],
                    lhsT=codes.bitcast(FP8X4),
                    lhsT_scale=scales,
                    rhs=z_codes.bitcast(FP8X4),
                    rhs_scale=z_scales,
                    start=(a == 0 and e == 0),
                    stop=(a == 1 and e == len(cells) - 1),
                )

        every, low, high = slice(0, 4), slice(0, 2), slice(2, 4)
        pieces = [slice(0, P), slice(P, QUARTER), slice(QUARTER, HALF)]
        by_piece = [([pieces[0]], every), ([pieces[1]], every), ([pieces[2]], low), ([pieces[2]], high)]
        early = [bank(n, f"y_first{n}") for n in range(4)]
        for acc, (runs, slots) in zip(early, by_piece):
            project(acc, runs, 0, slots, 0)
        warm = bank(7, "warm")
        for n in range(WARM_UPS):
            codes, scales = w3_operand(0, 0, 0)
            z_codes, z_scales = z_operand(0, front)
            nc.tensor.matmul_mx(warm[:], lhsT=codes.bitcast(FP8X4), lhsT_scale=scales, rhs=z_codes.bitcast(FP8X4),
                                rhs_scale=z_scales, start=True, stop=True)
        nc.vector.tensor_tensor(pages[PAGES - 1][:].indirect(list3[:]), last_bumps[:], gains1[3], MULT)

        late_scales[0] = placed("second_scales", [P, 512], U8, page_bytes[5])

        def last_style(agents):
            half, start = divmod(agents.start, HALF)
            cols = slice(start, start + agents.stop - agents.start)
            nc.vector.tensor_tensor(z_rows1[1][:, half, 1, cols], pages[7][:, agents], styles[7][:, agents], MULT)

        for n, agents in enumerate(pieces):
            last_style(agents)
            weave(nc.vector.tensor_copy, 1, agents, high)
            if n == 0:
                quantise(second_codes[:], late_scales[0][:], second_bf[:])
            quantise(z1_first_codes[:, agents], z1_first_scales[:, agents], z_woven(1, agents))
        last_style(back)
        late_scales[1] = placed("w3_late_scales", [P, 2, 512], U8, page_bytes[5] + 512)
        quantise(*(tile[:].rearrange("p a c -> p (a c)") for tile in (w3_late_codes, late_scales[1], w3_late_bf)))
        for n, agents in enumerate(quarters):
            weave(nc.vector.tensor_copy, 1, agents, high)
            quantise(*(tile[:, n].rearrange("p a c -> p (a c)") for tile in (z_late_codes, z_late_scales, z_late_bf)))

        y_codes = [held(f"y_codes{g}", [P, T2], U32) for g in range(2)]
        y_scales = held("y_scales", [P, 2, T2], U8)
        y_rows = out_0.rearrange("(g p t) n -> g p t n", g=2, t=4)

        def quantise_y(values, g_out, agents, on_vector):
            width = agents.stop - agents.start
            woven = placed(f"y_woven{g_out}_{agents.start}", [P, width, 4], BF16, PAGE + 8 * agents.start + 8 * KIB * g_out)
            shares = ((slice(0, on_vector), nc.vector.tensor_copy), (slice(on_vector, width), nc.scalar.copy))
            for share, copy in shares[: 1 if on_vector == width else 2]:
                copy(
                    woven[:, share, :].rearrange("p (n i) t -> p n t i", i=4),
                    values[:, :, share].rearrange("p t (n i) -> p n t i", i=4),
                )
                done = slice(agents.start + share.start, agents.start + share.stop)
                quantise(y_codes[g_out][:, done], y_scales[:, g_out, done], woven[:, share, :].rearrange("p n t -> p (n t)"))

        def store_codes(g_out, agents):
            nc.sync.dma_start(
                out_1[g_out].rearrange("p n i -> p (n i)").bitcast(I32)[:, agents],
                y_codes[g_out][:, agents].bitcast(I32),
            )

        def sums(g_out, half, layout, banks, passes, stores):
            rows = placed(f"y{g_out}{half}", [P, 4, HALF], F32, (RAW + 8 * KIB, STYLE)[half] + 8 * KIB * g_out)

            def local(agents):
                return slice(agents.start - HALF * half, agents.stop - HALF * half)

            for n, (acc, (runs, slots)) in enumerate(zip(banks, layout)):
                for a in passes:
                    project(acc, runs, g_out, slots, a)
                agents = slice(runs[0].start, runs[-1].stop)
                width = agents.stop - agents.start
                nc.scalar.copy(rows[:, slots, local(agents)], acc[:].rearrange("p (t n) -> p t n", n=width))
                if n in stores:
                    done, done_slots = stores[n]
                    nc.sync.dma_start(y_rows[g_out][:, done_slots, done], rows[:, done_slots, local(done)])
            return rows

        def banks(g_out, half):
            return [bank(4 * g_out + n, f"y{g_out}{half}{n}") for n in range(4)]

        by_slot = [([front], slice(t, t + 1)) for t in range(4)]
        by_quarter = [([agents], slots) for agents in quarters for slots in (low, high)]
        last_by_slot = [(quarters, slice(t, t + 1)) for t in range(4)]
        first_stores = {0: (pieces[0], every), 1: (pieces[1], every), 3: (pieces[2], every)}
        y00 = sums(0, 0, by_piece, early, (1,), first_stores)
        y10 = sums(1, 0, by_slot, banks(1, 0), (0, 1), {1: (front, low), 3: (front, high)})
        quarter_stores = {2: (back, low), 3: (back, high)}
        y01 = sums(0, 1, by_quarter, banks(0, 1), (0, 1), quarter_stores)
        y11 = sums(1, 1, last_by_slot, banks(1, 1), (0, 1), {1: (back, low), 3: (back, high)})
        for values, g_out, agents in ((y00, 0, front), (y10, 1, front), (y01, 0, back)):
            quantise_y(values[:], g_out, agents, HALF)
            store_codes(g_out, agents)
        quantise_y(y11[:], 1, back, LAST_SHARE)
        store_codes(1, back)
        for q in range(4):
            (nc.scalar, nc.sync)[q % 2].dma_start(
                out_2[:, 4 * q : 4 * q + 4, :].rearrange("g r n -> r g n").bitcast(I32),
                y_scales[32 * q : 32 * q + 4].bitcast(I32),
            )
